import numpy as np
import ml_dtypes


def mxq(x, axis, fmt="e4m3"):
    dtype, down = {"e4m3": (ml_dtypes.float8_e4m3fn, 7), "e5m2": (ml_dtypes.float8_e5m2, 14)}[fmt]
    v = np.moveaxis(np.asarray(x, np.float32).astype(ml_dtypes.bfloat16).astype(np.float64), axis, -1)
    blocks = v.reshape(v.shape[:-1] + (-1, 32))
    amax = np.abs(blocks).max(-1, keepdims=True)
    byte = np.maximum(np.where(amax > 0, np.frexp(amax)[1] - 1 + 127, 0) - down, 1)
    scale = np.exp2(byte - 127.0)
    codes = (blocks / scale).astype(np.float32).astype(dtype).astype(np.float64)
    return np.moveaxis((codes * scale).reshape(v.shape), -1, axis)


WIDE = False


def mx_kscale(k):
    if not WIDE:
        return np.ones(k)
    levels = np.array([10, -10, 5, -5, 0])
    if k % 512:
        return np.exp2(np.random.permutation(np.resize(levels, k // 32))).repeat(32)
    a = np.empty((k // 512, 16))
    for p in range(k // 512):
        a[p, :8] = np.random.permutation(np.resize(levels, 8))
        for g in range(8):
            far = levels[np.abs(levels - a[p, g]) >= 10]
            a[p, g + 8] = far[np.random.randint(len(far))]
    return np.exp2(a.ravel()).repeat(32)


def f64(x):
    return np.asarray(x).astype(np.float64)


def striped(idx):
    return np.tile(idx.reshape(-1, 16).T, (8, 1)).astype(np.uint16)


def unstriped(offs):
    return offs[:16].T.reshape(-1).astype(np.int64)


E2M1 = np.array([0.0, 0.5, 1.0, 1.5, 2.0, 3.0, 4.0, 6.0, -0.0, -0.5, -1.0, -1.5, -2.0, -3.0, -4.0, -6.0])


def pack_weight(w, fmt):
    k, n = w.shape
    w = f64(np.asarray(w, np.float32).astype(ml_dtypes.bfloat16)).reshape(k // 32, 32, n)
    amax = np.abs(w).max(1)
    if fmt == "e4m3":
        byte = np.frexp(amax)[1] - 1 + 127 - 7
    else:
        mant, ex = np.frexp(amax / 6.0)
        byte = np.where(mant > 0.5, ex, ex - 1) + 127
    byte = np.clip(np.where(amax > 0, byte, 1), 1, 254)
    scaled = (w * np.exp2(127.0 - byte)[:, None, :]).reshape(k, n).astype(np.float32)
    by_word = np.ascontiguousarray(scaled.reshape(k // 512, 128, 4, n).transpose(0, 1, 3, 2))
    if fmt == "e4m3":
        words = by_word.astype(ml_dtypes.float8_e4m3fn).view(np.uint8)
    else:
        c = by_word.astype(ml_dtypes.float4_e2m1fn).view(np.uint8) & 0xF
        words = (c[..., 0::2] | (c[..., 1::2] << 4)).reshape(k // 512, 128, 2 * n)
    return np.ascontiguousarray(words), np.ascontiguousarray(byte.astype(np.uint8).reshape(k // 512, 16, n))


def unpack_weight(words, scales, fmt):
    g, _, n = scales.shape
    words = np.ascontiguousarray(words).reshape(g, 128, n, -1)
    if fmt == "e4m3":
        vals = words.view(ml_dtypes.float8_e4m3fn).astype(np.float64)
    else:
        nib = np.empty((g, 128, n, 4), np.uint8)
        nib[..., 0::2] = words & 0xF
        nib[..., 1::2] = words >> 4
        vals = E2M1[nib]
    vals = vals * np.repeat(np.exp2(scales.astype(np.float64) - 127.0), 8, axis=1)[..., None]
    return vals.transpose(0, 1, 3, 2).reshape(g * 512, n)


def gelu(v):
    return 0.5 * v * (1.0 + np.tanh(np.sqrt(2.0 / np.pi) * (v + 0.044715 * v**3)))


K, T, S, M, N = 1024, 2048, 1024, 1024, 256


def setup_inputs():
    n = np.random.standard_normal
    s = mx_kscale(K)[:, None]
    u = mx_kscale(S)
    idx = np.random.permutation(T)[:S]
    tab_words, tab_scales = pack_weight(n((K, T)) / np.sqrt(K) * s, "e4m3")
    wl_words, wl_scales = pack_weight(0.4 * n((K, N)) / np.sqrt(K) * s, "e2m1")
    wdT = 0.5 * n((N, T)) / np.sqrt(S)
    wdT[:, idx] /= u
    return {
        "x": (n((K, M)) / s).astype(np.float32),
        "tab_words": tab_words,
        "tab_scales": tab_scales,
        "offs": striped(idx),
        "g": (np.exp(0.3 * n(S)) * u).astype(np.float32),
        "wdT": wdT.astype(np.float32),
        "wl_words": wl_words,
        "wl_scales": wl_scales,
    }


def reference(x, tab_words, tab_scales, offs, g, wdT, wl_words, wl_scales):
    v = unpack_weight(tab_words, tab_scales, "e4m3")[:, unstriped(offs)]
    wl = unpack_weight(wl_words, wl_scales, "e2m1")
    wd = f64(wdT)[:, unstriped(offs)]
    xq = mxq(f64(x), 0, "e4m3")
    a = v.T @ xq
    h = np.log(1.0 + np.exp(a)) * f64(g)[:, None]
    y = mxq(wd, 1, "e4m3") @ mxq(h, 0, "e4m3") + wl.T @ xq
    return np.exp(y)

@@ -1,0 +1,274 @@
+from contextlib import ExitStack
+
+import concourse.mybir as mybir
+from concourse.masks import make_identity
+
+K, T, S, M, N = 1024, 2048, 1024, 1024, 256
+FLOPS = 2 * S * K * M + 2 * N * S * M + 2 * N * K * M
+
+F32 = mybir.dt.float32
+BF16 = mybir.dt.bfloat16
+I32 = mybir.dt.int32
+U32 = mybir.dt.uint32
+U16 = mybir.dt.uint16
+U8 = mybir.dt.uint8
+FP8X4 = mybir.dt.float8_e4m3fn_x4
+FP4X4 = mybir.dt.float4_e2m1fn_x4
+ACT = mybir.ActivationFunctionType
+ALU = mybir.AluOpType
+
+P = 128
+PASS = 512
+FLOOR = 2.0 ** -60
+X_CHUNKS = ((0, 128, "SS"), (128, 128, "SS"), (256, 256, "SV"), (512, 256, "GG"), (768, 256, "GG"))
+GAIN_ENGINES = ("VVVVVVVV", "VVVVVVVV")
+
+
+def tile_list_claim_intensity_sparse_kernel(tc, x, tab_words, tab_scales, offs, g, wdT, wl_words, wl_scales, out):
+    nc = tc.nc
+    with ExitStack() as ctx:
+        keep = ctx.enter_context(tc.tile_pool(name="keep", bufs=1))
+        psum = ctx.enter_context(tc.psum_pool(name="psum", bufs=1))
+
+        def sb(name, shape, dtype):
+            return keep.tile(shape, dtype, name=name, align_bytes=64)
+
+        def bank(i, name):
+            return psum.tile([P, 512], F32, name=name, tag="bank%d" % i)
+
+        offsets = keep.tile([P, S // 16], U16, name="offsets")
+        nc.sync.dma_start(offsets[:], offs)
+
+        tab_s = sb("tab_s", [P, T // 4], I32)
+        nc.vector.memset(tab_s[:], 0)
+        warm = sb("warm", [P, 8], F32)
+        g_rows = sb("g_rows", [P, P], F32)
+        nc.gpsimd.memset(g_rows[:], 0.0)
+        nc.scalar.activation(warm[:, 0:1], g_rows[:, 0:1], ACT.Sigmoid)
+        tab_w = []
+        for a in range(2):
+            tw = sb("tab_w%d" % a, [P, T], I32)
+            nc.sync.dma_start(tw[:], tab_words[a].rearrange("p t i -> p (t i)").bitcast(I32))
+            tab_w.append(tw)
+            if a == 0:
+                for q in range(4):
+                    nc.sync.dma_start(tab_s[32 * q : 32 * q + 8, :], tab_scales[:, 4 * q : 4 * q + 4, :].bitcast(I32))
+        x_raw = {}
+
+        def load_x(c):
+            m0, w, engines = X_CHUNKS[c]
+            for a in range(2):
+                raw = sb("x_raw%d_%d" % (c, a), [P, 4, w], F32)
+                nc.sync.dma_start(raw[:], x[PASS * a : PASS * (a + 1), m0 : m0 + w].rearrange("(p j) m -> p j m", j=4))
+                x_raw[c, a] = raw
+
+        for c in range(3):
+            load_x(c)
+        wd_raw = []
+        for h in range(2):
+            raw = sb("wd_raw%d" % h, [P, T], F32)
+            nc.sync.dma_start(raw[:], wdT[P * h : P * (h + 1), :])
+            wd_raw.append(raw)
+        for c in range(3, len(X_CHUNKS)):
+            load_x(c)
+        for b in range(2):
+            nc.sync.dma_start(
+                g_rows[4 * b : 4 * b + 4, :].rearrange("t (q r) -> t q r", r=8),
+                g[PASS * b : PASS * (b + 1)].rearrange("(q t r) -> t q r", t=4, r=8),
+            )
+        wl_w = sb("wl_w", [P, 2, N // 2], I32)
+        nc.sync.dma_start(wl_w[:], wl_words.bitcast(I32).rearrange("a p c -> p a c"))
+        wl_s = sb("wl_s", [P, 2, N // 4], I32)
+        nc.gpsimd.memset(wl_s[:], 0)
+        for q in range(4):
+            nc.sync.dma_start(wl_s[32 * q : 32 * q + 4, :, :], wl_scales[:, 4 * q : 4 * q + 4, :].bitcast(I32).rearrange("a r c -> r a c"))
+        ident = sb("ident", [P, P], F32)
+        make_identity(nc, ident[:])
+
+        v_w = [sb("v_w%d" % a, [P, S], U32) for a in range(2)]
+        listed_s = sb("listed_s", [P, S], U8)
+        v_s = sb("v_s", [P, S], U8)
+
+        def picks(b):
+            return offsets[:, 32 * b : 32 * (b + 1)]
+
+        def placed(t, b):
+            return t[:, PASS * b : PASS * (b + 1)].rearrange("p (t q r) -> p q t r", t=4, r=8)
+
+        def gather_scales(b):
+            nc.vector.tensor_copy(listed_s[:, PASS * b : PASS * (b + 1)], tab_s[:].bitcast(U8).indirect(picks(b)))
+
+        def place_scales(b):
+            js = slice(PASS * b, PASS * (b + 1))
+            nc.vector.tensor_copy(
+                v_s[:, js].bitcast(I32).rearrange("p (t q w) -> p t q w", t=4, w=2),
+                listed_s[:, js].bitcast(I32).rearrange("p (q t w) -> p t q w", t=4, w=2),
+            )
+
+        def gather_words(a, b):
+            nc.vector.tensor_copy(placed(v_w[a], b), tab_w[a][:].bitcast(U32).indirect(picks(b)))
+
+        x_w = [sb("x_w%d" % a, [P, M], U32) for a in range(2)]
+        x_s = [sb("x_s%d" % a, [P, M], U8) for a in range(2)]
+
+        def quantise_x(c):
+            m0, w, engines = X_CHUNKS[c]
+            grouped = []
+            for a in range(2):
+                xb = sb("x_b%d_%d" % (c, a), [P, w, 4], BF16)
+                if engines[a] == "G":
+                    nc.gpsimd.tensor_scalar(xb[:], x_raw[c, a][:].rearrange("p j m -> p m j"), 1.0, 0.0, ALU.mult, ALU.add)
+                else:
+                    dst = xb[:].rearrange("p (c i) j -> p c j i", i=4)
+                    src = x_raw[c, a][:].rearrange("p j (c i) -> p c j i", i=4)
+                    if engines[a] == "S":
+                        nc.scalar.copy(dst, src)
+                    else:
+                        nc.vector.tensor_copy(dst, src)
+                grouped.append(xb)
+            for a in range(2):
+                nc.vector.quantize_mx(x_w[a][:, m0 : m0 + w].bitcast(FP8X4), x_s[a][:, m0 : m0 + w], grouped[a][:].rearrange("p m j -> p (m j)"))
+
+        gather_words(0, 0)
+        gather_scales(0)
+        gather_words(1, 0)
+        place_scales(0)
+        quantise_x(0)
+        quantise_x(1)
+        gather_scales(1)
+        gather_words(0, 1)
+        place_scales(1)
+        gather_words(1, 1)
+        quantise_x(2)
+
+        def scores(name, i, b, mq):
+            acc = bank(i, "acc_" + name)
+            cols = slice(P * mq, P * (mq + 1))
+            for t in range(4):
+                js = slice(PASS * b + P * t, PASS * b + P * (t + 1))
+                for a in range(2):
+                    nc.tensor.matmul_mx(
+                        out=acc[:, P * t : P * (t + 1)],
+                        lhsT=v_w[a][:, js].bitcast(FP8X4),
+                        lhsT_scale=v_s[4 * a : P, js],
+                        rhs=x_w[a][:, cols].bitcast(FP8X4),
+                        rhs_scale=x_s[a][:, cols],
+                        start=(a == 0),
+                        stop=(a == 1),
+                    )
+            soft = sb("soft_" + name, [P, P, 4], F32)
+            a_view = acc[:].rearrange("p (t m) -> p m t", t=4)
+            nc.scalar.activation(soft[:], a_view, ACT.Sigmoid, scale=-1.0)
+            return soft, a_view
+
+        def floor_after(name, soft):
+            col = sb("floor_" + name, [P, 8], F32)
+            nc.scalar.activation(col[:, 0:1], soft[:, 0, 0:1], ACT.Copy, scale=0.0, bias=FLOOR)
+            return col[:, 0:1]
+
+        def softplus(soft, a_view, floor):
+            nc.scalar.activation(soft[:], soft[:], ACT.Ln, bias=floor)
+            nc.vector.scalar_tensor_tensor(soft[:], soft[:], -1.0, a_view, ALU.mult, ALU.max)
+
+        h_b = {(half, b): sb("h_b%d_%d" % (half, b), [P, PASS, 4], BF16) for half in range(2) for b in range(2)}
+        h_w = {(half, b): sb("h_w%d_%d" % (half, b), [P, PASS], U32) for half in range(2) for b in range(2)}
+        h_s = {(half, b): sb("h_s%d_%d" % (half, b), [P, PASS], U8) for half in range(2) for b in range(2)}
+        gains = sb("gains", [P, 8], F32)
+
+        def apply_gain(engine, soft, b, mq):
+            half, m0 = mq // 4, P * (mq % 4)
+            eng = nc.vector if engine == "V" else nc.gpsimd
+            eng.tensor_tensor(h_b[half, b][:, m0 : m0 + P, :], soft[:], gains[:, 4 * b : 4 * b + 4].unsqueeze(1).to_broadcast([P, P, 4]), ALU.mult)
+
+        def quantise_h(half, b, m0, w):
+            nc.vector.quantize_mx(
+                h_w[half, b][:, m0 : m0 + w].bitcast(FP8X4), h_s[half, b][:, m0 : m0 + w], h_b[half, b][:, m0 : m0 + w, :].rearrange("p m t -> p (m t)")
+            )
+
+        units0 = [(b, mq) for pair in range(2) for b in range(2) for mq in (2 * pair, 2 * pair + 1)]
+        done0 = [scores("0_%d" % i, i, b, mq) for i, (b, mq) in enumerate(units0)]
+        floor0 = floor_after("0", done0[-1][0])
+        for c in range(3, len(X_CHUNKS)):
+            quantise_x(c)
+        for soft, a_view in done0:
+            softplus(soft, a_view, floor0)
+
+        wd_g = [sb("wd_g%d" % h, [P, S], BF16) for h in range(2)]
+        for b in range(2):
+            for h in range(2):
+                nc.vector.tensor_copy(
+                    wd_g[h][:, PASS * b : PASS * (b + 1)].rearrange("p (u q r e) -> p q u e r", u=2, r=8, e=2),
+                    wd_raw[h][:].indirect(picks(b)),
+                )
+        wd_b = sb("wd_b", [P, 2, N, 4], BF16)
+        g_bank = bank(2, "g_bank")
+        nc.tensor.transpose(g_bank[:, 0:P], g_rows[:], ident[:])
+        nc.vector.tensor_copy(gains[:], g_bank[:, 0:8])
+        for b in range(2):
+            turned = bank(b, "turned%d" % b)
+            for h in range(2):
+                words = wd_g[h][:].bitcast(F32)
+                for u in range(2):
+                    c0 = 256 * b + P * u
+                    nc.tensor.transpose(turned[:, 256 * h + P * u : 256 * h + P * (u + 1)], words[:, c0 : c0 + P], ident[:])
+            nc.vector.tensor_copy(
+                wd_b[:, b, :, :].rearrange("p n t -> p (n t)").bitcast(F32).rearrange("p (h n u) -> p h n u", h=2, u=2),
+                turned[:].rearrange("p (h u n) -> p h n u", h=2, u=2),
+            )
+
+        units1 = [(b, mq) for mq in range(4, 8) for b in range(2)]
+        banks1 = [3, 4, 5, 6, 7, 0, 1, 2]
+        done1 = [scores("1_%d" % i, banks1[i], b, mq) for i, (b, mq) in enumerate(units1)]
+        floor1 = floor_after("1", done1[-1][0])
+
+        for i, (b, mq) in enumerate(units0):
+            apply_gain(GAIN_ENGINES[0][i], done0[i][0], b, mq)
+        for b in range(2):
+            quantise_h(0, b, 0, PASS)
+        wd_w = sb("wd_w", [P, 2 * N], U32)
+        wd_s = sb("wd_s", [P, 2 * N], U8)
+        nc.vector.quantize_mx(wd_w[:].bitcast(FP8X4), wd_s[:], wd_b[:].rearrange("p b n t -> p (b n t)"))
+
+        for soft, a_view in done1:
+            softplus(soft, a_view, floor1)
+        def intensities(name, half, m0, w, banks):
+            cols = slice(PASS * half + m0, PASS * half + m0 + w)
+            accs = [bank(banks[h], "y%s_%d" % (name, h)) for h in range(2)]
+            for a in range(2):
+                for h in range(2):
+                    nc.tensor.matmul_mx(
+                        out=accs[h][:, 0:w],
+                        lhsT=wl_w[:, a, 64 * h : 64 * (h + 1)].bitcast(U8).bitcast(FP4X4),
+                        lhsT_scale=wl_s[:, a, 32 * h : 32 * (h + 1)].bitcast(U8),
+                        rhs=x_w[a][:, cols].bitcast(FP8X4),
+                        rhs_scale=x_s[a][:, cols],
+                        start=(a == 0),
+                        stop=False,
+                    )
+            for b in range(2):
+                for h in range(2):
+                    ns = slice(N * b + P * h, N * b + P * (h + 1))
+                    nc.tensor.matmul_mx(
+                        out=accs[h][:, 0:w],
+                        lhsT=wd_w[:, ns].bitcast(FP8X4),
+                        lhsT_scale=wd_s[:, ns],
+                        rhs=h_w[half, b][:, m0 : m0 + w].bitcast(FP8X4),
+                        rhs_scale=h_s[half, b][:, m0 : m0 + w],
+                        start=False,
+                        stop=(b == 1),
+                    )
+            res = sb("res" + name, [P, 2, w], F32)
+            for h in range(2):
+                nc.scalar.activation(res[:, h, :], accs[h][:, 0:w], ACT.Exp)
+            nc.sync.dma_start(out[:, cols].rearrange("(h p) m -> p h m", h=2), res[:])
+
+        intensities("0", 0, 0, PASS, banks1[0:2])
+        y_banks = [banks1[2:4], banks1[4:6], banks1[6:8], banks1[2:4]]
+        for i, (b, mq) in enumerate(units1):
+            apply_gain(GAIN_ENGINES[1][i], done1[i][0], b, mq)
+            if i > 0:
+                quantise_h(1, units1[i - 1][0], P * (units1[i - 1][1] - 4), P)
+            if i > 0 and i % 2 == 0:
+                intensities("1_%d" % i, 1, P * (units1[i - 1][1] - 4), P, y_banks[i // 2 - 1])
+        quantise_h(1, 1, 3 * P, P)
+        intensities("1_8", 1, 3 * P, P, y_banks[3])

@@ -20,8 +20,8 @@ ALU = mybir.AluOpType
 P = 128
 PASS = 512
 FLOOR = 2.0 ** -60
-X_CHUNKS = ((0, 128, "SS"), (128, 128, "SS"), (256, 256, "SV"), (512, 256, "GG"), (768, 256, "GG"))
-GAIN_ENGINES = ("VVVVVVVV", "VVVVVVVV")
+X_CHUNKS = ((0, 256, "SS"), (256, 256, "SV"), (512, 256, "GG"), (768, 256, "GG"))
+GAIN_ENGINES = ("VVVVVVVV", "GGGGVVVV")
 
 
 def tile_list_claim_intensity_sparse_kernel(tc, x, tab_words, tab_scales, offs, g, wdT, wl_words, wl_scales, out):
@@ -41,6 +41,11 @@ def tile_list_claim_intensity_sparse_kernel(tc, x, tab_words, tab_scales, offs, 
 
         tab_s = sb("tab_s", [P, T // 4], I32)
         nc.vector.memset(tab_s[:], 0)
+        tab_rows = sb("tab_rows", [P, T // 4], I32)
+        for q in range(4):
+            nc.sync.dma_start(tab_rows[32 * q : 32 * q + 8, :], tab_scales[:, 4 * q : 4 * q + 4, :].bitcast(I32))
+        for q in range(4):
+            nc.vector.tensor_copy(tab_s[32 * q : 32 * q + 8, :], tab_rows[32 * q : 32 * q + 8, :])
         warm = sb("warm", [P, 8], F32)
         g_rows = sb("g_rows", [P, P], F32)
         nc.gpsimd.memset(g_rows[:], 0.0)
@@ -50,9 +55,6 @@ def tile_list_claim_intensity_sparse_kernel(tc, x, tab_words, tab_scales, offs, 
             tw = sb("tab_w%d" % a, [P, T], I32)
             nc.sync.dma_start(tw[:], tab_words[a].rearrange("p t i -> p (t i)").bitcast(I32))
             tab_w.append(tw)
-            if a == 0:
-                for q in range(4):
-                    nc.sync.dma_start(tab_s[32 * q : 32 * q + 8, :], tab_scales[:, 4 * q : 4 * q + 4, :].bitcast(I32))
         x_raw = {}
 
         def load_x(c):
@@ -62,14 +64,14 @@ def tile_list_claim_intensity_sparse_kernel(tc, x, tab_words, tab_scales, offs, 
                 nc.sync.dma_start(raw[:], x[PASS * a : PASS * (a + 1), m0 : m0 + w].rearrange("(p j) m -> p j m", j=4))
                 x_raw[c, a] = raw
 
-        for c in range(3):
+        for c in range(2):
             load_x(c)
         wd_raw = []
         for h in range(2):
             raw = sb("wd_raw%d" % h, [P, T], F32)
             nc.sync.dma_start(raw[:], wdT[P * h : P * (h + 1), :])
             wd_raw.append(raw)
-        for c in range(3, len(X_CHUNKS)):
+        for c in range(2, len(X_CHUNKS)):
             load_x(c)
         for b in range(2):
             nc.sync.dma_start(
@@ -129,17 +131,16 @@ def tile_list_claim_intensity_sparse_kernel(tc, x, tab_words, tab_scales, offs, 
             for a in range(2):
                 nc.vector.quantize_mx(x_w[a][:, m0 : m0 + w].bitcast(FP8X4), x_s[a][:, m0 : m0 + w], grouped[a][:].rearrange("p m j -> p (m j)"))
 
-        gather_words(0, 0)
         gather_scales(0)
+        gather_words(0, 0)
         gather_words(1, 0)
         place_scales(0)
         quantise_x(0)
-        quantise_x(1)
         gather_scales(1)
         gather_words(0, 1)
         place_scales(1)
         gather_words(1, 1)
-        quantise_x(2)
+        quantise_x(1)
 
         def scores(name, i, b, mq):
             acc = bank(i, "acc_" + name)
@@ -188,7 +189,7 @@ def tile_list_claim_intensity_sparse_kernel(tc, x, tab_words, tab_scales, offs, 
         units0 = [(b, mq) for pair in range(2) for b in range(2) for mq in (2 * pair, 2 * pair + 1)]
         done0 = [scores("0_%d" % i, i, b, mq) for i, (b, mq) in enumerate(units0)]
         floor0 = floor_after("0", done0[-1][0])
-        for c in range(3, len(X_CHUNKS)):
+        for c in range(2, len(X_CHUNKS)):
             quantise_x(c)
         for soft, a_view in done0:
             softplus(soft, a_view, floor0)

@@ -20,8 +20,9 @@ ALU = mybir.AluOpType
 P = 128
 PASS = 512
 FLOOR = 2.0 ** -60
-X_CHUNKS = ((0, 256, "SS"), (256, 256, "SV"), (512, 256, "GG"), (768, 256, "GG"))
-GAIN_ENGINES = ("VVVVVVVV", "GGGGVVVV")
+KNEE = 32.0
+CHUNK = 256
+X_CASTS = (("SS", "SG"), ("GG", "SG"), ("GG", "SG"), ("GG", "SG"))
 
 
 def tile_list_claim_intensity_sparse_kernel(tc, x, tab_words, tab_scales, offs, g, wdT, wl_words, wl_scales, out):
@@ -49,35 +50,27 @@ def tile_list_claim_intensity_sparse_kernel(tc, x, tab_words, tab_scales, offs, 
         warm = sb("warm", [P, 8], F32)
         g_rows = sb("g_rows", [P, P], F32)
         nc.gpsimd.memset(g_rows[:], 0.0)
-        nc.scalar.activation(warm[:, 0:1], g_rows[:, 0:1], ACT.Sigmoid)
         tab_w = []
         for a in range(2):
             tw = sb("tab_w%d" % a, [P, T], I32)
             nc.sync.dma_start(tw[:], tab_words[a].rearrange("p t i -> p (t i)").bitcast(I32))
             tab_w.append(tw)
-        x_raw = {}
-
-        def load_x(c):
-            m0, w, engines = X_CHUNKS[c]
-            for a in range(2):
-                raw = sb("x_raw%d_%d" % (c, a), [P, 4, w], F32)
-                nc.sync.dma_start(raw[:], x[PASS * a : PASS * (a + 1), m0 : m0 + w].rearrange("(p j) m -> p j m", j=4))
-                x_raw[c, a] = raw
-
-        for c in range(2):
-            load_x(c)
-        wd_raw = []
-        for h in range(2):
-            raw = sb("wd_raw%d" % h, [P, T], F32)
-            nc.sync.dma_start(raw[:], wdT[P * h : P * (h + 1), :])
-            wd_raw.append(raw)
-        for c in range(2, len(X_CHUNKS)):
-            load_x(c)
         for b in range(2):
             nc.sync.dma_start(
                 g_rows[4 * b : 4 * b + 4, :].rearrange("t (q r) -> t q r", r=8),
                 g[PASS * b : PASS * (b + 1)].rearrange("(q t r) -> t q r", t=4, r=8),
             )
+        x_raw = {}
+        for c in range(M // CHUNK):
+            for a in range(2):
+                raw = sb("x_raw%d_%d" % (c, a), [P, 4, CHUNK], F32)
+                nc.sync.dma_start(raw[:], x[PASS * a : PASS * (a + 1), CHUNK * c : CHUNK * (c + 1)].rearrange("(p j) m -> p j m", j=4))
+                x_raw[c, a] = raw
+        wd_raw = []
+        for h in range(2):
+            raw = sb("wd_raw%d" % h, [P, T], F32)
+            nc.sync.dma_start(raw[:], wdT[P * h : P * (h + 1), :])
+            wd_raw.append(raw)
         wl_w = sb("wl_w", [P, 2, N // 2], I32)
         nc.sync.dma_start(wl_w[:], wl_words.bitcast(I32).rearrange("a p c -> p a c"))
         wl_s = sb("wl_s", [P, 2, N // 4], I32)
@@ -86,6 +79,7 @@ def tile_list_claim_intensity_sparse_kernel(tc, x, tab_words, tab_scales, offs, 
             nc.sync.dma_start(wl_s[32 * q : 32 * q + 4, :, :], wl_scales[:, 4 * q : 4 * q + 4, :].bitcast(I32).rearrange("a r c -> r a c"))
         ident = sb("ident", [P, P], F32)
         make_identity(nc, ident[:])
+        nc.scalar.activation(warm[:, 0:1], ident[:, 0:1], ACT.Sigmoid)
 
         v_w = [sb("v_w%d" % a, [P, S], U32) for a in range(2)]
         listed_s = sb("listed_s", [P, S], U8)
@@ -110,166 +104,166 @@ def tile_list_claim_intensity_sparse_kernel(tc, x, tab_words, tab_scales, offs, 
         def gather_words(a, b):
             nc.vector.tensor_copy(placed(v_w[a], b), tab_w[a][:].bitcast(U32).indirect(picks(b)))
 
-        x_w = [sb("x_w%d" % a, [P, M], U32) for a in range(2)]
-        x_s = [sb("x_s%d" % a, [P, M], U8) for a in range(2)]
+        x_w = [sb("x_w%d" % c, [P, 2 * CHUNK], U32) for c in range(M // CHUNK)]
+        x_s = [sb("x_s%d" % c, [P, 2 * CHUNK], U8) for c in range(M // CHUNK)]
+
+        def cast_piece(engine, dst, src):
+            if engine == "G":
+                nc.gpsimd.tensor_scalar(dst, src.rearrange("p j m -> p m j"), 1.0, 0.0, ALU.mult, ALU.add)
+            else:
+                eng_copy = nc.scalar.copy if engine == "S" else nc.vector.tensor_copy
+                eng_copy(dst.rearrange("p (c i) j -> p c j i", i=4), src.rearrange("p j (c i) -> p c j i", i=4))
 
         def quantise_x(c):
-            m0, w, engines = X_CHUNKS[c]
-            grouped = []
+            xb = keep.tile([P, 2, CHUNK, 4], BF16, name="x_b%d" % c, tag="x_b", align_bytes=64)
             for a in range(2):
-                xb = sb("x_b%d_%d" % (c, a), [P, w, 4], BF16)
-                if engines[a] == "G":
-                    nc.gpsimd.tensor_scalar(xb[:], x_raw[c, a][:].rearrange("p j m -> p m j"), 1.0, 0.0, ALU.mult, ALU.add)
+                engines = X_CASTS[c][a]
+                if engines[0] == engines[1]:
+                    cast_piece(engines[0], xb[:, a, :, :], x_raw[c, a][:])
                 else:
-                    dst = xb[:].rearrange("p (c i) j -> p c j i", i=4)
-                    src = x_raw[c, a][:].rearrange("p j (c i) -> p c j i", i=4)
-                    if engines[a] == "S":
-                        nc.scalar.copy(dst, src)
-                    else:
-                        nc.vector.tensor_copy(dst, src)
-                grouped.append(xb)
-            for a in range(2):
-                nc.vector.quantize_mx(x_w[a][:, m0 : m0 + w].bitcast(FP8X4), x_s[a][:, m0 : m0 + w], grouped[a][:].rearrange("p m j -> p (m j)"))
+                    for i in range(2):
+                        cast_piece(engines[i], xb[:, a, P * i : P * (i + 1), :], x_raw[c, a][:, :, P * i : P * (i + 1)])
+            nc.vector.quantize_mx(x_w[c][:].bitcast(FP8X4), x_s[c][:], xb[:].rearrange("p a m j -> p (a m j)"))
+
+        def x_cols(a, mq):
+            c0 = CHUNK * a + P * (mq % 2)
+            return x_w[mq // 2][:, c0 : c0 + P].bitcast(FP8X4), x_s[mq // 2][:, c0 : c0 + P]
+
+        g_bank = bank(7, "g_bank")
+        nc.tensor.transpose(g_bank[:, 0:P], g_rows[:], ident[:])
+        gains = sb("gains", [P, 8], F32)
 
         gather_scales(0)
         gather_words(0, 0)
-        gather_words(1, 0)
-        place_scales(0)
-        quantise_x(0)
         gather_scales(1)
         gather_words(0, 1)
+        place_scales(0)
         place_scales(1)
+        gather_words(1, 0)
+        quantise_x(0)
         gather_words(1, 1)
-        quantise_x(1)
+        nc.vector.tensor_scalar(gains[:], g_bank[:, 0:8], -1.0 / KNEE, None, ALU.mult)
+        for c in range(1, M // CHUNK):
+            quantise_x(c)
 
-        def scores(name, i, b, mq):
-            acc = bank(i, "acc_" + name)
-            cols = slice(P * mq, P * (mq + 1))
+        units = [(b, mq) for c in range(M // CHUNK) for b in range(2) for mq in (2 * c, 2 * c + 1)]
+        units[-4:] = [(0, 6), (1, 6), (0, 7), (1, 7)]
+        soft, factor = [], []
+        for i, (b, mq) in enumerate(units):
+            acc = bank(i % 8, "acc%d" % i)
             for t in range(4):
                 js = slice(PASS * b + P * t, PASS * b + P * (t + 1))
                 for a in range(2):
+                    codes, scales = x_cols(a, mq)
                     nc.tensor.matmul_mx(
                         out=acc[:, P * t : P * (t + 1)],
                         lhsT=v_w[a][:, js].bitcast(FP8X4),
                         lhsT_scale=v_s[4 * a : P, js],
-                        rhs=x_w[a][:, cols].bitcast(FP8X4),
-                        rhs_scale=x_s[a][:, cols],
+                        rhs=codes,
+                        rhs_scale=scales,
                         start=(a == 0),
                         stop=(a == 1),
                     )
-            soft = sb("soft_" + name, [P, P, 4], F32)
             a_view = acc[:].rearrange("p (t m) -> p m t", t=4)
-            nc.scalar.activation(soft[:], a_view, ACT.Sigmoid, scale=-1.0)
-            return soft, a_view
-
-        def floor_after(name, soft):
-            col = sb("floor_" + name, [P, 8], F32)
-            nc.scalar.activation(col[:, 0:1], soft[:, 0, 0:1], ACT.Copy, scale=0.0, bias=FLOOR)
-            return col[:, 0:1]
-
-        def softplus(soft, a_view, floor):
-            nc.scalar.activation(soft[:], soft[:], ACT.Ln, bias=floor)
-            nc.vector.scalar_tensor_tensor(soft[:], soft[:], -1.0, a_view, ALU.mult, ALU.max)
-
-        h_b = {(half, b): sb("h_b%d_%d" % (half, b), [P, PASS, 4], BF16) for half in range(2) for b in range(2)}
-        h_w = {(half, b): sb("h_w%d_%d" % (half, b), [P, PASS], U32) for half in range(2) for b in range(2)}
-        h_s = {(half, b): sb("h_s%d_%d" % (half, b), [P, PASS], U8) for half in range(2) for b in range(2)}
-        gains = sb("gains", [P, 8], F32)
-
-        def apply_gain(engine, soft, b, mq):
-            half, m0 = mq // 4, P * (mq % 4)
-            eng = nc.vector if engine == "V" else nc.gpsimd
-            eng.tensor_tensor(h_b[half, b][:, m0 : m0 + P, :], soft[:], gains[:, 4 * b : 4 * b + 4].unsqueeze(1).to_broadcast([P, P, 4]), ALU.mult)
-
-        def quantise_h(half, b, m0, w):
-            nc.vector.quantize_mx(
-                h_w[half, b][:, m0 : m0 + w].bitcast(FP8X4), h_s[half, b][:, m0 : m0 + w], h_b[half, b][:, m0 : m0 + w, :].rearrange("p m t -> p (m t)")
+            soft.append(sb("soft%d" % i, [P, P, 4], F32))
+            nc.scalar.activation(soft[i][:], a_view, ACT.Sigmoid, scale=-1.0)
+            factor.append(sb("factor%d" % i, [P, P, 4], F32))
+            nc.vector.scalar_tensor_tensor(
+                factor[i][:], a_view, KNEE, gains[:, 4 * b : 4 * b + 4].unsqueeze(1).to_broadcast([P, P, 4]), ALU.max, ALU.mult
             )
-
-        units0 = [(b, mq) for pair in range(2) for b in range(2) for mq in (2 * pair, 2 * pair + 1)]
-        done0 = [scores("0_%d" % i, i, b, mq) for i, (b, mq) in enumerate(units0)]
-        floor0 = floor_after("0", done0[-1][0])
-        for c in range(2, len(X_CHUNKS)):
-            quantise_x(c)
-        for soft, a_view in done0:
-            softplus(soft, a_view, floor0)
+        floor = sb("floor", [P, 8], F32)
+        nc.scalar.activation(floor[:, 0:1], soft[-1][:, 0, 0:1], ACT.Copy, scale=0.0, bias=FLOOR)
 
         wd_g = [sb("wd_g%d" % h, [P, S], BF16) for h in range(2)]
-        for b in range(2):
-            for h in range(2):
+        for h in range(2):
+            for b in range(2):
                 nc.vector.tensor_copy(
                     wd_g[h][:, PASS * b : PASS * (b + 1)].rearrange("p (u q r e) -> p q u e r", u=2, r=8, e=2),
                     wd_raw[h][:].indirect(picks(b)),
                 )
-        wd_b = sb("wd_b", [P, 2, N, 4], BF16)
-        g_bank = bank(2, "g_bank")
-        nc.tensor.transpose(g_bank[:, 0:P], g_rows[:], ident[:])
-        nc.vector.tensor_copy(gains[:], g_bank[:, 0:8])
-        for b in range(2):
-            turned = bank(b, "turned%d" % b)
-            for h in range(2):
-                words = wd_g[h][:].bitcast(F32)
-                for u in range(2):
-                    c0 = 256 * b + P * u
-                    nc.tensor.transpose(turned[:, 256 * h + P * u : 256 * h + P * (u + 1)], words[:, c0 : c0 + P], ident[:])
-            nc.vector.tensor_copy(
-                wd_b[:, b, :, :].rearrange("p n t -> p (n t)").bitcast(F32).rearrange("p (h n u) -> p h n u", h=2, u=2),
-                turned[:].rearrange("p (h u n) -> p h n u", h=2, u=2),
-            )
-
-        units1 = [(b, mq) for mq in range(4, 8) for b in range(2)]
-        banks1 = [3, 4, 5, 6, 7, 0, 1, 2]
-        done1 = [scores("1_%d" % i, banks1[i], b, mq) for i, (b, mq) in enumerate(units1)]
-        floor1 = floor_after("1", done1[-1][0])
-
-        for i, (b, mq) in enumerate(units0):
-            apply_gain(GAIN_ENGINES[0][i], done0[i][0], b, mq)
-        for b in range(2):
-            quantise_h(0, b, 0, PASS)
+        turned = [bank(h, "turned%d" % h) for h in range(2)]
+        for h in range(2):
+            words = wd_g[h][:].bitcast(F32)
+            for i in range(4):
+                nc.tensor.transpose(turned[h][:, P * i : P * (i + 1)], words[:, P * i : P * (i + 1)], ident[:])
+        wd_b = sb("wd_b", [P, 2, 2, P, 4], BF16)
         wd_w = sb("wd_w", [P, 2 * N], U32)
         wd_s = sb("wd_s", [P, 2 * N], U8)
-        nc.vector.quantize_mx(wd_w[:].bitcast(FP8X4), wd_s[:], wd_b[:].rearrange("p b n t -> p (b n t)"))
 
-        for soft, a_view in done1:
-            softplus(soft, a_view, floor1)
-        def intensities(name, half, m0, w, banks):
-            cols = slice(PASS * half + m0, PASS * half + m0 + w)
+        def unload_wd(h):
+            nc.scalar.copy(
+                wd_b[:, h, :, :, :].rearrange("p b n t -> p (b n t)").bitcast(F32).rearrange("p (b n u) -> p b n u", b=2, u=2),
+                turned[h][:].rearrange("p (b u n) -> p b n u", b=2, u=2),
+            )
+
+        h_b = [sb("h_b%d" % c, [P, 2, CHUNK, 4], BF16) for c in range(M // CHUNK)]
+        h_w = [sb("h_w%d" % c, [P, 2 * CHUNK], U32) for c in range(M // CHUNK)]
+        h_s = [sb("h_s%d" % c, [P, 2 * CHUNK], U8) for c in range(M // CHUNK)]
+
+        def finish(i):
+            b, mq = units[i]
+            m0 = P * (mq % 2)
+            nc.vector.scalar_tensor_tensor(h_b[mq // 2][:, b, m0 : m0 + P, :], soft[i][:], -KNEE, factor[i][:], ALU.max, ALU.mult)
+
+        def quantise_h(c, c0, w):
+            nc.vector.quantize_mx(
+                h_w[c][:, c0 : c0 + w].bitcast(FP8X4), h_s[c][:, c0 : c0 + w], h_b[c][:].rearrange("p b m t -> p (b m t)")[:, 4 * c0 : 4 * (c0 + w)]
+            )
+
+        for i in range(16):
+            nc.scalar.activation(soft[i][:], soft[i][:], ACT.Ln, bias=floor[:, 0:1])
+            if i == 7:
+                unload_wd(0)
+                unload_wd(1)
+        for i in range(16):
+            finish(i)
+            if i in (4, 8, 12):
+                quantise_h(i // 4 - 1, 0, 2 * CHUNK)
+            if i == 9:
+                nc.vector.quantize_mx(wd_w[:].bitcast(FP8X4), wd_s[:], wd_b[:].rearrange("p h b n t -> p (h b n t)"))
+            if i >= 13:
+                b, mq = units[i - 1]
+                quantise_h(3, CHUNK * b + P * (mq % 2), P)
+        quantise_h(3, CHUNK + P, P)
+
+        def intensities(name, mq0, quarters, banks):
+            w = P * quarters
             accs = [bank(banks[h], "y%s_%d" % (name, h)) for h in range(2)]
-            for a in range(2):
-                for h in range(2):
-                    nc.tensor.matmul_mx(
-                        out=accs[h][:, 0:w],
-                        lhsT=wl_w[:, a, 64 * h : 64 * (h + 1)].bitcast(U8).bitcast(FP4X4),
-                        lhsT_scale=wl_s[:, a, 32 * h : 32 * (h + 1)].bitcast(U8),
-                        rhs=x_w[a][:, cols].bitcast(FP8X4),
-                        rhs_scale=x_s[a][:, cols],
-                        start=(a == 0),
-                        stop=False,
-                    )
-            for b in range(2):
-                for h in range(2):
-                    ns = slice(N * b + P * h, N * b + P * (h + 1))
-                    nc.tensor.matmul_mx(
-                        out=accs[h][:, 0:w],
-                        lhsT=wd_w[:, ns].bitcast(FP8X4),
-                        lhsT_scale=wd_s[:, ns],
-                        rhs=h_w[half, b][:, m0 : m0 + w].bitcast(FP8X4),
-                        rhs_scale=h_s[half, b][:, m0 : m0 + w],
-                        start=False,
-                        stop=(b == 1),
-                    )
+            for h in range(2):
+                for k in range(quarters):
+                    for a in range(2):
+                        codes, scales = x_cols(a, mq0 + k)
+                        nc.tensor.matmul_mx(
+                            out=accs[h][:, P * k : P * (k + 1)],
+                            lhsT=wl_w[:, a, 64 * h : 64 * (h + 1)].bitcast(U8).bitcast(FP4X4),
+                            lhsT_scale=wl_s[:, a, 32 * h : 32 * (h + 1)].bitcast(U8),
+                            rhs=codes,
+                            rhs_scale=scales,
+                            start=(k == 0 and a == 0),
+                            stop=False,
+                        )
+            step = min(w, CHUNK)
+            for m0 in range(0, w, step):
+                m = P * mq0 + m0
+                for b in range(2):
+                    c0 = CHUNK * b + m % CHUNK
+                    for h in range(2):
+                        ns = slice(N * h + P * b, N * h + P * (b + 1))
+                        nc.tensor.matmul_mx(
+                            out=accs[h][:, m0 : m0 + step],
+                            lhsT=wd_w[:, ns].bitcast(FP8X4),
+                            lhsT_scale=wd_s[:, ns],
+                            rhs=h_w[m // CHUNK][:, c0 : c0 + step].bitcast(FP8X4),
+                            rhs_scale=h_s[m // CHUNK][:, c0 : c0 + step],
+                            start=False,
+                            stop=(b == 1 and m0 + step == w),
+                        )
             res = sb("res" + name, [P, 2, w], F32)
             for h in range(2):
                 nc.scalar.activation(res[:, h, :], accs[h][:, 0:w], ACT.Exp)
-            nc.sync.dma_start(out[:, cols].rearrange("(h p) m -> p h m", h=2), res[:])
+            nc.sync.dma_start(out[:, P * mq0 : P * mq0 + w].rearrange("(h p) m -> p h m", h=2), res[:])
 
-        intensities("0", 0, 0, PASS, banks1[0:2])
-        y_banks = [banks1[2:4], banks1[4:6], banks1[6:8], banks1[2:4]]
-        for i, (b, mq) in enumerate(units1):
-            apply_gain(GAIN_ENGINES[1][i], done1[i][0], b, mq)
-            if i > 0:
-                quantise_h(1, units1[i - 1][0], P * (units1[i - 1][1] - 4), P)
-            if i > 0 and i % 2 == 0:
-                intensities("1_%d" % i, 1, P * (units1[i - 1][1] - 4), P, y_banks[i // 2 - 1])
-        quantise_h(1, 1, 3 * P, P)
-        intensities("1_8", 1, 3 * P, P, y_banks[3])
+        intensities("A", 0, 4, (2, 3))
+        intensities("B", 4, 2, (4, 5))
+        intensities("C", 6, 1, (6, 7))
+        intensities("D", 7, 1, (0, 1))

@@ -22,7 +22,10 @@ PASS = 512
 FLOOR = 2.0 ** -60
 KNEE = 32.0
 CHUNK = 256
-X_CASTS = (("SS", "SG"), ("GG", "SG"), ("GG", "SG"), ("GG", "SG"))
+X_LOADS = ((0, 2), (2, 2), (4, 2), (6, 2))
+X_CHUNKS = ((0, 2, "S", "S"), (2, 2, "G", "V"), (4, 2, "G", "SG"), (6, 2, "G", "SG"),)
+LOAD_ORDER = (("tab", 0), ("x", 0), ("tab", 1), ("g", 0), ("g", 1), ("x", 1), ("x", 2), ("x", 3), ("wd", 0), ("wd", 1))
+UNITS = tuple((b, mq) for c in range(3) for b in range(2) for mq in (2 * c, 2 * c + 1)) + ((0, 6), (1, 6), (0, 7), (1, 7))
 
 
 def tile_list_claim_intensity_sparse_kernel(tc, x, tab_words, tab_scales, offs, g, wdT, wl_words, wl_scales, out):
@@ -50,27 +53,28 @@ def tile_list_claim_intensity_sparse_kernel(tc, x, tab_words, tab_scales, offs, 
         warm = sb("warm", [P, 8], F32)
         g_rows = sb("g_rows", [P, P], F32)
         nc.gpsimd.memset(g_rows[:], 0.0)
-        tab_w = []
-        for a in range(2):
-            tw = sb("tab_w%d" % a, [P, T], I32)
-            nc.sync.dma_start(tw[:], tab_words[a].rearrange("p t i -> p (t i)").bitcast(I32))
-            tab_w.append(tw)
-        for b in range(2):
-            nc.sync.dma_start(
-                g_rows[4 * b : 4 * b + 4, :].rearrange("t (q r) -> t q r", r=8),
-                g[PASS * b : PASS * (b + 1)].rearrange("(q t r) -> t q r", t=4, r=8),
-            )
+        tab_w = {}
         x_raw = {}
-        for c in range(M // CHUNK):
-            for a in range(2):
-                raw = sb("x_raw%d_%d" % (c, a), [P, 4, CHUNK], F32)
-                nc.sync.dma_start(raw[:], x[PASS * a : PASS * (a + 1), CHUNK * c : CHUNK * (c + 1)].rearrange("(p j) m -> p j m", j=4))
-                x_raw[c, a] = raw
-        wd_raw = []
-        for h in range(2):
-            raw = sb("wd_raw%d" % h, [P, T], F32)
-            nc.sync.dma_start(raw[:], wdT[P * h : P * (h + 1), :])
-            wd_raw.append(raw)
+        wd_raw = {}
+        for kind, i in LOAD_ORDER:
+            if kind == "x":
+                mq0, quarters = X_LOADS[i]
+                for a in range(2):
+                    raw = keep.tile([P, 4, P * quarters], F32, name="x_raw%d_%d" % (i, a), tag="x_raw%d_%d" % (i, a), align_bytes=64)
+                    nc.sync.dma_start(raw[:], x[PASS * a : PASS * (a + 1), P * mq0 : P * (mq0 + quarters)].rearrange("(p j) m -> p j m", j=4))
+                    for k in range(quarters):
+                        x_raw[mq0 + k, a] = (raw, P * k)
+            elif kind == "tab":
+                tab_w[i] = sb("tab_w%d" % i, [P, T], I32)
+                nc.sync.dma_start(tab_w[i][:], tab_words[i].rearrange("p t i -> p (t i)").bitcast(I32))
+            elif kind == "g":
+                nc.sync.dma_start(
+                    g_rows[4 * i : 4 * i + 4, :].rearrange("t (q r) -> t q r", r=8),
+                    g[PASS * i : PASS * (i + 1)].rearrange("(q t r) -> t q r", t=4, r=8),
+                )
+            else:
+                wd_raw[i] = sb("wd_raw%d" % i, [P, T], F32)
+                nc.sync.dma_start(wd_raw[i][:], wdT[P * i : P * (i + 1), :])
         wl_w = sb("wl_w", [P, 2, N // 2], I32)
         nc.sync.dma_start(wl_w[:], wl_words.bitcast(I32).rearrange("a p c -> p a c"))
         wl_s = sb("wl_s", [P, 2, N // 4], I32)
@@ -81,31 +85,31 @@ def tile_list_claim_intensity_sparse_kernel(tc, x, tab_words, tab_scales, offs, 
         make_identity(nc, ident[:])
         nc.scalar.activation(warm[:, 0:1], ident[:, 0:1], ACT.Sigmoid)
 
-        v_w = [sb("v_w%d" % a, [P, S], U32) for a in range(2)]
-        listed_s = sb("listed_s", [P, S], U8)
+        v_w = {}
+        listed_s = {}
         v_s = sb("v_s", [P, S], U8)
 
         def picks(b):
             return offsets[:, 32 * b : 32 * (b + 1)]
 
-        def placed(t, b):
-            return t[:, PASS * b : PASS * (b + 1)].rearrange("p (t q r) -> p q t r", t=4, r=8)
-
-        def gather_scales(b):
-            nc.vector.tensor_copy(listed_s[:, PASS * b : PASS * (b + 1)], tab_s[:].bitcast(U8).indirect(picks(b)))
+        def gather_scales(b, tag):
+            listed_s[b] = keep.tile([P, PASS], U8, name="listed_s%d" % b, tag=tag, align_bytes=64)
+            nc.vector.tensor_copy(listed_s[b][:], tab_s[:].bitcast(U8).indirect(picks(b)))
 
         def place_scales(b):
             js = slice(PASS * b, PASS * (b + 1))
             nc.vector.tensor_copy(
                 v_s[:, js].bitcast(I32).rearrange("p (t q w) -> p t q w", t=4, w=2),
-                listed_s[:, js].bitcast(I32).rearrange("p (q t w) -> p t q w", t=4, w=2),
+                listed_s[b][:].bitcast(I32).rearrange("p (q t w) -> p t q w", t=4, w=2),
             )
 
-        def gather_words(a, b):
-            nc.vector.tensor_copy(placed(v_w[a], b), tab_w[a][:].bitcast(U32).indirect(picks(b)))
+        def gather_words(a, b, tag):
+            v_w[a, b] = keep.tile([P, PASS], U32, name="v_w%d_%d" % (a, b), tag=tag, align_bytes=64)
+            nc.vector.tensor_copy(v_w[a, b][:].rearrange("p (t q r) -> p q t r", t=4, r=8), tab_w[a][:].bitcast(U32).indirect(picks(b)))
 
-        x_w = [sb("x_w%d" % c, [P, 2 * CHUNK], U32) for c in range(M // CHUNK)]
-        x_s = [sb("x_s%d" % c, [P, 2 * CHUNK], U8) for c in range(M // CHUNK)]
+        x_w = [sb("x_w%d" % c, [P, 2 * P * chunk[1]], U32) for c, chunk in enumerate(X_CHUNKS)]
+        x_s = [sb("x_s%d" % c, [P, 2 * P * chunk[1]], U8) for c, chunk in enumerate(X_CHUNKS)]
+        chunk_of = {chunk[0] + k: (c, k) for c, chunk in enumerate(X_CHUNKS) for k in range(chunk[1])}
 
         def cast_piece(engine, dst, src):
             if engine == "G":
@@ -115,40 +119,50 @@ def tile_list_claim_intensity_sparse_kernel(tc, x, tab_words, tab_scales, offs, 
                 eng_copy(dst.rearrange("p (c i) j -> p c j i", i=4), src.rearrange("p j (c i) -> p c j i", i=4))
 
         def quantise_x(c):
-            xb = keep.tile([P, 2, CHUNK, 4], BF16, name="x_b%d" % c, tag="x_b", align_bytes=64)
+            width = P * X_CHUNKS[c][1]
+            xb = keep.tile([P, 2, width, 4], BF16, name="x_b%d" % c, tag="x_b%d" % min(c, 0), align_bytes=64)
             for a in range(2):
-                engines = X_CASTS[c][a]
-                if engines[0] == engines[1]:
-                    cast_piece(engines[0], xb[:, a, :, :], x_raw[c, a][:])
-                else:
-                    for i in range(2):
-                        cast_piece(engines[i], xb[:, a, P * i : P * (i + 1), :], x_raw[c, a][:, :, P * i : P * (i + 1)])
+                engines = X_CHUNKS[c][2 + a]
+                share = width // len(engines)
+                for i, engine in enumerate(engines):
+                    raw, m0 = x_raw[X_CHUNKS[c][0], a]
+                    cast_piece(engine, xb[:, a, share * i : share * (i + 1), :], raw[:, :, m0 + share * i : m0 + share * (i + 1)])
             nc.vector.quantize_mx(x_w[c][:].bitcast(FP8X4), x_s[c][:], xb[:].rearrange("p a m j -> p (a m j)"))
 
         def x_cols(a, mq):
-            c0 = CHUNK * a + P * (mq % 2)
-            return x_w[mq // 2][:, c0 : c0 + P].bitcast(FP8X4), x_s[mq // 2][:, c0 : c0 + P]
+            c, k = chunk_of[mq]
+            c0 = P * (X_CHUNKS[c][1] * a + k)
+            return x_w[c][:, c0 : c0 + P].bitcast(FP8X4), x_s[c][:, c0 : c0 + P]
+
+        wd_g = [sb("wd_g%d" % h, [P, S], BF16) for h in range(2)]
+
+        def gather_wd(h):
+            for b in range(2):
+                nc.vector.tensor_copy(
+                    wd_g[h][:, PASS * b : PASS * (b + 1)].rearrange("p (u q r e) -> p q u e r", u=2, r=8, e=2),
+                    wd_raw[h][:].indirect(picks(b)),
+                )
 
         g_bank = bank(7, "g_bank")
         nc.tensor.transpose(g_bank[:, 0:P], g_rows[:], ident[:])
         gains = sb("gains", [P, 8], F32)
 
-        gather_scales(0)
-        gather_words(0, 0)
-        gather_scales(1)
-        gather_words(0, 1)
+        gather_scales(0, "listed_s0")
         place_scales(0)
+        gather_scales(1, "listed_s1")
         place_scales(1)
-        gather_words(1, 0)
+        gather_words(0, 0, "v_w0_0")
+        gather_words(0, 1, "v_w0_1")
         quantise_x(0)
-        gather_words(1, 1)
+        gather_words(1, 0, "v_w1_0")
+        gather_words(1, 1, "v_w1_1")
         nc.vector.tensor_scalar(gains[:], g_bank[:, 0:8], -1.0 / KNEE, None, ALU.mult)
-        for c in range(1, M // CHUNK):
+        for c in range(1, len(X_CHUNKS)):
             quantise_x(c)
 
-        units = [(b, mq) for c in range(M // CHUNK) for b in range(2) for mq in (2 * c, 2 * c + 1)]
-        units[-4:] = [(0, 6), (1, 6), (0, 7), (1, 7)]
-        soft, factor = [], []
+        units = list(UNITS)
+        soft = [sb("soft%d" % mq, [P, 2, P, 4], F32) for mq in range(8)]
+        factor = [sb("factor%d" % mq, [P, 2, P, 4], F32) for mq in range(8)]
         for i, (b, mq) in enumerate(units):
             acc = bank(i % 8, "acc%d" % i)
             for t in range(4):
@@ -157,7 +171,7 @@ def tile_list_claim_intensity_sparse_kernel(tc, x, tab_words, tab_scales, offs, 
                     codes, scales = x_cols(a, mq)
                     nc.tensor.matmul_mx(
                         out=acc[:, P * t : P * (t + 1)],
-                        lhsT=v_w[a][:, js].bitcast(FP8X4),
+                        lhsT=v_w[a, b][:, P * t : P * (t + 1)].bitcast(FP8X4),
                         lhsT_scale=v_s[4 * a : P, js],
                         rhs=codes,
                         rhs_scale=scales,
@@ -165,22 +179,15 @@ def tile_list_claim_intensity_sparse_kernel(tc, x, tab_words, tab_scales, offs, 
                         stop=(a == 1),
                     )
             a_view = acc[:].rearrange("p (t m) -> p m t", t=4)
-            soft.append(sb("soft%d" % i, [P, P, 4], F32))
-            nc.scalar.activation(soft[i][:], a_view, ACT.Sigmoid, scale=-1.0)
-            factor.append(sb("factor%d" % i, [P, P, 4], F32))
+            nc.scalar.activation(soft[mq][:, b, :, :], a_view, ACT.Sigmoid, scale=-1.0)
             nc.vector.scalar_tensor_tensor(
-                factor[i][:], a_view, KNEE, gains[:, 4 * b : 4 * b + 4].unsqueeze(1).to_broadcast([P, P, 4]), ALU.max, ALU.mult
+                factor[mq][:, b, :, :], a_view, KNEE, gains[:, 4 * b : 4 * b + 4].unsqueeze(1).to_broadcast([P, P, 4]), ALU.max, ALU.mult
             )
         floor = sb("floor", [P, 8], F32)
-        nc.scalar.activation(floor[:, 0:1], soft[-1][:, 0, 0:1], ACT.Copy, scale=0.0, bias=FLOOR)
+        nc.scalar.activation(floor[:, 0:1], soft[-1][:, 1, 0, 0:1], ACT.Copy, scale=0.0, bias=FLOOR)
 
-        wd_g = [sb("wd_g%d" % h, [P, S], BF16) for h in range(2)]
-        for h in range(2):
-            for b in range(2):
-                nc.vector.tensor_copy(
-                    wd_g[h][:, PASS * b : PASS * (b + 1)].rearrange("p (u q r e) -> p q u e r", u=2, r=8, e=2),
-                    wd_raw[h][:].indirect(picks(b)),
-                )
+        for h in range(0, 2):
+            gather_wd(h)
         turned = [bank(h, "turned%d" % h) for h in range(2)]
         for h in range(2):
             words = wd_g[h][:].bitcast(F32)
@@ -200,31 +207,39 @@ def tile_list_claim_intensity_sparse_kernel(tc, x, tab_words, tab_scales, offs, 
         h_w = [sb("h_w%d" % c, [P, 2 * CHUNK], U32) for c in range(M // CHUNK)]
         h_s = [sb("h_s%d" % c, [P, 2 * CHUNK], U8) for c in range(M // CHUNK)]
 
-        def finish(i):
-            b, mq = units[i]
+        def finish(mq, bs):
             m0 = P * (mq % 2)
-            nc.vector.scalar_tensor_tensor(h_b[mq // 2][:, b, m0 : m0 + P, :], soft[i][:], -KNEE, factor[i][:], ALU.max, ALU.mult)
+            nc.vector.scalar_tensor_tensor(
+                h_b[mq // 2][:, bs, m0 : m0 + P, :].rearrange("p b m t -> p b (m t)"),
+                soft[mq][:, bs, :, :].rearrange("p b m t -> p b (m t)"),
+                -KNEE,
+                factor[mq][:, bs, :, :].rearrange("p b m t -> p b (m t)"),
+                ALU.max,
+                ALU.mult,
+            )
 
         def quantise_h(c, c0, w):
             nc.vector.quantize_mx(
                 h_w[c][:, c0 : c0 + w].bitcast(FP8X4), h_s[c][:, c0 : c0 + w], h_b[c][:].rearrange("p b m t -> p (b m t)")[:, 4 * c0 : 4 * (c0 + w)]
             )
 
-        for i in range(16):
-            nc.scalar.activation(soft[i][:], soft[i][:], ACT.Ln, bias=floor[:, 0:1])
-            if i == 7:
+        for mq in range(8):
+            nc.scalar.activation(soft[mq][:], soft[mq][:], ACT.Ln, bias=floor[:, 0:1])
+            if mq == 3:
                 unload_wd(0)
                 unload_wd(1)
-        for i in range(16):
-            finish(i)
-            if i in (4, 8, 12):
-                quantise_h(i // 4 - 1, 0, 2 * CHUNK)
-            if i == 9:
+        for mq in range(7):
+            finish(mq, slice(0, 2))
+            if mq in (2, 4, 6):
+                quantise_h(mq // 2 - 1, 0, 2 * CHUNK)
+            if mq == 4:
                 nc.vector.quantize_mx(wd_w[:].bitcast(FP8X4), wd_s[:], wd_b[:].rearrange("p h b n t -> p (h b n t)"))
-            if i >= 13:
-                b, mq = units[i - 1]
-                quantise_h(3, CHUNK * b + P * (mq % 2), P)
-        quantise_h(3, CHUNK + P, P)
+        finish(7, slice(0, 1))
+        for b in range(2):
+            quantise_h(3, CHUNK * b, P)
+        finish(7, slice(1, 2))
+        for b in range(2):
+            quantise_h(3, CHUNK * b + P, P)
 
         def intensities(name, mq0, quarters, banks):
             w = P * quarters

@@ -19,11 +19,11 @@ ALU = mybir.AluOpType
 
 P = 128
 PASS = 512
-FLOOR = 2.0 ** -60
+FLOOR_SCORE = -42.0
 KNEE = 32.0
 CHUNK = 256
 X_LOADS = ((0, 2), (2, 2), (4, 2), (6, 2))
-X_CHUNKS = ((0, 2, "S", "S"), (2, 2, "G", "V"), (4, 2, "G", "SG"), (6, 2, "G", "SG"),)
+X_CHUNKS = ((0, 2, "S", "S"), (2, 2, "S", "V"), (4, 2, "G", "S"), (6, 2, "G", "S"),)
 LOAD_ORDER = (("tab", 0), ("x", 0), ("tab", 1), ("g", 0), ("g", 1), ("x", 1), ("x", 2), ("x", 3), ("wd", 0), ("wd", 1))
 UNITS = tuple((b, mq) for c in range(3) for b in range(2) for mq in (2 * c, 2 * c + 1)) + ((0, 6), (1, 6), (0, 7), (1, 7))
 
@@ -50,7 +50,10 @@ def tile_list_claim_intensity_sparse_kernel(tc, x, tab_words, tab_scales, offs, 
             nc.sync.dma_start(tab_rows[32 * q : 32 * q + 8, :], tab_scales[:, 4 * q : 4 * q + 4, :].bitcast(I32))
         for q in range(4):
             nc.vector.tensor_copy(tab_s[32 * q : 32 * q + 8, :], tab_rows[32 * q : 32 * q + 8, :])
-        warm = sb("warm", [P, 8], F32)
+        low = sb("low", [P, 8], F32)
+        nc.gpsimd.memset(low[:], FLOOR_SCORE)
+        tiny = sb("tiny", [P, 8], F32)
+        nc.scalar.activation(tiny[:, 0:1], low[:, 0:1], ACT.Sigmoid)
         g_rows = sb("g_rows", [P, P], F32)
         nc.gpsimd.memset(g_rows[:], 0.0)
         tab_w = {}
@@ -83,7 +86,6 @@ def tile_list_claim_intensity_sparse_kernel(tc, x, tab_words, tab_scales, offs, 
             nc.sync.dma_start(wl_s[32 * q : 32 * q + 4, :, :], wl_scales[:, 4 * q : 4 * q + 4, :].bitcast(I32).rearrange("a r c -> r a c"))
         ident = sb("ident", [P, P], F32)
         make_identity(nc, ident[:])
-        nc.scalar.activation(warm[:, 0:1], ident[:, 0:1], ACT.Sigmoid)
 
         v_w = {}
         listed_s = {}
@@ -184,7 +186,7 @@ def tile_list_claim_intensity_sparse_kernel(tc, x, tab_words, tab_scales, offs, 
                 factor[mq][:, b, :, :], a_view, KNEE, gains[:, 4 * b : 4 * b + 4].unsqueeze(1).to_broadcast([P, P, 4]), ALU.max, ALU.mult
             )
         floor = sb("floor", [P, 8], F32)
-        nc.scalar.activation(floor[:, 0:1], soft[-1][:, 1, 0, 0:1], ACT.Copy, scale=0.0, bias=FLOOR)
+        nc.scalar.activation(floor[:, 0:1], soft[-1][:, 1, 0, 0:1], ACT.Identity, scale=0.0, bias=tiny[:, 0:1])
 
         for h in range(0, 2):
             gather_wd(h)

@@ -23,9 +23,11 @@ FLOOR_SCORE = -42.0
 KNEE = 32.0
 CHUNK = 256
 X_LOADS = ((0, 2), (2, 2), (4, 2), (6, 2))
-X_CHUNKS = ((0, 2, "S", "S"), (2, 2, "S", "V"), (4, 2, "G", "S"), (6, 2, "G", "S"),)
-LOAD_ORDER = (("tab", 0), ("x", 0), ("tab", 1), ("g", 0), ("g", 1), ("x", 1), ("x", 2), ("x", 3), ("wd", 0), ("wd", 1))
+X_CHUNKS = ((0, 2, "S", "S"), (2, 2, "S", "V"), (4, 2, "GG", "SG"), (6, 2, "GG", "SG"),)
+LOAD_ORDER = (("tab", 0), ("g", 0), ("g", 1), ("x", 0), ("tab", 1), ("x", 1), ("x", 2), ("x", 3), ("wd", 0), ("wd", 1))
 UNITS = tuple((b, mq) for c in range(3) for b in range(2) for mq in (2 * c, 2 * c + 1)) + ((0, 6), (1, 6), (0, 7), (1, 7))
+SOFT_OVER = {}
+FACTOR_OVER = {0: "x_b1", 3: "x_b2"}
 
 
 def tile_list_claim_intensity_sparse_kernel(tc, x, tab_words, tab_scales, offs, g, wdT, wl_words, wl_scales, out):
@@ -122,7 +124,7 @@ def tile_list_claim_intensity_sparse_kernel(tc, x, tab_words, tab_scales, offs, 
 
         def quantise_x(c):
             width = P * X_CHUNKS[c][1]
-            xb = keep.tile([P, 2, width, 4], BF16, name="x_b%d" % c, tag="x_b%d" % min(c, 0), align_bytes=64)
+            xb = keep.tile([P, 2, width, 4], BF16, name="x_b%d" % c, tag="x_b%d" % (0, 1, 2, 3)[c], align_bytes=64)
             for a in range(2):
                 engines = X_CHUNKS[c][2 + a]
                 share = width // len(engines)
@@ -163,8 +165,8 @@ def tile_list_claim_intensity_sparse_kernel(tc, x, tab_words, tab_scales, offs, 
             quantise_x(c)
 
         units = list(UNITS)
-        soft = [sb("soft%d" % mq, [P, 2, P, 4], F32) for mq in range(8)]
-        factor = [sb("factor%d" % mq, [P, 2, P, 4], F32) for mq in range(8)]
+        soft = [keep.tile([P, 2, P, 4], F32, name="soft%d" % mq, tag=SOFT_OVER.get(mq, "soft%d" % mq), align_bytes=64) for mq in range(8)]
+        factor = [keep.tile([P, 2, P, 4], F32, name="factor%d" % mq, tag=FACTOR_OVER.get(mq, "factor%d" % mq), align_bytes=64) for mq in range(8)]
         for i, (b, mq) in enumerate(units):
             acc = bank(i % 8, "acc%d" % i)
             for t in range(4):

@@ -22,12 +22,13 @@ PASS = 512
 FLOOR_SCORE = -42.0
 KNEE = 32.0
 CHUNK = 256
-X_LOADS = ((0, 2), (2, 2), (4, 2), (6, 2))
-X_CHUNKS = ((0, 2, "S", "S"), (2, 2, "S", "V"), (4, 2, "GG", "SG"), (6, 2, "GG", "SG"),)
-LOAD_ORDER = (("tab", 0), ("g", 0), ("g", 1), ("x", 0), ("tab", 1), ("x", 1), ("x", 2), ("x", 3), ("wd", 0), ("wd", 1))
+X_LOADS = ((0, 2), (2, 2), (4, 2), (6, 1), (7, 1))
+X_CHUNKS = ((0, 2, "S", "S"), (2, 2, "S", "V"), (4, 2, "GG", "SG"), (6, 1, "G", "S"), (7, 1, "G", "G"),)
+LOAD_ORDER = (("tab", 0), ("g", 0), ("g", 1), ("x", 0), ("tab", 1), ("x", 1), ("x", 2), ("x", 3), ("x", 4), ("wd", 0), ("wd", 1))
 UNITS = tuple((b, mq) for c in range(3) for b in range(2) for mq in (2 * c, 2 * c + 1)) + ((0, 6), (1, 6), (0, 7), (1, 7))
 SOFT_OVER = {}
 FACTOR_OVER = {0: "x_b1", 3: "x_b2"}
+WD_CASTS = "GGGV"
 
 
 def tile_list_claim_intensity_sparse_kernel(tc, x, tab_words, tab_scales, offs, g, wdT, wl_words, wl_scales, out):
@@ -78,8 +79,8 @@ def tile_list_claim_intensity_sparse_kernel(tc, x, tab_words, tab_scales, offs, 
                     g[PASS * i : PASS * (i + 1)].rearrange("(q t r) -> t q r", t=4, r=8),
                 )
             else:
-                wd_raw[i] = sb("wd_raw%d" % i, [P, T], F32)
-                nc.sync.dma_start(wd_raw[i][:], wdT[P * i : P * (i + 1), :])
+                wd_raw[i] = sb("wd_raw%d" % i, [P, 2, T // 2], F32)
+                nc.sync.dma_start(wd_raw[i][:], wdT[:, T // 2 * i : T // 2 * (i + 1)].rearrange("(h p) t -> p h t", h=2))
         wl_w = sb("wl_w", [P, 2, N // 2], I32)
         nc.sync.dma_start(wl_w[:], wl_words.bitcast(I32).rearrange("a p c -> p a c"))
         wl_s = sb("wl_s", [P, 2, N // 4], I32)
@@ -124,7 +125,7 @@ def tile_list_claim_intensity_sparse_kernel(tc, x, tab_words, tab_scales, offs, 
 
         def quantise_x(c):
             width = P * X_CHUNKS[c][1]
-            xb = keep.tile([P, 2, width, 4], BF16, name="x_b%d" % c, tag="x_b%d" % (0, 1, 2, 3)[c], align_bytes=64)
+            xb = keep.tile([P, 2, width, 4], BF16, name="x_b%d" % c, tag="x_b%d" % (0, 1, 2, 3, 4)[c], align_bytes=64)
             for a in range(2):
                 engines = X_CHUNKS[c][2 + a]
                 share = width // len(engines)
@@ -137,15 +138,6 @@ def tile_list_claim_intensity_sparse_kernel(tc, x, tab_words, tab_scales, offs, 
             c, k = chunk_of[mq]
             c0 = P * (X_CHUNKS[c][1] * a + k)
             return x_w[c][:, c0 : c0 + P].bitcast(FP8X4), x_s[c][:, c0 : c0 + P]
-
-        wd_g = [sb("wd_g%d" % h, [P, S], BF16) for h in range(2)]
-
-        def gather_wd(h):
-            for b in range(2):
-                nc.vector.tensor_copy(
-                    wd_g[h][:, PASS * b : PASS * (b + 1)].rearrange("p (u q r e) -> p q u e r", u=2, r=8, e=2),
-                    wd_raw[h][:].indirect(picks(b)),
-                )
 
         g_bank = bank(7, "g_bank")
         nc.tensor.transpose(g_bank[:, 0:P], g_rows[:], ident[:])
@@ -190,24 +182,35 @@ def tile_list_claim_intensity_sparse_kernel(tc, x, tab_words, tab_scales, offs, 
         floor = sb("floor", [P, 8], F32)
         nc.scalar.activation(floor[:, 0:1], soft[-1][:, 1, 0, 0:1], ACT.Identity, scale=0.0, bias=tiny[:, 0:1])
 
-        for h in range(0, 2):
-            gather_wd(h)
-        turned = [bank(h, "turned%d" % h) for h in range(2)]
-        for h in range(2):
-            words = wd_g[h][:].bitcast(F32)
-            for i in range(4):
-                nc.tensor.transpose(turned[h][:, P * i : P * (i + 1)], words[:, P * i : P * (i + 1)], ident[:])
+        wd_pairs = keep.tile([P, T, 2], BF16, name="wd_pairs", tag="x_b4", align_bytes=64)
+        for i, engine in enumerate(WD_CASTS):
+            share = T // len(WD_CASTS)
+            half, c0 = divmod(share * i, T // 2)
+            dst = wd_pairs[:, share * i : share * (i + 1), :]
+            src = wd_raw[half][:, :, c0 : c0 + share].rearrange("p h t -> p t h")
+            if engine == "G":
+                nc.gpsimd.tensor_copy(dst, src)
+            elif engine == "V":
+                nc.vector.tensor_copy(dst, src)
+            else:
+                nc.scalar.copy(dst, src)
+        wd_g = sb("wd_g", [P, S], U32)
+        window = wd_pairs[:].rearrange("p t h -> p (t h)").bitcast(U32)
+        for b in range(2):
+            nc.vector.tensor_copy(wd_g[:, PASS * b : PASS * (b + 1)].rearrange("p (t q r) -> p q t r", t=4, r=8), window.indirect(picks(b)))
+        turned = [bank(b, "turned%d" % b) for b in range(2)]
+        for b in range(2):
+            for t in range(4):
+                c0 = PASS * b + P * t
+                nc.tensor.transpose(turned[b][:, P * t : P * (t + 1)], wd_g[:, c0 : c0 + P].bitcast(F32), ident[:])
         wd_b = sb("wd_b", [P, 2, 2, P, 4], BF16)
         wd_w = sb("wd_w", [P, 2 * N], U32)
         wd_s = sb("wd_s", [P, 2 * N], U8)
 
-        def unload_wd(h):
-            nc.scalar.copy(
-                wd_b[:, h, :, :, :].rearrange("p b n t -> p (b n t)").bitcast(F32).rearrange("p (b n u) -> p b n u", b=2, u=2),
-                turned[h][:].rearrange("p (b u n) -> p b n u", b=2, u=2),
-            )
+        def unload_wd(b):
+            nc.scalar.copy(wd_b[:, b, :, :, :], turned[b][:].bitcast(BF16).rearrange("p (t n h) -> p h n t", t=4, h=2))
 
-        h_b = [sb("h_b%d" % c, [P, 2, CHUNK, 4], BF16) for c in range(M // CHUNK)]
+        h_b = [keep.tile([P, 2, CHUNK, 4], BF16, name="h_b%d" % c, tag="x_b4" if c == 0 else "h_b%d" % c, align_bytes=64) for c in range(M // CHUNK)]
         h_w = [sb("h_w%d" % c, [P, 2 * CHUNK], U32) for c in range(M // CHUNK)]
         h_s = [sb("h_s%d" % c, [P, 2 * CHUNK], U8) for c in range(M // CHUNK)]
 
@@ -229,15 +232,14 @@ def tile_list_claim_intensity_sparse_kernel(tc, x, tab_words, tab_scales, offs, 
 
         for mq in range(8):
             nc.scalar.activation(soft[mq][:], soft[mq][:], ACT.Ln, bias=floor[:, 0:1])
-            if mq == 3:
-                unload_wd(0)
-                unload_wd(1)
+            if mq in (2, 3):
+                unload_wd((2, 3).index(mq))
         for mq in range(7):
             finish(mq, slice(0, 2))
             if mq in (2, 4, 6):
                 quantise_h(mq // 2 - 1, 0, 2 * CHUNK)
             if mq == 4:
-                nc.vector.quantize_mx(wd_w[:].bitcast(FP8X4), wd_s[:], wd_b[:].rearrange("p h b n t -> p (h b n t)"))
+                nc.vector.quantize_mx(wd_w[:].bitcast(FP8X4), wd_s[:], wd_b[:].rearrange("p b h n t -> p (b h n t)"))
         finish(7, slice(0, 1))
         for b in range(2):
             quantise_h(3, CHUNK * b, P)
@@ -267,7 +269,7 @@ def tile_list_claim_intensity_sparse_kernel(tc, x, tab_words, tab_scales, offs, 
                 for b in range(2):
                     c0 = CHUNK * b + m % CHUNK
                     for h in range(2):
-                        ns = slice(N * h + P * b, N * h + P * (b + 1))
+                        ns = slice(N * b + P * h, N * b + P * (h + 1))
                         nc.tensor.matmul_mx(
                             out=accs[h][:, m0 : m0 + step],
                             lhsT=wd_w[:, ns].bitcast(FP8X4),
@@ -280,7 +282,10 @@ def tile_list_claim_intensity_sparse_kernel(tc, x, tab_words, tab_scales, offs, 
             res = sb("res" + name, [P, 2, w], F32)
             for h in range(2):
                 nc.scalar.activation(res[:, h, :], accs[h][:, 0:w], ACT.Exp)
-            nc.sync.dma_start(out[:, P * mq0 : P * mq0 + w].rearrange("(h p) m -> p h m", h=2), res[:])
+                if True:
+                    nc.sync.dma_start(out[P * h : P * (h + 1), P * mq0 : P * mq0 + w], res[:, h, :])
+            if not (True):
+                nc.sync.dma_start(out[:, P * mq0 : P * mq0 + w].rearrange("(h p) m -> p h m", h=2), res[:])
 
         intensities("A", 0, 4, (2, 3))
         intensities("B", 4, 2, (4, 5))

@@ -22,12 +22,12 @@ PASS = 512
 FLOOR_SCORE = -42.0
 KNEE = 32.0
 CHUNK = 256
-X_LOADS = ((0, 2), (2, 2), (4, 2), (6, 1), (7, 1))
-X_CHUNKS = ((0, 2, "S", "S"), (2, 2, "S", "V"), (4, 2, "GG", "SG"), (6, 1, "G", "S"), (7, 1, "G", "G"),)
-LOAD_ORDER = (("tab", 0), ("g", 0), ("g", 1), ("x", 0), ("tab", 1), ("x", 1), ("x", 2), ("x", 3), ("x", 4), ("wd", 0), ("wd", 1))
-UNITS = tuple((b, mq) for c in range(3) for b in range(2) for mq in (2 * c, 2 * c + 1)) + ((0, 6), (1, 6), (0, 7), (1, 7))
-SOFT_OVER = {}
-FACTOR_OVER = {0: "x_b1", 3: "x_b2"}
+X_LOADS = ((0, 1), (1, 1), (2, 2), (4, 2), (6, 2))
+X_CHUNKS = ((0, 1, "S", "SG"), (1, 1, "S", "SG"), (2, 2, "GG", "SG"), (4, 2, "GG", "SG"), (6, 2, "GG", "SG"))
+LOAD_ORDER = (("g", 0), ("tab", 0), ("tab", 1), ("x", 0), ("x", 1), ("x", 2), ("x", 3), ("x", 4), ("wd", 0), ("wd", 1), ("wd", 2), ("wd", 3))
+UNITS = tuple((b, mq) for mq in range(8) for b in range(2))
+SOFT_OVER = {1: "x_raw2_1", 3: "x_raw3_1", 5: "x_raw4_1"}
+FACTOR_OVER = {0: "x_b1", 1: "x_b2", 3: "x_b3", 5: "x_b4"}
 WD_CASTS = "GGGV"
 
 
@@ -47,7 +47,7 @@ def tile_list_claim_intensity_sparse_kernel(tc, x, tab_words, tab_scales, offs, 
         nc.sync.dma_start(offsets[:], offs)
 
         tab_s = sb("tab_s", [P, T // 4], I32)
-        nc.vector.memset(tab_s[:], 0)
+        nc.gpsimd.memset(tab_s[:], 0)
         tab_rows = sb("tab_rows", [P, T // 4], I32)
         for q in range(4):
             nc.sync.dma_start(tab_rows[32 * q : 32 * q + 8, :], tab_scales[:, 4 * q : 4 * q + 4, :].bitcast(I32))
@@ -57,7 +57,8 @@ def tile_list_claim_intensity_sparse_kernel(tc, x, tab_words, tab_scales, offs, 
         nc.gpsimd.memset(low[:], FLOOR_SCORE)
         tiny = sb("tiny", [P, 8], F32)
         nc.scalar.activation(tiny[:, 0:1], low[:, 0:1], ACT.Sigmoid)
-        g_rows = sb("g_rows", [P, P], F32)
+        g_raw = sb("g_raw", [2, PASS], F32)
+        g_rows = sb("g_rows", [P, PASS], F32)
         nc.gpsimd.memset(g_rows[:], 0.0)
         tab_w = {}
         x_raw = {}
@@ -74,13 +75,10 @@ def tile_list_claim_intensity_sparse_kernel(tc, x, tab_words, tab_scales, offs, 
                 tab_w[i] = sb("tab_w%d" % i, [P, T], I32)
                 nc.sync.dma_start(tab_w[i][:], tab_words[i].rearrange("p t i -> p (t i)").bitcast(I32))
             elif kind == "g":
-                nc.sync.dma_start(
-                    g_rows[4 * i : 4 * i + 4, :].rearrange("t (q r) -> t q r", r=8),
-                    g[PASS * i : PASS * (i + 1)].rearrange("(q t r) -> t q r", t=4, r=8),
-                )
+                nc.sync.dma_start(g_raw[:], g.rearrange("(b j) -> b j", b=2))
             else:
-                wd_raw[i] = sb("wd_raw%d" % i, [P, 2, T // 2], F32)
-                nc.sync.dma_start(wd_raw[i][:], wdT[:, T // 2 * i : T // 2 * (i + 1)].rearrange("(h p) t -> p h t", h=2))
+                wd_raw[i] = sb("wd_raw%d" % i, [P, 2, T // 4], F32)
+                nc.sync.dma_start(wd_raw[i][:], wdT[:, T // 4 * i : T // 4 * (i + 1)].rearrange("(h p) t -> p h t", h=2))
         wl_w = sb("wl_w", [P, 2, N // 2], I32)
         nc.sync.dma_start(wl_w[:], wl_words.bitcast(I32).rearrange("a p c -> p a c"))
         wl_s = sb("wl_s", [P, 2, N // 4], I32)
@@ -140,19 +138,25 @@ def tile_list_claim_intensity_sparse_kernel(tc, x, tab_words, tab_scales, offs, 
             return x_w[c][:, c0 : c0 + P].bitcast(FP8X4), x_s[c][:, c0 : c0 + P]
 
         g_bank = bank(7, "g_bank")
-        nc.tensor.transpose(g_bank[:, 0:P], g_rows[:], ident[:])
+        nc.gpsimd.tensor_copy(g_rows[0:2, :].rearrange("b (t q r) -> b t q r", t=4, r=8), g_raw[:].rearrange("b (q t r) -> b t q r", t=4, r=8))
+        for t in range(4):
+            nc.tensor.transpose(g_bank[:, P * t : P * (t + 1)], g_rows[:, P * t : P * (t + 1)], ident[:])
         gains = sb("gains", [P, 8], F32)
 
-        gather_scales(0, "listed_s0")
-        place_scales(0)
-        gather_scales(1, "listed_s1")
-        place_scales(1)
+        listed = sb("listed", [P, S], U8)
+        nc.vector.tensor_copy(listed[:], tab_s[:].bitcast(U8).indirect(offsets[:]))
+        nc.vector.tensor_copy(
+            v_s[:].bitcast(I32).rearrange("p (b t q w) -> p b t q w", b=2, t=4, w=2),
+            listed[:].bitcast(I32).rearrange("p (b q t w) -> p b t q w", b=2, t=4, w=2),
+        )
         gather_words(0, 0, "v_w0_0")
         gather_words(0, 1, "v_w0_1")
-        quantise_x(0)
         gather_words(1, 0, "v_w1_0")
-        gather_words(1, 1, "v_w1_1")
-        nc.vector.tensor_scalar(gains[:], g_bank[:, 0:8], -1.0 / KNEE, None, ALU.mult)
+        quantise_x(0)
+        gather_words(1, 1, "x_b0")
+        nc.scalar.activation(
+            gains[:].rearrange("p (b t) -> p b t", b=2), g_bank[:].rearrange("p (t k) -> p k t", t=4)[:, 0:2, :], ACT.Copy, scale=-1.0 / KNEE
+        )
         for c in range(1, len(X_CHUNKS)):
             quantise_x(c)
 
@@ -180,12 +184,12 @@ def tile_list_claim_intensity_sparse_kernel(tc, x, tab_words, tab_scales, offs, 
                 factor[mq][:, b, :, :], a_view, KNEE, gains[:, 4 * b : 4 * b + 4].unsqueeze(1).to_broadcast([P, P, 4]), ALU.max, ALU.mult
             )
         floor = sb("floor", [P, 8], F32)
-        nc.scalar.activation(floor[:, 0:1], soft[-1][:, 1, 0, 0:1], ACT.Identity, scale=0.0, bias=tiny[:, 0:1])
+        nc.scalar.activation(floor[:, 0:1], soft[-1][:, 0, 0, 0:1], ACT.Identity, scale=0.0, bias=tiny[:, 0:1])
 
-        wd_pairs = keep.tile([P, T, 2], BF16, name="wd_pairs", tag="x_b4", align_bytes=64)
+        wd_pairs = keep.tile([P, T, 2], BF16, name="wd_pairs", tag="wd_pairs", align_bytes=64)
         for i, engine in enumerate(WD_CASTS):
             share = T // len(WD_CASTS)
-            half, c0 = divmod(share * i, T // 2)
+            half, c0 = divmod(share * i, T // 4)
             dst = wd_pairs[:, share * i : share * (i + 1), :]
             src = wd_raw[half][:, :, c0 : c0 + share].rearrange("p h t -> p t h")
             if engine == "G":
@@ -210,7 +214,7 @@ def tile_list_claim_intensity_sparse_kernel(tc, x, tab_words, tab_scales, offs, 
         def unload_wd(b):
             nc.scalar.copy(wd_b[:, b, :, :, :], turned[b][:].bitcast(BF16).rearrange("p (t n h) -> p h n t", t=4, h=2))
 
-        h_b = [keep.tile([P, 2, CHUNK, 4], BF16, name="h_b%d" % c, tag="x_b4" if c == 0 else "h_b%d" % c, align_bytes=64) for c in range(M // CHUNK)]
+        h_b = [keep.tile([P, 2, CHUNK, 4], BF16, name="h_b%d" % c, tag="h_b%d" % c, align_bytes=64) for c in range(M // CHUNK)]
         h_w = [sb("h_w%d" % c, [P, 2 * CHUNK], U32) for c in range(M // CHUNK)]
         h_s = [sb("h_s%d" % c, [P, 2 * CHUNK], U8) for c in range(M // CHUNK)]
 
@@ -232,13 +236,13 @@ def tile_list_claim_intensity_sparse_kernel(tc, x, tab_words, tab_scales, offs, 
 
         for mq in range(8):
             nc.scalar.activation(soft[mq][:], soft[mq][:], ACT.Ln, bias=floor[:, 0:1])
-            if mq in (2, 3):
-                unload_wd((2, 3).index(mq))
+            if mq in (3, 4):
+                unload_wd((3, 4).index(mq))
         for mq in range(7):
             finish(mq, slice(0, 2))
             if mq in (2, 4, 6):
                 quantise_h(mq // 2 - 1, 0, 2 * CHUNK)
-            if mq == 4:
+            if mq == 5:
                 nc.vector.quantize_mx(wd_w[:].bitcast(FP8X4), wd_s[:], wd_b[:].rearrange("p b h n t -> p (b h n t)"))
         finish(7, slice(0, 1))
         for b in range(2):

@@ -23,11 +23,14 @@ FLOOR_SCORE = -42.0
 KNEE = 32.0
 CHUNK = 256
 X_LOADS = ((0, 1), (1, 1), (2, 2), (4, 2), (6, 2))
-X_CHUNKS = ((0, 1, "S", "SG"), (1, 1, "S", "SG"), (2, 2, "GG", "SG"), (4, 2, "GG", "SG"), (6, 2, "GG", "SG"))
+X_CHUNKS = ((0, 1, "S", "SG"), (1, 1, "S", "SG"), (2, 2, "GG", "SG"), (4, 2, "GG", "SG"), (6, 1, "G", "S"), (7, 1, "G", "G"))
+CAST_AT = {1: (0, 6208), 2: (6144, 14400), 3: (14336, 28736), 4: (22528, 28672), 5: (28672, 34880)}
+FACTOR_AT = {0: 2048, 1: 10240, 3: 18432, 5: 24576, 6: 30720}
+PAIRS_AT = 34816
+HELD_BYTES = 1024 + 2048 + 6 * 4096 + 4 * 4096 + 1024 + 512
 LOAD_ORDER = (("g", 0), ("tab", 0), ("tab", 1), ("x", 0), ("x", 1), ("x", 2), ("x", 3), ("x", 4), ("wd", 0), ("wd", 1), ("wd", 2), ("wd", 3))
 UNITS = tuple((b, mq) for mq in range(8) for b in range(2))
-SOFT_OVER = {1: "x_raw2_1", 3: "x_raw3_1", 5: "x_raw4_1"}
-FACTOR_OVER = {0: "x_b1", 1: "x_b2", 3: "x_b3", 5: "x_b4"}
+SOFT_OVER = {1: (2, 1), 3: (3, 1), 5: (4, 1)}
 WD_CASTS = "GGGV"
 
 
@@ -35,6 +38,8 @@ def tile_list_claim_intensity_sparse_kernel(tc, x, tab_words, tab_scales, offs, 
     nc = tc.nc
     with ExitStack() as ctx:
         keep = ctx.enter_context(tc.tile_pool(name="keep", bufs=1))
+        held = ctx.enter_context(tc.tile_pool(name="held", bufs=1))
+        cast = ctx.enter_context(tc.tile_pool(name="cast", bufs=1))
         psum = ctx.enter_context(tc.psum_pool(name="psum", bufs=1))
 
         def sb(name, shape, dtype):
@@ -47,12 +52,27 @@ def tile_list_claim_intensity_sparse_kernel(tc, x, tab_words, tab_scales, offs, 
         nc.sync.dma_start(offsets[:], offs)
 
         tab_s = sb("tab_s", [P, T // 4], I32)
-        nc.gpsimd.memset(tab_s[:], 0)
-        tab_rows = sb("tab_rows", [P, T // 4], I32)
-        for q in range(4):
-            nc.sync.dma_start(tab_rows[32 * q : 32 * q + 8, :], tab_scales[:, 4 * q : 4 * q + 4, :].bitcast(I32))
-        for q in range(4):
-            nc.vector.tensor_copy(tab_s[32 * q : 32 * q + 8, :], tab_rows[32 * q : 32 * q + 8, :])
+        nc.gpsimd.memset(tab_s[32:64, :], 0)
+        nc.gpsimd.memset(tab_s[64:128, :], 0)
+        for u in range(2):
+            for a in range(2):
+                nc.sync.dma_start(tab_s[16 * u + 8 * a : 16 * u + 8 * a + 8, :], tab_scales[a, 8 * u : 8 * u + 8, :].bitcast(I32))
+        listed = held.tile([P, HELD_BYTES], U8, name="listed", offset=0, align_bytes=64)
+        v_s = sb("v_s", [P, S], U8)
+        nc.vector.tensor_copy(listed[:, 0:S], tab_s[:].bitcast(U8).indirect(offsets[:]))
+        nc.vector.tensor_copy(
+            v_s[:].bitcast(I32).rearrange("p (b t q w) -> p b t q w", b=2, t=4, w=2),
+            listed[:, 0:S].bitcast(I32).rearrange("p (b q t w) -> p b t q w", b=2, t=4, w=2),
+        )
+        for src, dst in ((4, 32), (16, 64), (16, 92)):
+            nc.scalar.dma_start(v_s[dst : dst + 16, :].bitcast(I32), v_s[src : src + 16, :].bitcast(I32))
+        at = [S]
+        raw_at = {}
+
+        def held_tile(name, shape, dtype, size):
+            at.append(at[-1] + size)
+            return held.tile(shape, dtype, name=name, offset=at[-2], align_bytes=64)
+
         low = sb("low", [P, 8], F32)
         nc.gpsimd.memset(low[:], FLOOR_SCORE)
         tiny = sb("tiny", [P, 8], F32)
@@ -67,7 +87,11 @@ def tile_list_claim_intensity_sparse_kernel(tc, x, tab_words, tab_scales, offs, 
             if kind == "x":
                 mq0, quarters = X_LOADS[i]
                 for a in range(2):
-                    raw = keep.tile([P, 4, P * quarters], F32, name="x_raw%d_%d" % (i, a), tag="x_raw%d_%d" % (i, a), align_bytes=64)
+                    if (i, a) < (1, 1):
+                        raw = sb("x_raw%d_%d" % (i, a), [P, 4, P * quarters], F32)
+                    else:
+                        raw_at[i, a] = at[-1]
+                        raw = held_tile("x_raw%d_%d" % (i, a), [P, 4, P * quarters], F32, 2048 * quarters)
                     nc.sync.dma_start(raw[:], x[PASS * a : PASS * (a + 1), P * mq0 : P * (mq0 + quarters)].rearrange("(p j) m -> p j m", j=4))
                     for k in range(quarters):
                         x_raw[mq0 + k, a] = (raw, P * k)
@@ -77,11 +101,11 @@ def tile_list_claim_intensity_sparse_kernel(tc, x, tab_words, tab_scales, offs, 
             elif kind == "g":
                 nc.sync.dma_start(g_raw[:], g.rearrange("(b j) -> b j", b=2))
             else:
-                wd_raw[i] = sb("wd_raw%d" % i, [P, 2, T // 4], F32)
+                wd_raw[i] = held_tile("wd_raw%d" % i, [P, 2, T // 4], F32, 4096)
                 nc.sync.dma_start(wd_raw[i][:], wdT[:, T // 4 * i : T // 4 * (i + 1)].rearrange("(h p) t -> p h t", h=2))
-        wl_w = sb("wl_w", [P, 2, N // 2], I32)
+        wl_w = held_tile("wl_w", [P, 2, N // 2], I32, 1024)
         nc.sync.dma_start(wl_w[:], wl_words.bitcast(I32).rearrange("a p c -> p a c"))
-        wl_s = sb("wl_s", [P, 2, N // 4], I32)
+        wl_s = held_tile("wl_s", [P, 2, N // 4], I32, 512)
         nc.gpsimd.memset(wl_s[:], 0)
         for q in range(4):
             nc.sync.dma_start(wl_s[32 * q : 32 * q + 4, :, :], wl_scales[:, 4 * q : 4 * q + 4, :].bitcast(I32).rearrange("a r c -> r a c"))
@@ -89,22 +113,9 @@ def tile_list_claim_intensity_sparse_kernel(tc, x, tab_words, tab_scales, offs, 
         make_identity(nc, ident[:])
 
         v_w = {}
-        listed_s = {}
-        v_s = sb("v_s", [P, S], U8)
 
         def picks(b):
             return offsets[:, 32 * b : 32 * (b + 1)]
-
-        def gather_scales(b, tag):
-            listed_s[b] = keep.tile([P, PASS], U8, name="listed_s%d" % b, tag=tag, align_bytes=64)
-            nc.vector.tensor_copy(listed_s[b][:], tab_s[:].bitcast(U8).indirect(picks(b)))
-
-        def place_scales(b):
-            js = slice(PASS * b, PASS * (b + 1))
-            nc.vector.tensor_copy(
-                v_s[:, js].bitcast(I32).rearrange("p (t q w) -> p t q w", t=4, w=2),
-                listed_s[b][:].bitcast(I32).rearrange("p (q t w) -> p t q w", t=4, w=2),
-            )
 
         def gather_words(a, b, tag):
             v_w[a, b] = keep.tile([P, PASS], U32, name="v_w%d_%d" % (a, b), tag=tag, align_bytes=64)
@@ -123,14 +134,18 @@ def tile_list_claim_intensity_sparse_kernel(tc, x, tab_words, tab_scales, offs, 
 
         def quantise_x(c):
             width = P * X_CHUNKS[c][1]
-            xb = keep.tile([P, 2, width, 4], BF16, name="x_b%d" % c, tag="x_b%d" % (0, 1, 2, 3, 4)[c], align_bytes=64)
+            if c == 0:
+                flat = keep.tile([P, 8 * width], BF16, name="x_b0", tag="x_b0", align_bytes=64)
+            else:
+                flat = cast.tile([P, (CAST_AT[c][1] - CAST_AT[c][0]) // 2], BF16, name="x_b%d" % c, offset=CAST_AT[c][0], align_bytes=64)
+            xb = flat[:, 0 : 8 * width].rearrange("p (a m j) -> p a m j", a=2, j=4)
             for a in range(2):
                 engines = X_CHUNKS[c][2 + a]
                 share = width // len(engines)
                 for i, engine in enumerate(engines):
                     raw, m0 = x_raw[X_CHUNKS[c][0], a]
                     cast_piece(engine, xb[:, a, share * i : share * (i + 1), :], raw[:, :, m0 + share * i : m0 + share * (i + 1)])
-            nc.vector.quantize_mx(x_w[c][:].bitcast(FP8X4), x_s[c][:], xb[:].rearrange("p a m j -> p (a m j)"))
+            nc.vector.quantize_mx(x_w[c][:].bitcast(FP8X4), x_s[c][:], flat[:, 0 : 8 * width])
 
         def x_cols(a, mq):
             c, k = chunk_of[mq]
@@ -143,12 +158,6 @@ def tile_list_claim_intensity_sparse_kernel(tc, x, tab_words, tab_scales, offs, 
             nc.tensor.transpose(g_bank[:, P * t : P * (t + 1)], g_rows[:, P * t : P * (t + 1)], ident[:])
         gains = sb("gains", [P, 8], F32)
 
-        listed = sb("listed", [P, S], U8)
-        nc.vector.tensor_copy(listed[:], tab_s[:].bitcast(U8).indirect(offsets[:]))
-        nc.vector.tensor_copy(
-            v_s[:].bitcast(I32).rearrange("p (b t q w) -> p b t q w", b=2, t=4, w=2),
-            listed[:].bitcast(I32).rearrange("p (b q t w) -> p b t q w", b=2, t=4, w=2),
-        )
         gather_words(0, 0, "v_w0_0")
         gather_words(0, 1, "v_w0_1")
         gather_words(1, 0, "v_w1_0")
@@ -161,8 +170,14 @@ def tile_list_claim_intensity_sparse_kernel(tc, x, tab_words, tab_scales, offs, 
             quantise_x(c)
 
         units = list(UNITS)
-        soft = [keep.tile([P, 2, P, 4], F32, name="soft%d" % mq, tag=SOFT_OVER.get(mq, "soft%d" % mq), align_bytes=64) for mq in range(8)]
-        factor = [keep.tile([P, 2, P, 4], F32, name="factor%d" % mq, tag=FACTOR_OVER.get(mq, "factor%d" % mq), align_bytes=64) for mq in range(8)]
+        soft = [
+            held.tile([P, 2, P, 4], F32, name="soft%d" % mq, offset=raw_at[SOFT_OVER[mq]], align_bytes=64) if mq in SOFT_OVER else sb("soft%d" % mq, [P, 2, P, 4], F32)
+            for mq in range(8)
+        ]
+        factor = [
+            cast.tile([P, 2, P, 4], F32, name="factor%d" % mq, offset=FACTOR_AT[mq], align_bytes=64) if mq in FACTOR_AT else sb("factor%d" % mq, [P, 2, P, 4], F32)
+            for mq in range(8)
+        ]
         for i, (b, mq) in enumerate(units):
             acc = bank(i % 8, "acc%d" % i)
             for t in range(4):
@@ -172,7 +187,7 @@ def tile_list_claim_intensity_sparse_kernel(tc, x, tab_words, tab_scales, offs, 
                     nc.tensor.matmul_mx(
                         out=acc[:, P * t : P * (t + 1)],
                         lhsT=v_w[a, b][:, P * t : P * (t + 1)].bitcast(FP8X4),
-                        lhsT_scale=v_s[4 * a : P, js],
+                        lhsT_scale=v_s[8 * a : P, js],
                         rhs=codes,
                         rhs_scale=scales,
                         start=(a == 0),
@@ -186,7 +201,7 @@ def tile_list_claim_intensity_sparse_kernel(tc, x, tab_words, tab_scales, offs, 
         floor = sb("floor", [P, 8], F32)
         nc.scalar.activation(floor[:, 0:1], soft[-1][:, 0, 0, 0:1], ACT.Identity, scale=0.0, bias=tiny[:, 0:1])
 
-        wd_pairs = keep.tile([P, T, 2], BF16, name="wd_pairs", tag="wd_pairs", align_bytes=64)
+        wd_pairs = cast.tile([P, T, 2], BF16, name="wd_pairs", offset=PAIRS_AT, align_bytes=64)
         for i, engine in enumerate(WD_CASTS):
             share = T // len(WD_CASTS)
             half, c0 = divmod(share * i, T // 4)

@@ -19,31 +19,34 @@ ALU = mybir.AluOpType
 
 P = 128
 PASS = 512
+GROUPS = M // P
 FLOOR_SCORE = -42.0
 KNEE = 32.0
 CHUNK = 256
+QUARTER = 4096
+AFTER = {1: 1, 2: 2, 3: 3, 5: 4, 6: 5, 7: 6, 8: 7}
+X_AT = ((1, 23), (0, 2), (20, 24), (28, 32), (12, 16))
+WD_AT = (5, 6, 7, 8)
 X_LOADS = ((0, 1), (1, 1), (2, 2), (4, 2), (6, 2))
-X_CHUNKS = ((0, 1, "S", "SG"), (1, 1, "S", "SG"), (2, 2, "GG", "SG"), (4, 2, "GG", "SG"), (6, 1, "G", "S"), (7, 1, "G", "G"))
-CAST_AT = {1: (0, 6208), 2: (6144, 14400), 3: (14336, 28736), 4: (22528, 28672), 5: (28672, 34880)}
-FACTOR_AT = {0: 2048, 1: 10240, 3: 18432, 5: 24576, 6: 30720}
-PAIRS_AT = 34816
-HELD_BYTES = 1024 + 2048 + 6 * 4096 + 4 * 4096 + 1024 + 512
-LOAD_ORDER = (("g", 0), ("tab", 0), ("tab", 1), ("x", 0), ("x", 1), ("x", 2), ("x", 3), ("x", 4), ("wd", 0), ("wd", 1), ("wd", 2), ("wd", 3))
-UNITS = tuple((b, mq) for mq in range(8) for b in range(2))
-SOFT_OVER = {1: (2, 1), 3: (3, 1), 5: (4, 1)}
-WD_CASTS = "GGGV"
+X_CASTS = (("S", "S"), ("G", "S"), ("G", "G"), ("G", "G"), ("G", "G"), ("G", "G"), ("G", "V"), ("G", "V"))
+WD_CASTS = ("G", "G", "G", "V")
+HELD = 2
+VECTOR_FIRST = 2
+UNLOAD_AFTER = (1, 2)
 
 
 def tile_list_claim_intensity_sparse_kernel(tc, x, tab_words, tab_scales, offs, g, wdT, wl_words, wl_scales, out):
     nc = tc.nc
     with ExitStack() as ctx:
         keep = ctx.enter_context(tc.tile_pool(name="keep", bufs=1))
-        held = ctx.enter_context(tc.tile_pool(name="held", bufs=1))
-        cast = ctx.enter_context(tc.tile_pool(name="cast", bufs=1))
+        stage = ctx.enter_context(tc.tile_pool(name="stage", bufs=1))
         psum = ctx.enter_context(tc.psum_pool(name="psum", bufs=1))
 
-        def sb(name, shape, dtype):
-            return keep.tile(shape, dtype, name=name, align_bytes=64)
+        def sb(name, shape, dtype, tag=None):
+            return keep.tile(shape, dtype, name=name, tag=tag or name, align_bytes=64)
+
+        def staged(name, shape, dtype, at):
+            return stage.tile(shape, dtype, name=name, offset=at, align_bytes=64)
 
         def bank(i, name):
             return psum.tile([P, 512], F32, name=name, tag="bank%d" % i)
@@ -57,73 +60,58 @@ def tile_list_claim_intensity_sparse_kernel(tc, x, tab_words, tab_scales, offs, 
         for u in range(2):
             for a in range(2):
                 nc.sync.dma_start(tab_s[16 * u + 8 * a : 16 * u + 8 * a + 8, :], tab_scales[a, 8 * u : 8 * u + 8, :].bitcast(I32))
-        listed = held.tile([P, HELD_BYTES], U8, name="listed", offset=0, align_bytes=64)
-        v_s = sb("v_s", [P, S], U8)
-        nc.vector.tensor_copy(listed[:, 0:S], tab_s[:].bitcast(U8).indirect(offsets[:]))
-        nc.vector.tensor_copy(
-            v_s[:].bitcast(I32).rearrange("p (b t q w) -> p b t q w", b=2, t=4, w=2),
-            listed[:, 0:S].bitcast(I32).rearrange("p (b q t w) -> p b t q w", b=2, t=4, w=2),
-        )
-        for src, dst in ((4, 32), (16, 64), (16, 92)):
-            nc.scalar.dma_start(v_s[dst : dst + 16, :].bitcast(I32), v_s[src : src + 16, :].bitcast(I32))
-        at = [S]
-        raw_at = {}
+        g_raw = sb("g_raw", [2, PASS], F32)
+        nc.sync.dma_start(g_raw[:], g.rearrange("(b j) -> b j", b=2))
 
-        def held_tile(name, shape, dtype, size):
-            at.append(at[-1] + size)
-            return held.tile(shape, dtype, name=name, offset=at[-2], align_bytes=64)
+        x_raw = {}
+
+        def load_x(i):
+            k0, groups = X_LOADS[i]
+            for a in range(2):
+                name = "x_raw%d_%d" % (i, a)
+                at = X_AT[i][a] * QUARTER // 4
+                raw = staged(name, [P, 4, P * groups], F32, at)
+                nc.sync.dma_start(raw[:], x[PASS * a : PASS * (a + 1), P * k0 : P * (k0 + groups)].rearrange("(p j) m -> p j m", j=4))
+                for k in range(groups):
+                    x_raw[k0 + k, a] = raw[:, :, P * k : P * (k + 1)]
+
+        tab_w = [staged("tab_w%d" % a, [P, T], I32, QUARTER * (1 + 2 * a)) for a in range(2)]
+
+        def load_tab(a):
+            nc.sync.dma_start(tab_w[a][:], tab_words[a].rearrange("p t i -> p (t i)").bitcast(I32))
+
+        load_x(0)
+        load_tab(0)
+        load_tab(1)
 
         low = sb("low", [P, 8], F32)
         nc.gpsimd.memset(low[:], FLOOR_SCORE)
         tiny = sb("tiny", [P, 8], F32)
         nc.scalar.activation(tiny[:, 0:1], low[:, 0:1], ACT.Sigmoid)
-        g_raw = sb("g_raw", [2, PASS], F32)
-        g_rows = sb("g_rows", [P, PASS], F32)
+        g_rows = sb("g_rows", [P, PASS], F32, "v_w0_0")
         nc.gpsimd.memset(g_rows[:], 0.0)
-        tab_w = {}
-        x_raw = {}
-        wd_raw = {}
-        for kind, i in LOAD_ORDER:
-            if kind == "x":
-                mq0, quarters = X_LOADS[i]
-                for a in range(2):
-                    if (i, a) < (1, 1):
-                        raw = sb("x_raw%d_%d" % (i, a), [P, 4, P * quarters], F32)
-                    else:
-                        raw_at[i, a] = at[-1]
-                        raw = held_tile("x_raw%d_%d" % (i, a), [P, 4, P * quarters], F32, 2048 * quarters)
-                    nc.sync.dma_start(raw[:], x[PASS * a : PASS * (a + 1), P * mq0 : P * (mq0 + quarters)].rearrange("(p j) m -> p j m", j=4))
-                    for k in range(quarters):
-                        x_raw[mq0 + k, a] = (raw, P * k)
-            elif kind == "tab":
-                tab_w[i] = sb("tab_w%d" % i, [P, T], I32)
-                nc.sync.dma_start(tab_w[i][:], tab_words[i].rearrange("p t i -> p (t i)").bitcast(I32))
-            elif kind == "g":
-                nc.sync.dma_start(g_raw[:], g.rearrange("(b j) -> b j", b=2))
-            else:
-                wd_raw[i] = held_tile("wd_raw%d" % i, [P, 2, T // 4], F32, 4096)
-                nc.sync.dma_start(wd_raw[i][:], wdT[:, T // 4 * i : T // 4 * (i + 1)].rearrange("(h p) t -> p h t", h=2))
-        wl_w = held_tile("wl_w", [P, 2, N // 2], I32, 1024)
-        nc.sync.dma_start(wl_w[:], wl_words.bitcast(I32).rearrange("a p c -> p a c"))
-        wl_s = held_tile("wl_s", [P, 2, N // 4], I32, 512)
-        nc.gpsimd.memset(wl_s[:], 0)
-        for q in range(4):
-            nc.sync.dma_start(wl_s[32 * q : 32 * q + 4, :, :], wl_scales[:, 4 * q : 4 * q + 4, :].bitcast(I32).rearrange("a r c -> r a c"))
         ident = sb("ident", [P, P], F32)
         make_identity(nc, ident[:])
 
-        v_w = {}
+        listed = sb("listed", [P, S], U8)
+        v_s = sb("v_s", [P, S], U8)
+        nc.vector.tensor_copy(listed[:], tab_s[:].bitcast(U8).indirect(offsets[:]))
+        nc.vector.tensor_copy(
+            v_s[:].bitcast(I32).rearrange("p (b t q w) -> p b t q w", b=2, t=4, w=2),
+            listed[:].bitcast(I32).rearrange("p (b q t w) -> p b t q w", b=2, t=4, w=2),
+        )
 
         def picks(b):
             return offsets[:, 32 * b : 32 * (b + 1)]
 
-        def gather_words(a, b, tag):
-            v_w[a, b] = keep.tile([P, PASS], U32, name="v_w%d_%d" % (a, b), tag=tag, align_bytes=64)
+        v_w = {}
+
+        def gather_words(a, b):
+            v_w[a, b] = sb("v_w%d_%d" % (a, b), [P, PASS], U32)
             nc.vector.tensor_copy(v_w[a, b][:].rearrange("p (t q r) -> p q t r", t=4, r=8), tab_w[a][:].bitcast(U32).indirect(picks(b)))
 
-        x_w = [sb("x_w%d" % c, [P, 2 * P * chunk[1]], U32) for c, chunk in enumerate(X_CHUNKS)]
-        x_s = [sb("x_s%d" % c, [P, 2 * P * chunk[1]], U8) for c, chunk in enumerate(X_CHUNKS)]
-        chunk_of = {chunk[0] + k: (c, k) for c, chunk in enumerate(X_CHUNKS) for k in range(chunk[1])}
+        x_w = [staged("x_w0", [P, 2 * P], U32, QUARTER)] + [sb("x_w%d" % k, [P, 2 * P], U32) for k in range(1, GROUPS)]
+        x_s = [sb("x_s%d" % k, [P, 2 * P], U8) for k in range(GROUPS)]
 
         def cast_piece(engine, dst, src):
             if engine == "G":
@@ -132,147 +120,166 @@ def tile_list_claim_intensity_sparse_kernel(tc, x, tab_words, tab_scales, offs, 
                 eng_copy = nc.scalar.copy if engine == "S" else nc.vector.tensor_copy
                 eng_copy(dst.rearrange("p (c i) j -> p c j i", i=4), src.rearrange("p j (c i) -> p c j i", i=4))
 
-        def quantise_x(c):
-            width = P * X_CHUNKS[c][1]
-            if c == 0:
-                flat = keep.tile([P, 8 * width], BF16, name="x_b0", tag="x_b0", align_bytes=64)
+        def quantise_x(k):
+            if k == 0:
+                xb = staged("x_b0", [P, 2, P, 4], BF16, X_AT[3][1] * QUARTER // 4 - QUARTER // 4)
             else:
-                flat = cast.tile([P, (CAST_AT[c][1] - CAST_AT[c][0]) // 2], BF16, name="x_b%d" % c, offset=CAST_AT[c][0], align_bytes=64)
-            xb = flat[:, 0 : 8 * width].rearrange("p (a m j) -> p a m j", a=2, j=4)
+                xb = sb("x_b%d" % k, [P, 2, P, 4], BF16)
             for a in range(2):
-                engines = X_CHUNKS[c][2 + a]
-                share = width // len(engines)
+                engines = X_CASTS[k][a]
+                share = P // len(engines)
                 for i, engine in enumerate(engines):
-                    raw, m0 = x_raw[X_CHUNKS[c][0], a]
-                    cast_piece(engine, xb[:, a, share * i : share * (i + 1), :], raw[:, :, m0 + share * i : m0 + share * (i + 1)])
-            nc.vector.quantize_mx(x_w[c][:].bitcast(FP8X4), x_s[c][:], flat[:, 0 : 8 * width])
+                    cast_piece(engine, xb[:, a, share * i : share * (i + 1), :], x_raw[k, a][:, :, share * i : share * (i + 1)])
+            nc.vector.quantize_mx(x_w[k][:].bitcast(FP8X4), x_s[k][:], xb[:].rearrange("p a m j -> p (a m j)"))
 
-        def x_cols(a, mq):
-            c, k = chunk_of[mq]
-            c0 = P * (X_CHUNKS[c][1] * a + k)
-            return x_w[c][:, c0 : c0 + P].bitcast(FP8X4), x_s[c][:, c0 : c0 + P]
+        def x_cols(a, k):
+            return x_w[k][:, P * a : P * (a + 1)].bitcast(FP8X4), x_s[k][:, P * a : P * (a + 1)]
 
-        g_bank = bank(7, "g_bank")
+        g_bank = bank(0, "g_bank")
         nc.gpsimd.tensor_copy(g_rows[0:2, :].rearrange("b (t q r) -> b t q r", t=4, r=8), g_raw[:].rearrange("b (q t r) -> b t q r", t=4, r=8))
         for t in range(4):
             nc.tensor.transpose(g_bank[:, P * t : P * (t + 1)], g_rows[:, P * t : P * (t + 1)], ident[:])
-        gains = sb("gains", [P, 8], F32)
+        g_view = g_bank[:].rearrange("p (t k) -> p k t", t=4)[:, 0:2, :]
+        slopes = sb("slopes", [P, 2, 4], F32)
+        nc.scalar.activation(slopes[:], g_view, ACT.Copy, scale=-1.0 / KNEE)
+        gains = sb("gains", [P, 2, 4], F32)
+        nc.scalar.copy(gains[:], g_view)
 
-        gather_words(0, 0, "v_w0_0")
-        gather_words(0, 1, "v_w0_1")
-        gather_words(1, 0, "v_w1_0")
-        quantise_x(0)
-        gather_words(1, 1, "x_b0")
-        nc.scalar.activation(
-            gains[:].rearrange("p (b t) -> p b t", b=2), g_bank[:].rearrange("p (t k) -> p k t", t=4)[:, 0:2, :], ACT.Copy, scale=-1.0 / KNEE
-        )
-        for c in range(1, len(X_CHUNKS)):
-            quantise_x(c)
+        for src, dst in ((4, 32), (16, 64), (16, 92)):
+            nc.scalar.dma_start(v_s[dst : dst + 16, :].bitcast(I32), v_s[src : src + 16, :].bitcast(I32))
 
-        units = list(UNITS)
-        soft = [
-            held.tile([P, 2, P, 4], F32, name="soft%d" % mq, offset=raw_at[SOFT_OVER[mq]], align_bytes=64) if mq in SOFT_OVER else sb("soft%d" % mq, [P, 2, P, 4], F32)
-            for mq in range(8)
-        ]
-        factor = [
-            cast.tile([P, 2, P, 4], F32, name="factor%d" % mq, offset=FACTOR_AT[mq], align_bytes=64) if mq in FACTOR_AT else sb("factor%d" % mq, [P, 2, P, 4], F32)
-            for mq in range(8)
-        ]
-        for i, (b, mq) in enumerate(units):
-            acc = bank(i % 8, "acc%d" % i)
-            for t in range(4):
-                js = slice(PASS * b + P * t, PASS * b + P * (t + 1))
-                for a in range(2):
-                    codes, scales = x_cols(a, mq)
-                    nc.tensor.matmul_mx(
-                        out=acc[:, P * t : P * (t + 1)],
-                        lhsT=v_w[a, b][:, P * t : P * (t + 1)].bitcast(FP8X4),
-                        lhsT_scale=v_s[8 * a : P, js],
-                        rhs=codes,
-                        rhs_scale=scales,
-                        start=(a == 0),
-                        stop=(a == 1),
-                    )
-            a_view = acc[:].rearrange("p (t m) -> p m t", t=4)
-            nc.scalar.activation(soft[mq][:, b, :, :], a_view, ACT.Sigmoid, scale=-1.0)
-            nc.vector.scalar_tensor_tensor(
-                factor[mq][:, b, :, :], a_view, KNEE, gains[:, 4 * b : 4 * b + 4].unsqueeze(1).to_broadcast([P, P, 4]), ALU.max, ALU.mult
-            )
-        floor = sb("floor", [P, 8], F32)
-        nc.scalar.activation(floor[:, 0:1], soft[-1][:, 0, 0, 0:1], ACT.Identity, scale=0.0, bias=tiny[:, 0:1])
-
-        wd_pairs = cast.tile([P, T, 2], BF16, name="wd_pairs", offset=PAIRS_AT, align_bytes=64)
-        for i, engine in enumerate(WD_CASTS):
-            share = T // len(WD_CASTS)
-            half, c0 = divmod(share * i, T // 4)
-            dst = wd_pairs[:, share * i : share * (i + 1), :]
-            src = wd_raw[half][:, :, c0 : c0 + share].rearrange("p h t -> p t h")
-            if engine == "G":
-                nc.gpsimd.tensor_copy(dst, src)
-            elif engine == "V":
-                nc.vector.tensor_copy(dst, src)
-            else:
-                nc.scalar.copy(dst, src)
-        wd_g = sb("wd_g", [P, S], U32)
-        window = wd_pairs[:].rearrange("p t h -> p (t h)").bitcast(U32)
         for b in range(2):
-            nc.vector.tensor_copy(wd_g[:, PASS * b : PASS * (b + 1)].rearrange("p (t q r) -> p q t r", t=4, r=8), window.indirect(picks(b)))
+            gather_words(0, b)
+        quantise_x(0)
+        for b in range(2):
+            gather_words(1, b)
+        for i in range(1, len(X_LOADS)):
+            load_x(i)
+        for k in range(1, GROUPS):
+            quantise_x(k)
+        wd_raw = []
+        for i in range(4):
+            wd_raw.append(staged("wd_raw%d" % i, [P, 2, T // 4], F32, QUARTER * WD_AT[i]))
+            nc.sync.dma_start(wd_raw[i][:], wdT[:, T // 4 * i : T // 4 * (i + 1)].rearrange("(h p) t -> p h t", h=2))
+        wl_w = staged("wl_w", [P, 2, N // 2], I32, X_AT[-1][0] * QUARTER // 4)
+        nc.sync.dma_start(wl_w[:], wl_words.bitcast(I32).rearrange("a p c -> p a c"))
+        wl_s = staged("wl_s", [P, 2, N // 4], I32, X_AT[-1][1] * QUARTER // 4)
+
+
+        free = GROUPS - HELD
+        soft = {}
+        factor = {}
+        scores = {}
+        pair = [sb("soft%d" % k, [P, 2, P, 4], F32) for k in range(free)]
+        for k in range(GROUPS):
+            for b in range(2):
+                i = 2 * k + b
+                acc = bank(i % 8, "acc%d" % i)
+                for t in range(4):
+                    js = slice(PASS * b + P * t, PASS * b + P * (t + 1))
+                    for a in range(2):
+                        codes, scales = x_cols(a, k)
+                        nc.tensor.matmul_mx(
+                            out=acc[:, P * t : P * (t + 1)],
+                            lhsT=v_w[a, b][:, P * t : P * (t + 1)].bitcast(FP8X4),
+                            lhsT_scale=v_s[8 * a : P, js],
+                            rhs=codes,
+                            rhs_scale=scales,
+                            start=(a == 0),
+                            stop=(a == 1),
+                        )
+                scores[k, b] = acc[:].rearrange("p (t m) -> p m t", t=4)
+                if k < free:
+                    soft[k, b] = pair[k][:, b, :, :]
+                    tag = "x_b%d" % AFTER[i] if i in AFTER else None
+                    tile = sb("factor%d" % i, [P, P, 4], F32, tag)
+                    factor[k, b] = tile[:]
+                    if i >= VECTOR_FIRST:
+                        nc.scalar.activation(soft[k, b], scores[k, b], ACT.Sigmoid, scale=-1.0)
+                    nc.vector.scalar_tensor_tensor(
+                        factor[k, b], scores[k, b], KNEE, slopes[:, b, :].unsqueeze(1).to_broadcast([P, P, 4]), ALU.max, ALU.mult
+                    )
+                    if i < VECTOR_FIRST:
+                        nc.scalar.activation(soft[k, b], scores[k, b], ACT.Sigmoid, scale=-1.0)
+                else:
+                    tile = sb("held%d" % i, [P, P, 4], F32)
+                    soft[k, b] = tile[:]
+                    nc.scalar.activation(soft[k, b], scores[k, b], ACT.Sigmoid, scale=-1.0)
+        floor = sb("floor", [P, 8], F32)
+        nc.scalar.activation(floor[:, 0:1], soft[GROUPS - 1, 0][:, 0, 0:1], ACT.Identity, scale=0.0, bias=tiny[:, 0:1])
+
+        wd_pairs = sb("wd_pairs", [P, T, 2], BF16)
+        for i, engines in enumerate(WD_CASTS):
+            share = T // 4 // len(engines)
+            for e, engine in enumerate(engines):
+                dst = wd_pairs[:, T // 4 * i + share * e : T // 4 * i + share * (e + 1), :]
+                src = wd_raw[i][:, :, share * e : share * (e + 1)].rearrange("p h t -> p t h")
+                {"G": nc.gpsimd.tensor_copy, "V": nc.vector.tensor_copy, "S": nc.scalar.copy}[engine](dst, src)
+        nc.gpsimd.memset(wl_s[:], 0)
+        for q in range(4):
+            nc.sync.dma_start(wl_s[32 * q : 32 * q + 4, :, :], wl_scales[:, 4 * q : 4 * q + 4, :].bitcast(I32).rearrange("a r c -> r a c"))
+
+        h_b = [sb("h_b%d" % c, [P, 2, CHUNK, 4], BF16) for c in range(M // CHUNK)]
+        h_w = [sb("h_w%d" % c, [P, 2 * CHUNK], U32) for c in range(M // CHUNK)]
+        h_s = [sb("h_s%d" % c, [P, 2 * CHUNK], U8) for c in range(M // CHUNK)]
+
+        def h_part(k, b):
+            return h_b[k // 2][:, b, P * (k % 2) : P * (k % 2 + 1), :]
+
+        for k in range(free, GROUPS):
+            for b in range(2):
+                nc.scalar.activation(soft[k, b], soft[k, b], ACT.Ln, bias=floor[:, 0:1])
+                peak = sb("peak%d_%d" % (k, b), [P, P, 4], F32)
+                nc.vector.scalar_tensor_tensor(peak[:], soft[k, b], -1.0, scores[k, b], ALU.mult, ALU.max)
+                nc.gpsimd.tensor_tensor(h_part(k, b), peak[:], gains[:, b, :].unsqueeze(1).to_broadcast([P, P, 4]), ALU.mult)
+
+        window = wd_pairs[:].rearrange("p t h -> p (t h)").bitcast(U32)
         turned = [bank(b, "turned%d" % b) for b in range(2)]
         for b in range(2):
+            wd_g = sb("wd_g%d" % b, [P, PASS], U32, "held%d" % (2 * free + 1 + 2 * b))
+            nc.vector.tensor_copy(wd_g[:].rearrange("p (t q r) -> p q t r", t=4, r=8), window.indirect(picks(b)))
             for t in range(4):
-                c0 = PASS * b + P * t
-                nc.tensor.transpose(turned[b][:, P * t : P * (t + 1)], wd_g[:, c0 : c0 + P].bitcast(F32), ident[:])
+                nc.tensor.transpose(turned[b][:, P * t : P * (t + 1)], wd_g[:, P * t : P * (t + 1)].bitcast(F32), ident[:])
         wd_b = sb("wd_b", [P, 2, 2, P, 4], BF16)
         wd_w = sb("wd_w", [P, 2 * N], U32)
         wd_s = sb("wd_s", [P, 2 * N], U8)
 
-        def unload_wd(b):
-            nc.scalar.copy(wd_b[:, b, :, :, :], turned[b][:].bitcast(BF16).rearrange("p (t n h) -> p h n t", t=4, h=2))
-
-        h_b = [keep.tile([P, 2, CHUNK, 4], BF16, name="h_b%d" % c, tag="h_b%d" % c, align_bytes=64) for c in range(M // CHUNK)]
-        h_w = [sb("h_w%d" % c, [P, 2 * CHUNK], U32) for c in range(M // CHUNK)]
-        h_s = [sb("h_s%d" % c, [P, 2 * CHUNK], U8) for c in range(M // CHUNK)]
-
-        def finish(mq, bs):
-            m0 = P * (mq % 2)
-            nc.vector.scalar_tensor_tensor(
-                h_b[mq // 2][:, bs, m0 : m0 + P, :].rearrange("p b m t -> p b (m t)"),
-                soft[mq][:, bs, :, :].rearrange("p b m t -> p b (m t)"),
-                -KNEE,
-                factor[mq][:, bs, :, :].rearrange("p b m t -> p b (m t)"),
-                ALU.max,
-                ALU.mult,
-            )
+        def finish(k, b):
+            nc.vector.scalar_tensor_tensor(h_part(k, b), soft[k, b], -KNEE, factor[k, b], ALU.max, ALU.mult)
 
         def quantise_h(c, c0, w):
             nc.vector.quantize_mx(
                 h_w[c][:, c0 : c0 + w].bitcast(FP8X4), h_s[c][:, c0 : c0 + w], h_b[c][:].rearrange("p b m t -> p (b m t)")[:, 4 * c0 : 4 * (c0 + w)]
             )
 
-        for mq in range(8):
-            nc.scalar.activation(soft[mq][:], soft[mq][:], ACT.Ln, bias=floor[:, 0:1])
-            if mq in (3, 4):
-                unload_wd((3, 4).index(mq))
-        for mq in range(7):
-            finish(mq, slice(0, 2))
-            if mq in (2, 4, 6):
-                quantise_h(mq // 2 - 1, 0, 2 * CHUNK)
-            if mq == 5:
+        for k in range(free):
+            nc.scalar.activation(pair[k][:], pair[k][:], ACT.Ln, bias=floor[:, 0:1])
+            if k in UNLOAD_AFTER:
+                b = UNLOAD_AFTER.index(k)
+                nc.scalar.copy(wd_b[:, b, :, :, :], turned[b][:].bitcast(BF16).rearrange("p (t n h) -> p h n t", t=4, h=2))
+        last = free - 1
+        for k in range(free):
+            finish(k, 0)
+            if k == last:
+                for b in range(2):
+                    quantise_h(k // 2, CHUNK * b, P)
+            elif k % 2 == 0 and k > 0:
+                quantise_h(k // 2 - 1, 0, 2 * CHUNK)
+            elif k == 3 and HELD:
+                quantise_h(free // 2, 0, 2 * CHUNK)
+            finish(k, 1)
+            if k == 2:
                 nc.vector.quantize_mx(wd_w[:].bitcast(FP8X4), wd_s[:], wd_b[:].rearrange("p b h n t -> p (b h n t)"))
-        finish(7, slice(0, 1))
         for b in range(2):
-            quantise_h(3, CHUNK * b, P)
-        finish(7, slice(1, 2))
-        for b in range(2):
-            quantise_h(3, CHUNK * b + P, P)
+            quantise_h(last // 2, CHUNK * b + P, P)
 
-        def intensities(name, mq0, quarters, banks):
-            w = P * quarters
+        def intensities(name, k0, groups, banks):
+            w = P * groups
             accs = [bank(banks[h], "y%s_%d" % (name, h)) for h in range(2)]
             for h in range(2):
-                for k in range(quarters):
+                for k in range(groups):
                     for a in range(2):
-                        codes, scales = x_cols(a, mq0 + k)
+                        codes, scales = x_cols(a, k0 + k)
                         nc.tensor.matmul_mx(
                             out=accs[h][:, P * k : P * (k + 1)],
                             lhsT=wl_w[:, a, 64 * h : 64 * (h + 1)].bitcast(U8).bitcast(FP4X4),
@@ -284,7 +291,7 @@ def tile_list_claim_intensity_sparse_kernel(tc, x, tab_words, tab_scales, offs, 
                         )
             step = min(w, CHUNK)
             for m0 in range(0, w, step):
-                m = P * mq0 + m0
+                m = P * k0 + m0
                 for b in range(2):
                     c0 = CHUNK * b + m % CHUNK
                     for h in range(2):
@@ -301,12 +308,9 @@ def tile_list_claim_intensity_sparse_kernel(tc, x, tab_words, tab_scales, offs, 
             res = sb("res" + name, [P, 2, w], F32)
             for h in range(2):
                 nc.scalar.activation(res[:, h, :], accs[h][:, 0:w], ACT.Exp)
-                if True:
-                    nc.sync.dma_start(out[P * h : P * (h + 1), P * mq0 : P * mq0 + w], res[:, h, :])
-            if not (True):
-                nc.sync.dma_start(out[:, P * mq0 : P * mq0 + w].rearrange("(h p) m -> p h m", h=2), res[:])
+                nc.sync.dma_start(out[P * h : P * (h + 1), P * k0 : P * k0 + w], res[:, h, :])
 
-        intensities("A", 0, 4, (2, 3))
-        intensities("B", 4, 2, (4, 5))
-        intensities("C", 6, 1, (6, 7))
-        intensities("D", 7, 1, (0, 1))
+        intensities("A", 6, 2, (2, 3))
+        intensities("B", 0, 4, (4, 5))
+        intensities("C", 4, 1, (6, 7))
+        intensities("D", 5, 1, (0, 1))

@@ -24,15 +24,17 @@ FLOOR_SCORE = -42.0
 KNEE = 32.0
 CHUNK = 256
 QUARTER = 4096
+LN_AHEAD = 2
+TURN_AFTER = (0, 1)
 AFTER = {1: 1, 2: 2, 3: 3, 5: 4, 6: 5, 7: 6, 8: 7}
 X_AT = ((1, 23), (0, 2), (20, 24), (28, 32), (12, 16))
 WD_AT = (5, 6, 7, 8)
 X_LOADS = ((0, 1), (1, 1), (2, 2), (4, 2), (6, 2))
 X_CASTS = (("S", "S"), ("G", "S"), ("G", "G"), ("G", "G"), ("G", "G"), ("G", "G"), ("G", "V"), ("G", "V"))
 WD_CASTS = ("G", "G", "G", "V")
-HELD = 2
+HELD = 0
 VECTOR_FIRST = 2
-UNLOAD_AFTER = (1, 2)
+UNLOAD_AFTER = (3, 4)
 
 
 def tile_list_claim_intensity_sparse_kernel(tc, x, tab_words, tab_scales, offs, g, wdT, wl_words, wl_scales, out):
@@ -142,8 +144,6 @@ def tile_list_claim_intensity_sparse_kernel(tc, x, tab_words, tab_scales, offs, 
         g_view = g_bank[:].rearrange("p (t k) -> p k t", t=4)[:, 0:2, :]
         slopes = sb("slopes", [P, 2, 4], F32)
         nc.scalar.activation(slopes[:], g_view, ACT.Copy, scale=-1.0 / KNEE)
-        gains = sb("gains", [P, 2, 4], F32)
-        nc.scalar.copy(gains[:], g_view)
 
         for src, dst in ((4, 32), (16, 64), (16, 92)):
             nc.scalar.dma_start(v_s[dst : dst + 16, :].bitcast(I32), v_s[src : src + 16, :].bitcast(I32))
@@ -226,20 +226,15 @@ def tile_list_claim_intensity_sparse_kernel(tc, x, tab_words, tab_scales, offs, 
         def h_part(k, b):
             return h_b[k // 2][:, b, P * (k % 2) : P * (k % 2 + 1), :]
 
-        for k in range(free, GROUPS):
-            for b in range(2):
-                nc.scalar.activation(soft[k, b], soft[k, b], ACT.Ln, bias=floor[:, 0:1])
-                peak = sb("peak%d_%d" % (k, b), [P, P, 4], F32)
-                nc.vector.scalar_tensor_tensor(peak[:], soft[k, b], -1.0, scores[k, b], ALU.mult, ALU.max)
-                nc.gpsimd.tensor_tensor(h_part(k, b), peak[:], gains[:, b, :].unsqueeze(1).to_broadcast([P, P, 4]), ALU.mult)
-
         window = wd_pairs[:].rearrange("p t h -> p (t h)").bitcast(U32)
         turned = [bank(b, "turned%d" % b) for b in range(2)]
-        for b in range(2):
-            wd_g = sb("wd_g%d" % b, [P, PASS], U32, "held%d" % (2 * free + 1 + 2 * b))
+
+        def turn_wd(b):
+            wd_g = sb("wd_g%d" % b, [P, PASS], U32, "soft%d" % b)
             nc.vector.tensor_copy(wd_g[:].rearrange("p (t q r) -> p q t r", t=4, r=8), window.indirect(picks(b)))
             for t in range(4):
                 nc.tensor.transpose(turned[b][:, P * t : P * (t + 1)], wd_g[:, P * t : P * (t + 1)].bitcast(F32), ident[:])
+
         wd_b = sb("wd_b", [P, 2, 2, P, 4], BF16)
         wd_w = sb("wd_w", [P, 2 * N], U32)
         wd_s = sb("wd_s", [P, 2 * N], U8)
@@ -252,23 +247,28 @@ def tile_list_claim_intensity_sparse_kernel(tc, x, tab_words, tab_scales, offs, 
                 h_w[c][:, c0 : c0 + w].bitcast(FP8X4), h_s[c][:, c0 : c0 + w], h_b[c][:].rearrange("p b m t -> p (b m t)")[:, 4 * c0 : 4 * (c0 + w)]
             )
 
-        for k in range(free):
+        def ln(k):
             nc.scalar.activation(pair[k][:], pair[k][:], ACT.Ln, bias=floor[:, 0:1])
             if k in UNLOAD_AFTER:
                 b = UNLOAD_AFTER.index(k)
                 nc.scalar.copy(wd_b[:, b, :, :, :], turned[b][:].bitcast(BF16).rearrange("p (t n h) -> p h n t", t=4, h=2))
+
         last = free - 1
+        for k in range(LN_AHEAD):
+            ln(k)
         for k in range(free):
+            if k + LN_AHEAD < free:
+                ln(k + LN_AHEAD)
             finish(k, 0)
             if k == last:
                 for b in range(2):
                     quantise_h(k // 2, CHUNK * b, P)
             elif k % 2 == 0 and k > 0:
                 quantise_h(k // 2 - 1, 0, 2 * CHUNK)
-            elif k == 3 and HELD:
-                quantise_h(free // 2, 0, 2 * CHUNK)
             finish(k, 1)
-            if k == 2:
+            if k in TURN_AFTER:
+                turn_wd(TURN_AFTER.index(k))
+            if k == 4:
                 nc.vector.quantize_mx(wd_w[:].bitcast(FP8X4), wd_s[:], wd_b[:].rearrange("p b h n t -> p (b h n t)"))
         for b in range(2):
             quantise_h(last // 2, CHUNK * b + P, P)
@@ -310,7 +310,7 @@ def tile_list_claim_intensity_sparse_kernel(tc, x, tab_words, tab_scales, offs, 
                 nc.scalar.activation(res[:, h, :], accs[h][:, 0:w], ACT.Exp)
                 nc.sync.dma_start(out[P * h : P * (h + 1), P * k0 : P * k0 + w], res[:, h, :])
 
-        intensities("A", 6, 2, (2, 3))
-        intensities("B", 0, 4, (4, 5))
-        intensities("C", 4, 1, (6, 7))
-        intensities("D", 5, 1, (0, 1))
+        intensities("A", 0, 4, (2, 3))
+        intensities("B", 4, 2, (4, 5))
+        intensities("C", 6, 1, (6, 7))
+        intensities("D", 7, 1, (0, 1))

@@ -22,19 +22,23 @@ PASS = 512
 GROUPS = M // P
 FLOOR_SCORE = -42.0
 KNEE = 32.0
-CHUNK = 256
-QUARTER = 4096
-LN_AHEAD = 2
-TURN_AFTER = (0, 1)
-AFTER = {1: 1, 2: 2, 3: 3, 5: 4, 6: 5, 7: 6, 8: 7}
-X_AT = ((1, 23), (0, 2), (20, 24), (28, 32), (12, 16))
-WD_AT = (5, 6, 7, 8)
+KB = 1024
 X_LOADS = ((0, 1), (1, 1), (2, 2), (4, 2), (6, 2))
-X_CASTS = (("S", "S"), ("G", "S"), ("G", "G"), ("G", "G"), ("G", "G"), ("G", "G"), ("G", "V"), ("G", "V"))
+X_AT = ((0, 2), (4, 6), (8, 12), (16, 22), (26, 30))
+TAB_AT = (14, 24)
+LISTED_AT = 8
+WD_AT = (8, 12, 16, 22)
+WL_AT = (26, 30)
+CHUNKS = ((0, 1, "S", "SG"), (1, 1, "S", "SG"), (2, 2, "SG", "G"), (4, 2, "SG", "G"), (6, 1, "S", "G"), (7, 1, "G", "G"))
+CAST_AT = {1: 2048, 2: 8192, 3: 16384, 4: 24576, 5: 32768}
+FACTOR_AT = {0: 0, 1: 8192, 3: 16384, 5: 22528, 6: 30720}
+PAIRS_AT = 36864
 WD_CASTS = ("G", "G", "G", "V")
-HELD = 0
 VECTOR_FIRST = 2
 UNLOAD_AFTER = (3, 4)
+TURN_AFTER = (-1, -1)
+WD_QUANTISE_AFTER = 5
+LN_AHEAD = 2
 
 
 def tile_list_claim_intensity_sparse_kernel(tc, x, tab_words, tab_scales, offs, g, wdT, wl_words, wl_scales, out):
@@ -42,13 +46,14 @@ def tile_list_claim_intensity_sparse_kernel(tc, x, tab_words, tab_scales, offs, 
     with ExitStack() as ctx:
         keep = ctx.enter_context(tc.tile_pool(name="keep", bufs=1))
         stage = ctx.enter_context(tc.tile_pool(name="stage", bufs=1))
+        cast = ctx.enter_context(tc.tile_pool(name="cast", bufs=1))
         psum = ctx.enter_context(tc.psum_pool(name="psum", bufs=1))
 
         def sb(name, shape, dtype, tag=None):
             return keep.tile(shape, dtype, name=name, tag=tag or name, align_bytes=64)
 
-        def staged(name, shape, dtype, at):
-            return stage.tile(shape, dtype, name=name, offset=at, align_bytes=64)
+        def placed(pool, name, shape, dtype, at):
+            return pool.tile(shape, dtype, name=name, offset=at, align_bytes=64)
 
         def bank(i, name):
             return psum.tile([P, 512], F32, name=name, tag="bank%d" % i)
@@ -67,110 +72,110 @@ def tile_list_claim_intensity_sparse_kernel(tc, x, tab_words, tab_scales, offs, 
 
         x_raw = {}
 
-        def load_x(i):
+        def load_x(i, a):
             k0, groups = X_LOADS[i]
-            for a in range(2):
-                name = "x_raw%d_%d" % (i, a)
-                at = X_AT[i][a] * QUARTER // 4
-                raw = staged(name, [P, 4, P * groups], F32, at)
-                nc.sync.dma_start(raw[:], x[PASS * a : PASS * (a + 1), P * k0 : P * (k0 + groups)].rearrange("(p j) m -> p j m", j=4))
-                for k in range(groups):
-                    x_raw[k0 + k, a] = raw[:, :, P * k : P * (k + 1)]
+            raw = placed(stage, "x_raw%d_%d" % (i, a), [P, 4, P * groups], F32, KB * X_AT[i][a])
+            nc.sync.dma_start(raw[:], x[PASS * a : PASS * (a + 1), P * k0 : P * (k0 + groups)].rearrange("(p j) m -> p j m", j=4))
+            for k in range(groups):
+                x_raw[k0 + k, a] = (raw, P * k)
 
-        tab_w = [staged("tab_w%d" % a, [P, T], I32, QUARTER * (1 + 2 * a)) for a in range(2)]
-
-        def load_tab(a):
+        tab_w = [placed(stage, "tab_w%d" % a, [P, T], I32, KB * TAB_AT[a]) for a in range(2)]
+        for a in range(2):
             nc.sync.dma_start(tab_w[a][:], tab_words[a].rearrange("p t i -> p (t i)").bitcast(I32))
-
-        load_x(0)
-        load_tab(0)
-        load_tab(1)
+        for i, a in ((0, 0), (0, 1), (1, 0)):
+            load_x(i, a)
 
         low = sb("low", [P, 8], F32)
         nc.gpsimd.memset(low[:], FLOOR_SCORE)
         tiny = sb("tiny", [P, 8], F32)
         nc.scalar.activation(tiny[:, 0:1], low[:, 0:1], ACT.Sigmoid)
-        g_rows = sb("g_rows", [P, PASS], F32, "v_w0_0")
+        g_rows = sb("g_rows", [P, PASS], F32, "v_w0_1")
         nc.gpsimd.memset(g_rows[:], 0.0)
         ident = sb("ident", [P, P], F32)
         make_identity(nc, ident[:])
 
-        listed = sb("listed", [P, S], U8)
+        listed = placed(stage, "listed", [P, S], U8, KB * LISTED_AT - S // 2)
         v_s = sb("v_s", [P, S], U8)
         nc.vector.tensor_copy(listed[:], tab_s[:].bitcast(U8).indirect(offsets[:]))
         nc.vector.tensor_copy(
             v_s[:].bitcast(I32).rearrange("p (b t q w) -> p b t q w", b=2, t=4, w=2),
             listed[:].bitcast(I32).rearrange("p (b q t w) -> p b t q w", b=2, t=4, w=2),
         )
+        for src, dst in ((4, 32), (16, 64), (16, 92)):
+            nc.sync.dma_start(v_s[dst : dst + 16, :].bitcast(I32), v_s[src : src + 16, :].bitcast(I32))
+
+        g_bank = bank(0, "g_bank")
+        nc.gpsimd.tensor_copy(g_rows[0:2, :].rearrange("b (t q r) -> b t q r", t=4, r=8), g_raw[:].rearrange("b (q t r) -> b t q r", t=4, r=8))
+        for t in range(4):
+            nc.tensor.transpose(g_bank[:, P * t : P * (t + 1)], g_rows[:, P * t : P * (t + 1)], ident[:])
+        slopes = sb("slopes", [P, 2, 4], F32)
+        nc.scalar.activation(slopes[:], g_bank[:].rearrange("p (t k) -> p k t", t=4)[:, 0:2, :], ACT.Copy, scale=-1.0 / KNEE)
 
         def picks(b):
             return offsets[:, 32 * b : 32 * (b + 1)]
 
         v_w = {}
 
-        def gather_words(a, b):
-            v_w[a, b] = sb("v_w%d_%d" % (a, b), [P, PASS], U32)
+        def gather_words(a, b, tag):
+            v_w[a, b] = sb("v_w%d_%d" % (a, b), [P, PASS], U32, tag)
             nc.vector.tensor_copy(v_w[a, b][:].rearrange("p (t q r) -> p q t r", t=4, r=8), tab_w[a][:].bitcast(U32).indirect(picks(b)))
 
-        x_w = [staged("x_w0", [P, 2 * P], U32, QUARTER)] + [sb("x_w%d" % k, [P, 2 * P], U32) for k in range(1, GROUPS)]
-        x_s = [sb("x_s%d" % k, [P, 2 * P], U8) for k in range(GROUPS)]
+        x_w = [sb("x_w%d" % c, [P, 2 * P * chunk[1]], U32) for c, chunk in enumerate(CHUNKS)]
+        x_s = [sb("x_s%d" % c, [P, 2 * P * chunk[1]], U8) for c, chunk in enumerate(CHUNKS)]
+        chunk_of = {chunk[0] + k: (c, k) for c, chunk in enumerate(CHUNKS) for k in range(chunk[1])}
 
         def cast_piece(engine, dst, src):
             if engine == "G":
-                nc.gpsimd.tensor_scalar(dst, src.rearrange("p j m -> p m j"), 1.0, 0.0, ALU.mult, ALU.add)
+                nc.gpsimd.tensor_copy(dst, src.rearrange("p j m -> p m j"))
             else:
                 eng_copy = nc.scalar.copy if engine == "S" else nc.vector.tensor_copy
                 eng_copy(dst.rearrange("p (c i) j -> p c j i", i=4), src.rearrange("p j (c i) -> p c j i", i=4))
 
-        def quantise_x(k):
-            if k == 0:
-                xb = staged("x_b0", [P, 2, P, 4], BF16, X_AT[3][1] * QUARTER // 4 - QUARTER // 4)
+        def quantise_x(c):
+            k0, groups = CHUNKS[c][:2]
+            width = P * groups
+            if c == 0:
+                flat = sb("x_b0", [P, 8 * width], BF16)
             else:
-                xb = sb("x_b%d" % k, [P, 2, P, 4], BF16)
+                flat = placed(cast, "x_b%d" % c, [P, 8 * width], BF16, CAST_AT[c])
+            xb = flat[:].rearrange("p (a m j) -> p a m j", a=2, j=4)
             for a in range(2):
-                engines = X_CASTS[k][a]
-                share = P // len(engines)
+                engines = CHUNKS[c][2 + a]
+                share = width // len(engines)
+                raw, m0 = x_raw[k0, a]
                 for i, engine in enumerate(engines):
-                    cast_piece(engine, xb[:, a, share * i : share * (i + 1), :], x_raw[k, a][:, :, share * i : share * (i + 1)])
-            nc.vector.quantize_mx(x_w[k][:].bitcast(FP8X4), x_s[k][:], xb[:].rearrange("p a m j -> p (a m j)"))
+                    cast_piece(engine, xb[:, a, share * i : share * (i + 1), :], raw[:, :, m0 + share * i : m0 + share * (i + 1)])
+            nc.vector.quantize_mx(x_w[c][:].bitcast(FP8X4), x_s[c][:], flat[:])
 
         def x_cols(a, k):
-            return x_w[k][:, P * a : P * (a + 1)].bitcast(FP8X4), x_s[k][:, P * a : P * (a + 1)]
+            c, i = chunk_of[k]
+            c0 = P * (CHUNKS[c][1] * a + i)
+            return x_w[c][:, c0 : c0 + P].bitcast(FP8X4), x_s[c][:, c0 : c0 + P]
 
-        g_bank = bank(0, "g_bank")
-        nc.gpsimd.tensor_copy(g_rows[0:2, :].rearrange("b (t q r) -> b t q r", t=4, r=8), g_raw[:].rearrange("b (q t r) -> b t q r", t=4, r=8))
-        for t in range(4):
-            nc.tensor.transpose(g_bank[:, P * t : P * (t + 1)], g_rows[:, P * t : P * (t + 1)], ident[:])
-        g_view = g_bank[:].rearrange("p (t k) -> p k t", t=4)[:, 0:2, :]
-        slopes = sb("slopes", [P, 2, 4], F32)
-        nc.scalar.activation(slopes[:], g_view, ACT.Copy, scale=-1.0 / KNEE)
-
-        for src, dst in ((4, 32), (16, 64), (16, 92)):
-            nc.scalar.dma_start(v_s[dst : dst + 16, :].bitcast(I32), v_s[src : src + 16, :].bitcast(I32))
-
-        for b in range(2):
-            gather_words(0, b)
+        gather_words(0, 0, None)
+        gather_words(0, 1, None)
+        gather_words(1, 0, None)
         quantise_x(0)
-        for b in range(2):
-            gather_words(1, b)
-        for i in range(1, len(X_LOADS)):
-            load_x(i)
-        for k in range(1, GROUPS):
-            quantise_x(k)
+        gather_words(1, 1, "x_b0")
+        load_x(1, 1)
+        for i in range(2, len(X_LOADS)):
+            for a in range(2):
+                load_x(i, a)
+        for c in range(1, len(CHUNKS)):
+            quantise_x(c)
         wd_raw = []
         for i in range(4):
-            wd_raw.append(staged("wd_raw%d" % i, [P, 2, T // 4], F32, QUARTER * WD_AT[i]))
+            wd_raw.append(placed(stage, "wd_raw%d" % i, [P, 2, T // 4], F32, KB * WD_AT[i]))
             nc.sync.dma_start(wd_raw[i][:], wdT[:, T // 4 * i : T // 4 * (i + 1)].rearrange("(h p) t -> p h t", h=2))
-        wl_w = staged("wl_w", [P, 2, N // 2], I32, X_AT[-1][0] * QUARTER // 4)
+        wl_w = placed(stage, "wl_w", [P, 2, N // 2], I32, KB * WL_AT[0])
         nc.sync.dma_start(wl_w[:], wl_words.bitcast(I32).rearrange("a p c -> p a c"))
-        wl_s = staged("wl_s", [P, 2, N // 4], I32, X_AT[-1][1] * QUARTER // 4)
+        wl_s = placed(stage, "wl_s", [P, 2, N // 4], I32, KB * WL_AT[1])
 
-
-        free = GROUPS - HELD
-        soft = {}
-        factor = {}
-        scores = {}
-        pair = [sb("soft%d" % k, [P, 2, P, 4], F32) for k in range(free)]
+        soft = [sb("soft%d" % k, [P, 2, P, 4], F32) for k in range(GROUPS)]
+        factor = [
+            placed(cast, "factor%d" % k, [P, 2, P, 4], F32, FACTOR_AT[k]) if k in FACTOR_AT else sb("factor%d" % k, [P, 2, P, 4], F32)
+            for k in range(GROUPS)
+        ]
         for k in range(GROUPS):
             for b in range(2):
                 i = 2 * k + b
@@ -188,27 +193,18 @@ def tile_list_claim_intensity_sparse_kernel(tc, x, tab_words, tab_scales, offs, 
                             start=(a == 0),
                             stop=(a == 1),
                         )
-                scores[k, b] = acc[:].rearrange("p (t m) -> p m t", t=4)
-                if k < free:
-                    soft[k, b] = pair[k][:, b, :, :]
-                    tag = "x_b%d" % AFTER[i] if i in AFTER else None
-                    tile = sb("factor%d" % i, [P, P, 4], F32, tag)
-                    factor[k, b] = tile[:]
-                    if i >= VECTOR_FIRST:
-                        nc.scalar.activation(soft[k, b], scores[k, b], ACT.Sigmoid, scale=-1.0)
-                    nc.vector.scalar_tensor_tensor(
-                        factor[k, b], scores[k, b], KNEE, slopes[:, b, :].unsqueeze(1).to_broadcast([P, P, 4]), ALU.max, ALU.mult
-                    )
-                    if i < VECTOR_FIRST:
-                        nc.scalar.activation(soft[k, b], scores[k, b], ACT.Sigmoid, scale=-1.0)
-                else:
-                    tile = sb("held%d" % i, [P, P, 4], F32)
-                    soft[k, b] = tile[:]
-                    nc.scalar.activation(soft[k, b], scores[k, b], ACT.Sigmoid, scale=-1.0)
+                scores = acc[:].rearrange("p (t m) -> p m t", t=4)
+                if i >= VECTOR_FIRST:
+                    nc.scalar.activation(soft[k][:, b, :, :], scores, ACT.Sigmoid, scale=-1.0)
+                nc.vector.scalar_tensor_tensor(
+                    factor[k][:, b, :, :], scores, KNEE, slopes[:, b, :].unsqueeze(1).to_broadcast([P, P, 4]), ALU.max, ALU.mult
+                )
+                if i < VECTOR_FIRST:
+                    nc.scalar.activation(soft[k][:, b, :, :], scores, ACT.Sigmoid, scale=-1.0)
         floor = sb("floor", [P, 8], F32)
-        nc.scalar.activation(floor[:, 0:1], soft[GROUPS - 1, 0][:, 0, 0:1], ACT.Identity, scale=0.0, bias=tiny[:, 0:1])
+        nc.scalar.activation(floor[:, 0:1], soft[-1][:, 0, 0, 0:1], ACT.Identity, scale=0.0, bias=tiny[:, 0:1])
 
-        wd_pairs = sb("wd_pairs", [P, T, 2], BF16)
+        wd_pairs = placed(cast, "wd_pairs", [P, T, 2], BF16, PAIRS_AT)
         for i, engines in enumerate(WD_CASTS):
             share = T // 4 // len(engines)
             for e, engine in enumerate(engines):
@@ -219,18 +215,11 @@ def tile_list_claim_intensity_sparse_kernel(tc, x, tab_words, tab_scales, offs, 
         for q in range(4):
             nc.sync.dma_start(wl_s[32 * q : 32 * q + 4, :, :], wl_scales[:, 4 * q : 4 * q + 4, :].bitcast(I32).rearrange("a r c -> r a c"))
 
-        h_b = [sb("h_b%d" % c, [P, 2, CHUNK, 4], BF16) for c in range(M // CHUNK)]
-        h_w = [sb("h_w%d" % c, [P, 2 * CHUNK], U32) for c in range(M // CHUNK)]
-        h_s = [sb("h_s%d" % c, [P, 2 * CHUNK], U8) for c in range(M // CHUNK)]
-
-        def h_part(k, b):
-            return h_b[k // 2][:, b, P * (k % 2) : P * (k % 2 + 1), :]
-
         window = wd_pairs[:].rearrange("p t h -> p (t h)").bitcast(U32)
         turned = [bank(b, "turned%d" % b) for b in range(2)]
 
         def turn_wd(b):
-            wd_g = sb("wd_g%d" % b, [P, PASS], U32, "soft%d" % b)
+            wd_g = sb("wd_g%d" % b, [P, PASS], U32, "soft%d" % TURN_AFTER[b] if TURN_AFTER[b] >= 0 else None)
             nc.vector.tensor_copy(wd_g[:].rearrange("p (t q r) -> p q t r", t=4, r=8), window.indirect(picks(b)))
             for t in range(4):
                 nc.tensor.transpose(turned[b][:, P * t : P * (t + 1)], wd_g[:, P * t : P * (t + 1)].bitcast(F32), ident[:])
@@ -238,40 +227,56 @@ def tile_list_claim_intensity_sparse_kernel(tc, x, tab_words, tab_scales, offs, 
         wd_b = sb("wd_b", [P, 2, 2, P, 4], BF16)
         wd_w = sb("wd_w", [P, 2 * N], U32)
         wd_s = sb("wd_s", [P, 2 * N], U8)
+        h_b = sb("h_b", [P, GROUPS, 2, PASS], BF16)
+        h_w = sb("h_w", [P, GROUPS, 2, P], U32)
+        h_s = sb("h_s", [P, GROUPS, 2, P], U8)
 
-        def finish(k, b):
-            nc.vector.scalar_tensor_tensor(h_part(k, b), soft[k, b], -KNEE, factor[k, b], ALU.max, ALU.mult)
-
-        def quantise_h(c, c0, w):
-            nc.vector.quantize_mx(
-                h_w[c][:, c0 : c0 + w].bitcast(FP8X4), h_s[c][:, c0 : c0 + w], h_b[c][:].rearrange("p b m t -> p (b m t)")[:, 4 * c0 : 4 * (c0 + w)]
-            )
+        def flat(tile):
+            return tile[:].rearrange("p k b c -> p (k b c)")
 
         def ln(k):
-            nc.scalar.activation(pair[k][:], pair[k][:], ACT.Ln, bias=floor[:, 0:1])
+            nc.scalar.activation(soft[k][:], soft[k][:], ACT.Ln, bias=floor[:, 0:1])
             if k in UNLOAD_AFTER:
                 b = UNLOAD_AFTER.index(k)
                 nc.scalar.copy(wd_b[:, b, :, :, :], turned[b][:].bitcast(BF16).rearrange("p (t n h) -> p h n t", t=4, h=2))
 
-        last = free - 1
+        def finish(k, b0, halves):
+            cols = slice(PASS * b0, PASS * (b0 + halves))
+            nc.vector.scalar_tensor_tensor(
+                flat(h_b)[:, PASS * (2 * k + b0) : PASS * (2 * k + b0 + halves)],
+                soft[k][:].rearrange("p b m t -> p (b m t)")[:, cols],
+                -KNEE,
+                factor[k][:].rearrange("p b m t -> p (b m t)")[:, cols],
+                ALU.max,
+                ALU.mult,
+            )
+
+        def quantise_h(u0, units):
+            nc.vector.quantize_mx(
+                flat(h_w)[:, P * u0 : P * (u0 + units)].bitcast(FP8X4), flat(h_s)[:, P * u0 : P * (u0 + units)], flat(h_b)[:, PASS * u0 : PASS * (u0 + units)]
+            )
+
+        for b in range(2):
+            if TURN_AFTER[b] < 0:
+                turn_wd(b)
         for k in range(LN_AHEAD):
             ln(k)
-        for k in range(free):
-            if k + LN_AHEAD < free:
+        for k in range(GROUPS - 1):
+            if k + LN_AHEAD < GROUPS:
                 ln(k + LN_AHEAD)
-            finish(k, 0)
-            if k == last:
-                for b in range(2):
-                    quantise_h(k // 2, CHUNK * b, P)
-            elif k % 2 == 0 and k > 0:
-                quantise_h(k // 2 - 1, 0, 2 * CHUNK)
-            finish(k, 1)
+            finish(k, 0, 2)
             if k in TURN_AFTER:
                 turn_wd(TURN_AFTER.index(k))
-            if k == 4:
+            if k % 2 == 0 and k > 0:
+                quantise_h(2 * k - 4, 4)
+            if k == WD_QUANTISE_AFTER:
                 nc.vector.quantize_mx(wd_w[:].bitcast(FP8X4), wd_s[:], wd_b[:].rearrange("p b h n t -> p (b h n t)"))
-        for b in range(2):
-            quantise_h(last // 2, CHUNK * b + P, P)
+        last = GROUPS - 1
+        finish(last, 0, 1)
+        quantise_h(2 * last - 2, 2)
+        finish(last, 1, 1)
+        quantise_h(2 * last, 1)
+        quantise_h(2 * last + 1, 1)
 
         def intensities(name, k0, groups, banks):
             w = P * groups
@@ -289,21 +294,18 @@ def tile_list_claim_intensity_sparse_kernel(tc, x, tab_words, tab_scales, offs, 
                             start=(k == 0 and a == 0),
                             stop=False,
                         )
-            step = min(w, CHUNK)
-            for m0 in range(0, w, step):
-                m = P * k0 + m0
+            for k in range(groups):
                 for b in range(2):
-                    c0 = CHUNK * b + m % CHUNK
                     for h in range(2):
                         ns = slice(N * b + P * h, N * b + P * (h + 1))
                         nc.tensor.matmul_mx(
-                            out=accs[h][:, m0 : m0 + step],
+                            out=accs[h][:, P * k : P * (k + 1)],
                             lhsT=wd_w[:, ns].bitcast(FP8X4),
                             lhsT_scale=wd_s[:, ns],
-                            rhs=h_w[m // CHUNK][:, c0 : c0 + step].bitcast(FP8X4),
-                            rhs_scale=h_s[m // CHUNK][:, c0 : c0 + step],
+                            rhs=h_w[:, k0 + k, b, :].bitcast(FP8X4),
+                            rhs_scale=h_s[:, k0 + k, b, :],
                             start=False,
-                            stop=(b == 1 and m0 + step == w),
+                            stop=(b == 1 and k == groups - 1),
                         )
             res = sb("res" + name, [P, 2, w], F32)
             for h in range(2):

@@ -30,9 +30,9 @@ LISTED_AT = 8
 WD_AT = (8, 12, 16, 22)
 WL_AT = (26, 30)
 CHUNKS = ((0, 1, "S", "SG"), (1, 1, "S", "SG"), (2, 2, "SG", "G"), (4, 2, "SG", "G"), (6, 1, "S", "G"), (7, 1, "G", "G"))
-CAST_AT = {1: 2048, 2: 8192, 3: 16384, 4: 24576, 5: 32768}
-FACTOR_AT = {0: 0, 1: 8192, 3: 16384, 5: 22528, 6: 30720}
-PAIRS_AT = 36864
+CAST_AT = {1: 2048, 2: 8192, 3: 12224, 4: 24576, 5: 32832}
+FACTOR_AT = {0: 0, 1: 8128, 3: 12224, 5: 22528, 6: 30720}
+PAIRS_AT = 34816
 WD_CASTS = ("G", "G", "G", "V")
 VECTOR_FIRST = 2
 UNLOAD_AFTER = (3, 4)
@@ -61,7 +61,7 @@ def tile_list_claim_intensity_sparse_kernel(tc, x, tab_words, tab_scales, offs, 
         offsets = keep.tile([P, S // 16], U16, name="offsets")
         nc.sync.dma_start(offsets[:], offs)
 
-        tab_s = sb("tab_s", [P, T // 4], I32)
+        tab_s = placed(stage, "tab_s", [P, T // 4], I32, KB * LISTED_AT - KB)
         nc.gpsimd.memset(tab_s[32:64, :], 0)
         nc.gpsimd.memset(tab_s[64:128, :], 0)
         for u in range(2):
@@ -94,15 +94,12 @@ def tile_list_claim_intensity_sparse_kernel(tc, x, tab_words, tab_scales, offs, 
         ident = sb("ident", [P, P], F32)
         make_identity(nc, ident[:])
 
-        listed = placed(stage, "listed", [P, S], U8, KB * LISTED_AT - S // 2)
+        listed = sb("listed", [P, S], U8)
         v_s = sb("v_s", [P, S], U8)
-        nc.vector.tensor_copy(listed[:], tab_s[:].bitcast(U8).indirect(offsets[:]))
-        nc.vector.tensor_copy(
-            v_s[:].bitcast(I32).rearrange("p (b t q w) -> p b t q w", b=2, t=4, w=2),
-            listed[:].bitcast(I32).rearrange("p (b q t w) -> p b t q w", b=2, t=4, w=2),
-        )
-        for src, dst in ((4, 32), (16, 64), (16, 92)):
-            nc.sync.dma_start(v_s[dst : dst + 16, :].bitcast(I32), v_s[src : src + 16, :].bitcast(I32))
+        nc.vector.memset(v_s[:].bitcast(I32), 0)
+        nc.vector.tensor_copy(listed[:].rearrange("p (b t q r) -> p b q t r", b=2, t=4, r=8), tab_s[:].bitcast(U8).indirect(offsets[:]))
+        for src, dst in ((0, 0), (4, 32), (16, 64), (16, 92)):
+            nc.sync.dma_start(v_s[dst : dst + 16, :].bitcast(I32), listed[src : src + 16, :].bitcast(I32))
 
         g_bank = bank(0, "g_bank")
         nc.gpsimd.tensor_copy(g_rows[0:2, :].rearrange("b (t q r) -> b t q r", t=4, r=8), g_raw[:].rearrange("b (q t r) -> b t q r", t=4, r=8))

@@ -24,21 +24,22 @@ FLOOR_SCORE = -42.0
 KNEE = 32.0
 KB = 1024
 X_LOADS = ((0, 1), (1, 1), (2, 2), (4, 2), (6, 2))
-X_AT = ((0, 2), (4, 6), (8, 12), (16, 22), (26, 30))
-TAB_AT = (14, 24)
+X_AT = ((0, 2), (4, 6), (8, 12), (19, 24), (33, 8))
+TAB_AT = (15, 26)
 LISTED_AT = 8
-WD_AT = (8, 12, 16, 22)
-WL_AT = (26, 30)
-CHUNKS = ((0, 1, "S", "SG"), (1, 1, "S", "SG"), (2, 2, "SG", "G"), (4, 2, "SG", "G"), (6, 1, "S", "G"), (7, 1, "G", "G"))
+WD_AT = (16, 20, 30, 36)
+WL_AT = (34, 35)
+CHUNKS = ((0, 1, "S", "SG"), (1, 1, "S", "SG"), (2, 2, "G", "SG"), (4, 2, "G", "SG"), (6, 1, "G", "SG"), (7, 1, "G", "SG"))
 CAST_AT = {1: 2048, 2: 8192, 3: 12224, 4: 24576, 5: 32832}
 FACTOR_AT = {0: 0, 1: 8128, 3: 12224, 5: 22528, 6: 30720}
 PAIRS_AT = 34816
 WD_CASTS = ("G", "G", "G", "V")
-VECTOR_FIRST = 2
+VECTOR_FIRST = 0
 UNLOAD_AFTER = (3, 4)
 TURN_AFTER = (-1, -1)
 WD_QUANTISE_AFTER = 5
 LN_AHEAD = 2
+SOFT_AT = {1: 12, 3: 24, 5: 8}
 
 
 def tile_list_claim_intensity_sparse_kernel(tc, x, tab_words, tab_scales, offs, g, wdT, wl_words, wl_scales, out):
@@ -74,6 +75,12 @@ def tile_list_claim_intensity_sparse_kernel(tc, x, tab_words, tab_scales, offs, 
 
         def load_x(i, a):
             k0, groups = X_LOADS[i]
+            if (i, a) == (len(X_LOADS) - 1, 1):
+                for k in range(k0, k0 + groups):
+                    raw = placed(stage, "x_last%d" % k, [P, 4, P], F32, KB * (X_AT[i][a] + 2 * (k - k0)))
+                    nc.sync.dma_start(raw[:], x[PASS:, P * k : P * (k + 1)].rearrange("(p j) m -> p j m", j=4))
+                    x_raw[k, a] = (raw, 0)
+                return
             raw = placed(stage, "x_raw%d_%d" % (i, a), [P, 4, P * groups], F32, KB * X_AT[i][a])
             nc.sync.dma_start(raw[:], x[PASS * a : PASS * (a + 1), P * k0 : P * (k0 + groups)].rearrange("(p j) m -> p j m", j=4))
             for k in range(groups):
@@ -168,7 +175,10 @@ def tile_list_claim_intensity_sparse_kernel(tc, x, tab_words, tab_scales, offs, 
         nc.sync.dma_start(wl_w[:], wl_words.bitcast(I32).rearrange("a p c -> p a c"))
         wl_s = placed(stage, "wl_s", [P, 2, N // 4], I32, KB * WL_AT[1])
 
-        soft = [sb("soft%d" % k, [P, 2, P, 4], F32) for k in range(GROUPS)]
+        soft = [
+            placed(stage, "soft%d" % k, [P, 2, P, 4], F32, KB * SOFT_AT[k]) if k in SOFT_AT else sb("soft%d" % k, [P, 2, P, 4], F32)
+            for k in range(GROUPS)
+        ]
         factor = [
             placed(cast, "factor%d" % k, [P, 2, P, 4], F32, FACTOR_AT[k]) if k in FACTOR_AT else sb("factor%d" % k, [P, 2, P, 4], F32)
             for k in range(GROUPS)

@@ -23,23 +23,29 @@ GROUPS = M // P
 FLOOR_SCORE = -42.0
 KNEE = 32.0
 KB = 1024
-X_LOADS = ((0, 1), (1, 1), (2, 2), (4, 2), (6, 2))
-X_AT = ((0, 2), (4, 6), (8, 12), (19, 24), (33, 8))
-TAB_AT = (15, 26)
-LISTED_AT = 8
-WD_AT = (16, 20, 30, 36)
-WL_AT = (34, 35)
-CHUNKS = ((0, 1, "S", "SG"), (1, 1, "S", "SG"), (2, 2, "G", "SG"), (4, 2, "G", "SG"), (6, 1, "G", "SG"), (7, 1, "G", "SG"))
-CAST_AT = {1: 2048, 2: 8192, 3: 12224, 4: 24576, 5: 32832}
-FACTOR_AT = {0: 0, 1: 8128, 3: 12224, 5: 22528, 6: 30720}
-PAIRS_AT = 34816
+X_LOADS = (
+    (0, 1, 0, 0), (0, 1, 1, 2 * KB), (1, 1, 0, 6 * KB + 64), (1, 1, 1, 10 * KB - 64),
+    (2, 2, 0, 12 * KB + 64), (2, 2, 1, 16 * KB + 64), (4, 2, 0, 20 * KB + 64), (4, 2, 1, 24 * KB + 128),
+    (6, 2, 0, 28 * KB + 128), (6, 1, 1, 32 * KB + 128), (7, 1, 1, 34 * KB + 128),
+)
+FREE_LOADS = 2
+SCALES_AT = 8 * KB
+TAB_AT = (16 * KB, 28 * KB)
+WD_AT = (12 * KB + 64, 20 * KB + 64, 78 * KB - 64, 28 * KB + 128)
+SOFT_AT = {1: 16 * KB + 64, 3: 24 * KB + 128, 5: 32 * KB + 128}
 WD_CASTS = ("G", "G", "G", "V")
+WL_AT = 8 * KB
+HELD_AT = 40 * KB
+FACTOR_AFTER = {0: 1, 3: 3, 5: 5}
+
+
+def rounded_at(c):
+    return HELD_AT + 10 * KB * c + 4 * KB
+CHUNKS = ((0, 1, "S", "SG", 0), (1, 1, "S", "SG", 0), (2, 2, "G", "SG", 1), (4, 2, "G", "SG", 3), (6, 1, "G", "SG", 7), (7, 1, "G", "SG", 8))
+UNLOAD_AFTER = (2, 3)
+WD_QUANTISE_AFTER = 4
 VECTOR_FIRST = 0
-UNLOAD_AFTER = (3, 4)
-TURN_AFTER = (-1, -1)
-WD_QUANTISE_AFTER = 5
 LN_AHEAD = 2
-SOFT_AT = {1: 12, 3: 24, 5: 8}
 
 
 def tile_list_claim_intensity_sparse_kernel(tc, x, tab_words, tab_scales, offs, g, wdT, wl_words, wl_scales, out):
@@ -47,22 +53,23 @@ def tile_list_claim_intensity_sparse_kernel(tc, x, tab_words, tab_scales, offs, 
     with ExitStack() as ctx:
         keep = ctx.enter_context(tc.tile_pool(name="keep", bufs=1))
         stage = ctx.enter_context(tc.tile_pool(name="stage", bufs=1))
-        cast = ctx.enter_context(tc.tile_pool(name="cast", bufs=1))
         psum = ctx.enter_context(tc.psum_pool(name="psum", bufs=1))
 
         def sb(name, shape, dtype, tag=None):
             return keep.tile(shape, dtype, name=name, tag=tag or name, align_bytes=64)
 
-        def placed(pool, name, shape, dtype, at):
-            return pool.tile(shape, dtype, name=name, offset=at, align_bytes=64)
+        def staged(name, shape, dtype, at):
+            return stage.tile(shape, dtype, name=name, offset=at, align_bytes=64)
 
         def bank(i, name):
             return psum.tile([P, 512], F32, name=name, tag="bank%d" % i)
 
+        copy_on = {"G": nc.gpsimd.tensor_copy, "V": nc.vector.tensor_copy, "S": nc.scalar.copy}
+
         offsets = keep.tile([P, S // 16], U16, name="offsets")
         nc.sync.dma_start(offsets[:], offs)
 
-        tab_s = placed(stage, "tab_s", [P, T // 4], I32, KB * LISTED_AT - KB)
+        tab_s = staged("tab_s", [P, T // 4], I32, SCALES_AT)
         nc.gpsimd.memset(tab_s[32:64, :], 0)
         nc.gpsimd.memset(tab_s[64:128, :], 0)
         for u in range(2):
@@ -71,26 +78,23 @@ def tile_list_claim_intensity_sparse_kernel(tc, x, tab_words, tab_scales, offs, 
         g_raw = sb("g_raw", [2, PASS], F32)
         nc.sync.dma_start(g_raw[:], g.rearrange("(b j) -> b j", b=2))
 
+        tab_w = [staged("tab_w%d" % a, [P, T], I32, TAB_AT[a]) for a in range(2)]
         x_raw = {}
 
-        def load_x(i, a):
-            k0, groups = X_LOADS[i]
-            if (i, a) == (len(X_LOADS) - 1, 1):
-                for k in range(k0, k0 + groups):
-                    raw = placed(stage, "x_last%d" % k, [P, 4, P], F32, KB * (X_AT[i][a] + 2 * (k - k0)))
-                    nc.sync.dma_start(raw[:], x[PASS:, P * k : P * (k + 1)].rearrange("(p j) m -> p j m", j=4))
-                    x_raw[k, a] = (raw, 0)
-                return
-            raw = placed(stage, "x_raw%d_%d" % (i, a), [P, 4, P * groups], F32, KB * X_AT[i][a])
+        def load_table(a):
+            nc.sync.dma_start(tab_w[a][:], tab_words[a].rearrange("p t i -> p (t i)").bitcast(I32))
+
+        def load_x(i):
+            k0, groups, a, at = X_LOADS[i]
+            raw = staged("x_raw%d" % i, [P, 4, P * groups], F32, at)
             nc.sync.dma_start(raw[:], x[PASS * a : PASS * (a + 1), P * k0 : P * (k0 + groups)].rearrange("(p j) m -> p j m", j=4))
             for k in range(groups):
                 x_raw[k0 + k, a] = (raw, P * k)
 
-        tab_w = [placed(stage, "tab_w%d" % a, [P, T], I32, KB * TAB_AT[a]) for a in range(2)]
-        for a in range(2):
-            nc.sync.dma_start(tab_w[a][:], tab_words[a].rearrange("p t i -> p (t i)").bitcast(I32))
-        for i, a in ((0, 0), (0, 1), (1, 0)):
-            load_x(i, a)
+        load_table(0)
+        for i in range(FREE_LOADS):
+            load_x(i)
+        load_table(1)
 
         low = sb("low", [P, 8], F32)
         nc.gpsimd.memset(low[:], FLOOR_SCORE)
@@ -104,51 +108,55 @@ def tile_list_claim_intensity_sparse_kernel(tc, x, tab_words, tab_scales, offs, 
         listed = sb("listed", [P, S], U8)
         v_s = sb("v_s", [P, S], U8)
         nc.vector.memset(v_s[:].bitcast(I32), 0)
-        nc.vector.tensor_copy(listed[:].rearrange("p (b t q r) -> p b q t r", b=2, t=4, r=8), tab_s[:].bitcast(U8).indirect(offsets[:]))
+
+        def picks(b):
+            return offsets[:, 32 * b : 32 * (b + 1)]
+
+        def in_slots(ap):
+            return ap.rearrange("p (u e q r) -> p q u r e", u=2, e=2, r=8)
+
+        for b in range(2):
+            nc.vector.tensor_copy(in_slots(listed[:, PASS * b : PASS * (b + 1)]), tab_s[:].bitcast(U8).indirect(picks(b)))
         for src, dst in ((0, 0), (4, 32), (16, 64), (16, 92)):
             nc.sync.dma_start(v_s[dst : dst + 16, :].bitcast(I32), listed[src : src + 16, :].bitcast(I32))
 
         g_bank = bank(0, "g_bank")
-        nc.gpsimd.tensor_copy(g_rows[0:2, :].rearrange("b (t q r) -> b t q r", t=4, r=8), g_raw[:].rearrange("b (q t r) -> b t q r", t=4, r=8))
+        nc.gpsimd.tensor_copy(g_rows[0:2, :].rearrange("b (u e q r) -> b u e q r", u=2, e=2, r=8), g_raw[:].rearrange("b (q u r e) -> b u e q r", u=2, e=2, r=8))
         for t in range(4):
             nc.tensor.transpose(g_bank[:, P * t : P * (t + 1)], g_rows[:, P * t : P * (t + 1)], ident[:])
         slopes = sb("slopes", [P, 2, 4], F32)
         nc.scalar.activation(slopes[:], g_bank[:].rearrange("p (t k) -> p k t", t=4)[:, 0:2, :], ACT.Copy, scale=-1.0 / KNEE)
 
-        def picks(b):
-            return offsets[:, 32 * b : 32 * (b + 1)]
-
         v_w = {}
 
-        def gather_words(a, b, tag):
-            v_w[a, b] = sb("v_w%d_%d" % (a, b), [P, PASS], U32, tag)
-            nc.vector.tensor_copy(v_w[a, b][:].rearrange("p (t q r) -> p q t r", t=4, r=8), tab_w[a][:].bitcast(U32).indirect(picks(b)))
+        def gather_words(a, b):
+            if a == 0:
+                v_w[a, b] = sb("v_w%d_%d" % (a, b), [P, PASS], U32)
+            else:
+                v_w[a, b] = staged("v_w%d_%d" % (a, b), [P, PASS], U32, rounded_at(0) + (2 * KB - 64) * (2 * b - 1))
+            nc.vector.tensor_copy(in_slots(v_w[a, b][:]), tab_w[a][:].bitcast(U32).indirect(picks(b)))
 
         x_w = [sb("x_w%d" % c, [P, 2 * P * chunk[1]], U32) for c, chunk in enumerate(CHUNKS)]
         x_s = [sb("x_s%d" % c, [P, 2 * P * chunk[1]], U8) for c, chunk in enumerate(CHUNKS)]
         chunk_of = {chunk[0] + k: (c, k) for c, chunk in enumerate(CHUNKS) for k in range(chunk[1])}
 
-        def cast_piece(engine, dst, src):
+        def round_piece(engine, dst, src):
             if engine == "G":
                 nc.gpsimd.tensor_copy(dst, src.rearrange("p j m -> p m j"))
             else:
-                eng_copy = nc.scalar.copy if engine == "S" else nc.vector.tensor_copy
-                eng_copy(dst.rearrange("p (c i) j -> p c j i", i=4), src.rearrange("p j (c i) -> p c j i", i=4))
+                copy_on[engine](dst.rearrange("p (c i) j -> p c j i", i=4), src.rearrange("p j (c i) -> p c j i", i=4))
 
         def quantise_x(c):
             k0, groups = CHUNKS[c][:2]
             width = P * groups
-            if c == 0:
-                flat = sb("x_b0", [P, 8 * width], BF16)
-            else:
-                flat = placed(cast, "x_b%d" % c, [P, 8 * width], BF16, CAST_AT[c])
+            flat = staged("x_b%d" % c, [P, 8 * width], BF16, rounded_at(c))
             xb = flat[:].rearrange("p (a m j) -> p a m j", a=2, j=4)
             for a in range(2):
                 engines = CHUNKS[c][2 + a]
                 share = width // len(engines)
                 raw, m0 = x_raw[k0, a]
                 for i, engine in enumerate(engines):
-                    cast_piece(engine, xb[:, a, share * i : share * (i + 1), :], raw[:, :, m0 + share * i : m0 + share * (i + 1)])
+                    round_piece(engine, xb[:, a, share * i : share * (i + 1), :], raw[:, :, m0 + share * i : m0 + share * (i + 1)])
             nc.vector.quantize_mx(x_w[c][:].bitcast(FP8X4), x_s[c][:], flat[:])
 
         def x_cols(a, k):
@@ -156,40 +164,32 @@ def tile_list_claim_intensity_sparse_kernel(tc, x, tab_words, tab_scales, offs, 
             c0 = P * (CHUNKS[c][1] * a + i)
             return x_w[c][:, c0 : c0 + P].bitcast(FP8X4), x_s[c][:, c0 : c0 + P]
 
-        gather_words(0, 0, None)
-        gather_words(0, 1, None)
-        gather_words(1, 0, None)
+        gather_words(0, 0)
+        gather_words(0, 1)
         quantise_x(0)
-        gather_words(1, 1, "x_b0")
-        load_x(1, 1)
-        for i in range(2, len(X_LOADS)):
-            for a in range(2):
-                load_x(i, a)
-        for c in range(1, len(CHUNKS)):
-            quantise_x(c)
-        wd_raw = []
-        for i in range(4):
-            wd_raw.append(placed(stage, "wd_raw%d" % i, [P, 2, T // 4], F32, KB * WD_AT[i]))
-            nc.sync.dma_start(wd_raw[i][:], wdT[:, T // 4 * i : T // 4 * (i + 1)].rearrange("(h p) t -> p h t", h=2))
-        wl_w = placed(stage, "wl_w", [P, 2, N // 2], I32, KB * WL_AT[0])
-        nc.sync.dma_start(wl_w[:], wl_words.bitcast(I32).rearrange("a p c -> p a c"))
-        wl_s = placed(stage, "wl_s", [P, 2, N // 4], I32, KB * WL_AT[1])
-
+        gather_words(1, 0)
+        gather_words(1, 1)
+        for i in range(FREE_LOADS, len(X_LOADS)):
+            load_x(i)
         soft = [
-            placed(stage, "soft%d" % k, [P, 2, P, 4], F32, KB * SOFT_AT[k]) if k in SOFT_AT else sb("soft%d" % k, [P, 2, P, 4], F32)
+            staged("soft%d" % k, [P, 2, P, 4], F32, SOFT_AT[k]) if k in SOFT_AT else sb("soft%d" % k, [P, 2, P, 4], F32)
             for k in range(GROUPS)
         ]
         factor = [
-            placed(cast, "factor%d" % k, [P, 2, P, 4], F32, FACTOR_AT[k]) if k in FACTOR_AT else sb("factor%d" % k, [P, 2, P, 4], F32)
+            staged("factor%d" % k, [P, 2, P, 4], F32, rounded_at(FACTOR_AFTER[k]) - 4 * KB + 64) if k in FACTOR_AFTER else sb("factor%d" % k, [P, 2, P, 4], F32)
             for k in range(GROUPS)
         ]
         for k in range(GROUPS):
             for b in range(2):
                 i = 2 * k + b
+                for c in range(1, len(CHUNKS)):
+                    if CHUNKS[c][4] == i:
+                        quantise_x(c)
                 acc = bank(i % 8, "acc%d" % i)
-                for t in range(4):
-                    js = slice(PASS * b + P * t, PASS * b + P * (t + 1))
-                    for a in range(2):
+                passes = [(a, t) for a in range(2) for t in range(4)] if k == 0 else [(a, t) for t in range(4) for a in range(2)]
+                for a, t in passes:
+                    if True:
+                        js = slice(PASS * b + P * t, PASS * b + P * (t + 1))
                         codes, scales = x_cols(a, k)
                         nc.tensor.matmul_mx(
                             out=acc[:, P * t : P * (t + 1)],
@@ -197,8 +197,8 @@ def tile_list_claim_intensity_sparse_kernel(tc, x, tab_words, tab_scales, offs, 
                             lhsT_scale=v_s[8 * a : P, js],
                             rhs=codes,
                             rhs_scale=scales,
-                            start=(a == 0),
-                            stop=(a == 1),
+                            start=(a == 0 and t == 0),
+                            stop=(a == 1 and t == 3),
                         )
                 scores = acc[:].rearrange("p (t m) -> p m t", t=4)
                 if i >= VECTOR_FIRST:
@@ -208,26 +208,29 @@ def tile_list_claim_intensity_sparse_kernel(tc, x, tab_words, tab_scales, offs, 
                 )
                 if i < VECTOR_FIRST:
                     nc.scalar.activation(soft[k][:, b, :, :], scores, ACT.Sigmoid, scale=-1.0)
+        wd_raw = []
+        for i in range(4):
+            wd_raw.append(staged("wd_raw%d" % i, [P, 2, T // 4], F32, WD_AT[i]))
+            nc.sync.dma_start(wd_raw[i][:], wdT[:, T // 4 * i : T // 4 * (i + 1)].rearrange("(h p) t -> p h t", h=2))
+        wl_w = staged("wl_w", [P, 2, N // 2], I32, WL_AT)
+        nc.sync.dma_start(wl_w[:], wl_words.bitcast(I32).rearrange("a p c -> p a c"))
+        wl_s = sb("wl_s", [P, 2, N // 4], I32)
+
         floor = sb("floor", [P, 8], F32)
         nc.scalar.activation(floor[:, 0:1], soft[-1][:, 0, 0, 0:1], ACT.Identity, scale=0.0, bias=tiny[:, 0:1])
 
-        wd_pairs = placed(cast, "wd_pairs", [P, T, 2], BF16, PAIRS_AT)
-        for i, engines in enumerate(WD_CASTS):
-            share = T // 4 // len(engines)
-            for e, engine in enumerate(engines):
-                dst = wd_pairs[:, T // 4 * i + share * e : T // 4 * i + share * (e + 1), :]
-                src = wd_raw[i][:, :, share * e : share * (e + 1)].rearrange("p h t -> p t h")
-                {"G": nc.gpsimd.tensor_copy, "V": nc.vector.tensor_copy, "S": nc.scalar.copy}[engine](dst, src)
+        wd_pairs = staged("wd_pairs", [P, T, 2], BF16, rounded_at(len(CHUNKS) - 1) + 2 * KB - 64)
+        for i, engine in enumerate(WD_CASTS):
+            copy_on[engine](wd_pairs[:, T // 4 * i : T // 4 * (i + 1), :], wd_raw[i][:].rearrange("p h t -> p t h"))
         nc.gpsimd.memset(wl_s[:], 0)
         for q in range(4):
             nc.sync.dma_start(wl_s[32 * q : 32 * q + 4, :, :], wl_scales[:, 4 * q : 4 * q + 4, :].bitcast(I32).rearrange("a r c -> r a c"))
 
         window = wd_pairs[:].rearrange("p t h -> p (t h)").bitcast(U32)
         turned = [bank(b, "turned%d" % b) for b in range(2)]
-
-        def turn_wd(b):
-            wd_g = sb("wd_g%d" % b, [P, PASS], U32, "soft%d" % TURN_AFTER[b] if TURN_AFTER[b] >= 0 else None)
-            nc.vector.tensor_copy(wd_g[:].rearrange("p (t q r) -> p q t r", t=4, r=8), window.indirect(picks(b)))
+        for b in range(2):
+            wd_g = sb("wd_g%d" % b, [P, PASS], U32)
+            nc.vector.tensor_copy(in_slots(wd_g[:]), window.indirect(picks(b)))
             for t in range(4):
                 nc.tensor.transpose(turned[b][:, P * t : P * (t + 1)], wd_g[:, P * t : P * (t + 1)].bitcast(F32), ident[:])
 
@@ -263,17 +266,12 @@ def tile_list_claim_intensity_sparse_kernel(tc, x, tab_words, tab_scales, offs, 
                 flat(h_w)[:, P * u0 : P * (u0 + units)].bitcast(FP8X4), flat(h_s)[:, P * u0 : P * (u0 + units)], flat(h_b)[:, PASS * u0 : PASS * (u0 + units)]
             )
 
-        for b in range(2):
-            if TURN_AFTER[b] < 0:
-                turn_wd(b)
         for k in range(LN_AHEAD):
             ln(k)
         for k in range(GROUPS - 1):
             if k + LN_AHEAD < GROUPS:
                 ln(k + LN_AHEAD)
             finish(k, 0, 2)
-            if k in TURN_AFTER:
-                turn_wd(TURN_AFTER.index(k))
             if k % 2 == 0 and k > 0:
                 quantise_h(2 * k - 4, 4)
             if k == WD_QUANTISE_AFTER:

@@ -26,7 +26,7 @@ KB = 1024
 X_LOADS = (
     (0, 1, 0, 0), (0, 1, 1, 2 * KB), (1, 1, 0, 6 * KB + 64), (1, 1, 1, 10 * KB - 64),
     (2, 2, 0, 12 * KB + 64), (2, 2, 1, 16 * KB + 64), (4, 2, 0, 20 * KB + 64), (4, 2, 1, 24 * KB + 128),
-    (6, 2, 0, 28 * KB + 128), (6, 1, 1, 32 * KB + 128), (7, 1, 1, 34 * KB + 128),
+    (6, 2, 0, 28 * KB + 128), (6, 2, 1, 32 * KB + 128),
 )
 FREE_LOADS = 2
 SCALES_AT = 8 * KB
@@ -34,7 +34,7 @@ TAB_AT = (16 * KB, 28 * KB)
 WD_AT = (12 * KB + 64, 20 * KB + 64, 78 * KB - 64, 28 * KB + 128)
 SOFT_AT = {1: 16 * KB + 64, 3: 24 * KB + 128, 5: 32 * KB + 128}
 WD_CASTS = ("G", "G", "G", "V")
-WL_AT = 8 * KB
+WL_AT = 12 * KB + 64
 HELD_AT = 40 * KB
 FACTOR_AFTER = {0: 1, 3: 3, 5: 5}
 
@@ -75,8 +75,6 @@ def tile_list_claim_intensity_sparse_kernel(tc, x, tab_words, tab_scales, offs, 
         for u in range(2):
             for a in range(2):
                 nc.sync.dma_start(tab_s[16 * u + 8 * a : 16 * u + 8 * a + 8, :], tab_scales[a, 8 * u : 8 * u + 8, :].bitcast(I32))
-        g_raw = sb("g_raw", [2, PASS], F32)
-        nc.sync.dma_start(g_raw[:], g.rearrange("(b j) -> b j", b=2))
 
         tab_w = [staged("tab_w%d" % a, [P, T], I32, TAB_AT[a]) for a in range(2)]
         x_raw = {}
@@ -92,6 +90,8 @@ def tile_list_claim_intensity_sparse_kernel(tc, x, tab_words, tab_scales, offs, 
                 x_raw[k0 + k, a] = (raw, P * k)
 
         load_table(0)
+        g_raw = sb("g_raw", [2, PASS], F32)
+        nc.sync.dma_start(g_raw[:], g.rearrange("(b j) -> b j", b=2))
         for i in range(FREE_LOADS):
             load_x(i)
         load_table(1)
@@ -100,7 +100,7 @@ def tile_list_claim_intensity_sparse_kernel(tc, x, tab_words, tab_scales, offs, 
         nc.gpsimd.memset(low[:], FLOOR_SCORE)
         tiny = sb("tiny", [P, 8], F32)
         nc.scalar.activation(tiny[:, 0:1], low[:, 0:1], ACT.Sigmoid)
-        g_rows = sb("g_rows", [P, PASS], F32, "v_w0_1")
+        g_rows = sb("g_rows", [P, PASS], F32)
         nc.gpsimd.memset(g_rows[:], 0.0)
         ident = sb("ident", [P, P], F32)
         make_identity(nc, ident[:])
@@ -214,7 +214,7 @@ def tile_list_claim_intensity_sparse_kernel(tc, x, tab_words, tab_scales, offs, 
             nc.sync.dma_start(wd_raw[i][:], wdT[:, T // 4 * i : T // 4 * (i + 1)].rearrange("(h p) t -> p h t", h=2))
         wl_w = staged("wl_w", [P, 2, N // 2], I32, WL_AT)
         nc.sync.dma_start(wl_w[:], wl_words.bitcast(I32).rearrange("a p c -> p a c"))
-        wl_s = sb("wl_s", [P, 2, N // 4], I32)
+        wl_s = staged("wl_s", [P, 2, N // 4], I32, WL_AT + KB)
 
         floor = sb("floor", [P, 8], F32)
         nc.scalar.activation(floor[:, 0:1], soft[-1][:, 0, 0, 0:1], ACT.Identity, scale=0.0, bias=tiny[:, 0:1])

@@ -33,7 +33,7 @@ SCALES_AT = 8 * KB
 TAB_AT = (16 * KB, 28 * KB)
 WD_AT = (12 * KB + 64, 20 * KB + 64, 78 * KB - 64, 28 * KB + 128)
 SOFT_AT = {1: 16 * KB + 64, 3: 24 * KB + 128, 5: 32 * KB + 128}
-WD_CASTS = ("G", "G", "G", "V")
+WD_CASTS = ("V", "G", "G", "G")
 WL_AT = 12 * KB + 64
 HELD_AT = 40 * KB
 FACTOR_AFTER = {0: 1, 3: 3, 5: 5}
@@ -229,7 +229,7 @@ def tile_list_claim_intensity_sparse_kernel(tc, x, tab_words, tab_scales, offs, 
         window = wd_pairs[:].rearrange("p t h -> p (t h)").bitcast(U32)
         turned = [bank(b, "turned%d" % b) for b in range(2)]
         for b in range(2):
-            wd_g = sb("wd_g%d" % b, [P, PASS], U32)
+            wd_g = sb("wd_g%d" % b, [P, PASS], U32, None if b else "slopes")
             nc.vector.tensor_copy(in_slots(wd_g[:]), window.indirect(picks(b)))
             for t in range(4):
                 nc.tensor.transpose(turned[b][:, P * t : P * (t + 1)], wd_g[:, P * t : P * (t + 1)].bitcast(F32), ident[:])

@@ -141,10 +141,7 @@ def tile_list_claim_intensity_sparse_kernel(tc, x, tab_words, tab_scales, offs, 
         chunk_of = {chunk[0] + k: (c, k) for c, chunk in enumerate(CHUNKS) for k in range(chunk[1])}
 
         def round_piece(engine, dst, src):
-            if engine == "G":
-                nc.gpsimd.tensor_copy(dst, src.rearrange("p j m -> p m j"))
-            else:
-                copy_on[engine](dst.rearrange("p (c i) j -> p c j i", i=4), src.rearrange("p j (c i) -> p c j i", i=4))
+            copy_on[engine](dst.rearrange("p (c i) j -> p c j i", i=4), src.rearrange("p j (c i) -> p c j i", i=4))
 
         def quantise_x(c):
             k0, groups = CHUNKS[c][:2]

from contextlib import ExitStack

import concourse.mybir as mybir
from concourse.masks import make_identity

K, T, S, M, N = 1024, 2048, 1024, 1024, 256
FLOPS = 2 * S * K * M + 2 * N * S * M + 2 * N * K * M

F32 = mybir.dt.float32
BF16 = mybir.dt.bfloat16
I32 = mybir.dt.int32
U32 = mybir.dt.uint32
U16 = mybir.dt.uint16
U8 = mybir.dt.uint8
FP8X4 = mybir.dt.float8_e4m3fn_x4
FP4X4 = mybir.dt.float4_e2m1fn_x4
ACT = mybir.ActivationFunctionType
ALU = mybir.AluOpType

P = 128
PASS = 512
GROUPS = M // P
FLOOR_SCORE = -42.0
KNEE = 32.0
KB = 1024
X_LOADS = (
    (0, 1, 0, 0), (0, 1, 1, 2 * KB), (1, 1, 0, 6 * KB + 64), (1, 1, 1, 10 * KB - 64),
    (2, 2, 0, 12 * KB + 64), (2, 2, 1, 16 * KB + 64), (4, 2, 0, 20 * KB + 64), (4, 2, 1, 24 * KB + 128),
    (6, 2, 0, 28 * KB + 128), (6, 2, 1, 32 * KB + 128),
)
FREE_LOADS = 2
SCALES_AT = 8 * KB
TAB_AT = (16 * KB, 28 * KB)
WD_AT = (12 * KB + 64, 20 * KB + 64, 78 * KB - 64, 28 * KB + 128)
SOFT_AT = {1: 16 * KB + 64, 3: 24 * KB + 128, 5: 32 * KB + 128}
WD_CASTS = ("V", "G", "G", "G")
WL_AT = 12 * KB + 64
HELD_AT = 40 * KB
FACTOR_AFTER = {0: 1, 3: 3, 5: 5}


def rounded_at(c):
    return HELD_AT + 10 * KB * c + 4 * KB
CHUNKS = ((0, 1, "S", "SG", 0), (1, 1, "S", "SG", 0), (2, 2, "G", "SG", 1), (4, 2, "G", "SG", 3), (6, 1, "G", "SG", 7), (7, 1, "G", "SG", 8))
UNLOAD_AFTER = (2, 3)
WD_QUANTISE_AFTER = 4
VECTOR_FIRST = 0
LN_AHEAD = 2


def tile_list_claim_intensity_sparse_kernel(tc, x, tab_words, tab_scales, offs, g, wdT, wl_words, wl_scales, out):
    nc = tc.nc
    with ExitStack() as ctx:
        keep = ctx.enter_context(tc.tile_pool(name="keep", bufs=1))
        stage = ctx.enter_context(tc.tile_pool(name="stage", bufs=1))
        psum = ctx.enter_context(tc.psum_pool(name="psum", bufs=1))

        def sb(name, shape, dtype, tag=None):
            return keep.tile(shape, dtype, name=name, tag=tag or name, align_bytes=64)

        def staged(name, shape, dtype, at):
            return stage.tile(shape, dtype, name=name, offset=at, align_bytes=64)

        def bank(i, name):
            return psum.tile([P, 512], F32, name=name, tag="bank%d" % i)

        copy_on = {"G": nc.gpsimd.tensor_copy, "V": nc.vector.tensor_copy, "S": nc.scalar.copy}

        offsets = keep.tile([P, S // 16], U16, name="offsets")
        nc.sync.dma_start(offsets[:], offs)

        tab_s = staged("tab_s", [P, T // 4], I32, SCALES_AT)
        nc.gpsimd.memset(tab_s[32:64, :], 0)
        nc.gpsimd.memset(tab_s[64:128, :], 0)
        for u in range(2):
            for a in range(2):
                nc.sync.dma_start(tab_s[16 * u + 8 * a : 16 * u + 8 * a + 8, :], tab_scales[a, 8 * u : 8 * u + 8, :].bitcast(I32))

        tab_w = [staged("tab_w%d" % a, [P, T], I32, TAB_AT[a]) for a in range(2)]
        x_raw = {}

        def load_table(a):
            nc.sync.dma_start(tab_w[a][:], tab_words[a].rearrange("p t i -> p (t i)").bitcast(I32))

        def load_x(i):
            k0, groups, a, at = X_LOADS[i]
            raw = staged("x_raw%d" % i, [P, 4, P * groups], F32, at)
            nc.sync.dma_start(raw[:], x[PASS * a : PASS * (a + 1), P * k0 : P * (k0 + groups)].rearrange("(p j) m -> p j m", j=4))
            for k in range(groups):
                x_raw[k0 + k, a] = (raw, P * k)

        load_table(0)
        g_raw = sb("g_raw", [2, PASS], F32)
        nc.sync.dma_start(g_raw[:], g.rearrange("(b j) -> b j", b=2))
        for i in range(FREE_LOADS):
            load_x(i)
        load_table(1)

        low = sb("low", [P, 8], F32)
        nc.gpsimd.memset(low[:], FLOOR_SCORE)
        tiny = sb("tiny", [P, 8], F32)
        nc.scalar.activation(tiny[:, 0:1], low[:, 0:1], ACT.Sigmoid)
        g_rows = sb("g_rows", [P, PASS], F32)
        nc.gpsimd.memset(g_rows[:], 0.0)
        ident = sb("ident", [P, P], F32)
        make_identity(nc, ident[:])

        listed = sb("listed", [P, S], U8)
        v_s = sb("v_s", [P, S], U8)
        nc.vector.memset(v_s[:].bitcast(I32), 0)

        def picks(b):
            return offsets[:, 32 * b : 32 * (b + 1)]

        def in_slots(ap):
            return ap.rearrange("p (u e q r) -> p q u r e", u=2, e=2, r=8)

        for b in range(2):
            nc.vector.tensor_copy(in_slots(listed[:, PASS * b : PASS * (b + 1)]), tab_s[:].bitcast(U8).indirect(picks(b)))
        for src, dst in ((0, 0), (4, 32), (16, 64), (16, 92)):
            nc.sync.dma_start(v_s[dst : dst + 16, :].bitcast(I32), listed[src : src + 16, :].bitcast(I32))

        g_bank = bank(0, "g_bank")
        nc.gpsimd.tensor_copy(g_rows[0:2, :].rearrange("b (u e q r) -> b u e q r", u=2, e=2, r=8), g_raw[:].rearrange("b (q u r e) -> b u e q r", u=2, e=2, r=8))
        for t in range(4):
            nc.tensor.transpose(g_bank[:, P * t : P * (t + 1)], g_rows[:, P * t : P * (t + 1)], ident[:])
        slopes = sb("slopes", [P, 2, 4], F32)
        nc.scalar.activation(slopes[:], g_bank[:].rearrange("p (t k) -> p k t", t=4)[:, 0:2, :], ACT.Copy, scale=-1.0 / KNEE)

        v_w = {}

        def gather_words(a, b):
            if a == 0:
                v_w[a, b] = sb("v_w%d_%d" % (a, b), [P, PASS], U32)
            else:
                v_w[a, b] = staged("v_w%d_%d" % (a, b), [P, PASS], U32, rounded_at(0) + (2 * KB - 64) * (2 * b - 1))
            nc.vector.tensor_copy(in_slots(v_w[a, b][:]), tab_w[a][:].bitcast(U32).indirect(picks(b)))

        x_w = [sb("x_w%d" % c, [P, 2 * P * chunk[1]], U32) for c, chunk in enumerate(CHUNKS)]
        x_s = [sb("x_s%d" % c, [P, 2 * P * chunk[1]], U8) for c, chunk in enumerate(CHUNKS)]
        chunk_of = {chunk[0] + k: (c, k) for c, chunk in enumerate(CHUNKS) for k in range(chunk[1])}

        def round_piece(engine, dst, src):
            copy_on[engine](dst.rearrange("p (c i) j -> p c j i", i=4), src.rearrange("p j (c i) -> p c j i", i=4))

        def quantise_x(c):
            k0, groups = CHUNKS[c][:2]
            width = P * groups
            flat = staged("x_b%d" % c, [P, 8 * width], BF16, rounded_at(c))
            xb = flat[:].rearrange("p (a m j) -> p a m j", a=2, j=4)
            for a in range(2):
                engines = CHUNKS[c][2 + a]
                share = width // len(engines)
                raw, m0 = x_raw[k0, a]
                for i, engine in enumerate(engines):
                    round_piece(engine, xb[:, a, share * i : share * (i + 1), :], raw[:, :, m0 + share * i : m0 + share * (i + 1)])
            nc.vector.quantize_mx(x_w[c][:].bitcast(FP8X4), x_s[c][:], flat[:])

        def x_cols(a, k):
            c, i = chunk_of[k]
            c0 = P * (CHUNKS[c][1] * a + i)
            return x_w[c][:, c0 : c0 + P].bitcast(FP8X4), x_s[c][:, c0 : c0 + P]

        gather_words(0, 0)
        gather_words(0, 1)
        quantise_x(0)
        gather_words(1, 0)
        gather_words(1, 1)
        for i in range(FREE_LOADS, len(X_LOADS)):
            load_x(i)
        soft = [
            staged("soft%d" % k, [P, 2, P, 4], F32, SOFT_AT[k]) if k in SOFT_AT else sb("soft%d" % k, [P, 2, P, 4], F32)
            for k in range(GROUPS)
        ]
        factor = [
            staged("factor%d" % k, [P, 2, P, 4], F32, rounded_at(FACTOR_AFTER[k]) - 4 * KB + 64) if k in FACTOR_AFTER else sb("factor%d" % k, [P, 2, P, 4], F32)
            for k in range(GROUPS)
        ]
        for k in range(GROUPS):
            for b in range(2):
                i = 2 * k + b
                for c in range(1, len(CHUNKS)):
                    if CHUNKS[c][4] == i:
                        quantise_x(c)
                acc = bank(i % 8, "acc%d" % i)
                passes = [(a, t) for a in range(2) for t in range(4)] if k == 0 else [(a, t) for t in range(4) for a in range(2)]
                for a, t in passes:
                    if True:
                        js = slice(PASS * b + P * t, PASS * b + P * (t + 1))
                        codes, scales = x_cols(a, k)
                        nc.tensor.matmul_mx(
                            out=acc[:, P * t : P * (t + 1)],
                            lhsT=v_w[a, b][:, P * t : P * (t + 1)].bitcast(FP8X4),
                            lhsT_scale=v_s[8 * a : P, js],
                            rhs=codes,
                            rhs_scale=scales,
                            start=(a == 0 and t == 0),
                            stop=(a == 1 and t == 3),
                        )
                scores = acc[:].rearrange("p (t m) -> p m t", t=4)
                if i >= VECTOR_FIRST:
                    nc.scalar.activation(soft[k][:, b, :, :], scores, ACT.Sigmoid, scale=-1.0)
                nc.vector.scalar_tensor_tensor(
                    factor[k][:, b, :, :], scores, KNEE, slopes[:, b, :].unsqueeze(1).to_broadcast([P, P, 4]), ALU.max, ALU.mult
                )
                if i < VECTOR_FIRST:
                    nc.scalar.activation(soft[k][:, b, :, :], scores, ACT.Sigmoid, scale=-1.0)
        wd_raw = []
        for i in range(4):
            wd_raw.append(staged("wd_raw%d" % i, [P, 2, T // 4], F32, WD_AT[i]))
            nc.sync.dma_start(wd_raw[i][:], wdT[:, T // 4 * i : T // 4 * (i + 1)].rearrange("(h p) t -> p h t", h=2))
        wl_w = staged("wl_w", [P, 2, N // 2], I32, WL_AT)
        nc.sync.dma_start(wl_w[:], wl_words.bitcast(I32).rearrange("a p c -> p a c"))
        wl_s = staged("wl_s", [P, 2, N // 4], I32, WL_AT + KB)

        floor = sb("floor", [P, 8], F32)
        nc.scalar.activation(floor[:, 0:1], soft[-1][:, 0, 0, 0:1], ACT.Identity, scale=0.0, bias=tiny[:, 0:1])

        wd_pairs = staged("wd_pairs", [P, T, 2], BF16, rounded_at(len(CHUNKS) - 1) + 2 * KB - 64)
        for i, engine in enumerate(WD_CASTS):
            copy_on[engine](wd_pairs[:, T // 4 * i : T // 4 * (i + 1), :], wd_raw[i][:].rearrange("p h t -> p t h"))
        nc.gpsimd.memset(wl_s[:], 0)
        for q in range(4):
            nc.sync.dma_start(wl_s[32 * q : 32 * q + 4, :, :], wl_scales[:, 4 * q : 4 * q + 4, :].bitcast(I32).rearrange("a r c -> r a c"))

        window = wd_pairs[:].rearrange("p t h -> p (t h)").bitcast(U32)
        turned = [bank(b, "turned%d" % b) for b in range(2)]
        for b in range(2):
            wd_g = sb("wd_g%d" % b, [P, PASS], U32, None if b else "slopes")
            nc.vector.tensor_copy(in_slots(wd_g[:]), window.indirect(picks(b)))
            for t in range(4):
                nc.tensor.transpose(turned[b][:, P * t : P * (t + 1)], wd_g[:, P * t : P * (t + 1)].bitcast(F32), ident[:])

        wd_b = sb("wd_b", [P, 2, 2, P, 4], BF16)
        wd_w = sb("wd_w", [P, 2 * N], U32)
        wd_s = sb("wd_s", [P, 2 * N], U8)
        h_b = sb("h_b", [P, GROUPS, 2, PASS], BF16)
        h_w = sb("h_w", [P, GROUPS, 2, P], U32)
        h_s = sb("h_s", [P, GROUPS, 2, P], U8)

        def flat(tile):
            return tile[:].rearrange("p k b c -> p (k b c)")

        def ln(k):
            nc.scalar.activation(soft[k][:], soft[k][:], ACT.Ln, bias=floor[:, 0:1])
            if k in UNLOAD_AFTER:
                b = UNLOAD_AFTER.index(k)
                nc.scalar.copy(wd_b[:, b, :, :, :], turned[b][:].bitcast(BF16).rearrange("p (t n h) -> p h n t", t=4, h=2))

        def finish(k, b0, halves):
            cols = slice(PASS * b0, PASS * (b0 + halves))
            nc.vector.scalar_tensor_tensor(
                flat(h_b)[:, PASS * (2 * k + b0) : PASS * (2 * k + b0 + halves)],
                soft[k][:].rearrange("p b m t -> p (b m t)")[:, cols],
                -KNEE,
                factor[k][:].rearrange("p b m t -> p (b m t)")[:, cols],
                ALU.max,
                ALU.mult,
            )

        def quantise_h(u0, units):
            nc.vector.quantize_mx(
                flat(h_w)[:, P * u0 : P * (u0 + units)].bitcast(FP8X4), flat(h_s)[:, P * u0 : P * (u0 + units)], flat(h_b)[:, PASS * u0 : PASS * (u0 + units)]
            )

        for k in range(LN_AHEAD):
            ln(k)
        for k in range(GROUPS - 1):
            if k + LN_AHEAD < GROUPS:
                ln(k + LN_AHEAD)
            finish(k, 0, 2)
            if k % 2 == 0 and k > 0:
                quantise_h(2 * k - 4, 4)
            if k == WD_QUANTISE_AFTER:
                nc.vector.quantize_mx(wd_w[:].bitcast(FP8X4), wd_s[:], wd_b[:].rearrange("p b h n t -> p (b h n t)"))
        last = GROUPS - 1
        finish(last, 0, 1)
        quantise_h(2 * last - 2, 2)
        finish(last, 1, 1)
        quantise_h(2 * last, 1)
        quantise_h(2 * last + 1, 1)

        def intensities(name, k0, groups, banks):
            w = P * groups
            accs = [bank(banks[h], "y%s_%d" % (name, h)) for h in range(2)]
            for h in range(2):
                for k in range(groups):
                    for a in range(2):
                        codes, scales = x_cols(a, k0 + k)
                        nc.tensor.matmul_mx(
                            out=accs[h][:, P * k : P * (k + 1)],
                            lhsT=wl_w[:, a, 64 * h : 64 * (h + 1)].bitcast(U8).bitcast(FP4X4),
                            lhsT_scale=wl_s[:, a, 32 * h : 32 * (h + 1)].bitcast(U8),
                            rhs=codes,
                            rhs_scale=scales,
                            start=(k == 0 and a == 0),
                            stop=False,
                        )
            for k in range(groups):
                for b in range(2):
                    for h in range(2):
                        ns = slice(N * b + P * h, N * b + P * (h + 1))
                        nc.tensor.matmul_mx(
                            out=accs[h][:, P * k : P * (k + 1)],
                            lhsT=wd_w[:, ns].bitcast(FP8X4),
                            lhsT_scale=wd_s[:, ns],
                            rhs=h_w[:, k0 + k, b, :].bitcast(FP8X4),
                            rhs_scale=h_s[:, k0 + k, b, :],
                            start=False,
                            stop=(b == 1 and k == groups - 1),
                        )
            res = sb("res" + name, [P, 2, w], F32)
            for h in range(2):
                nc.scalar.activation(res[:, h, :], accs[h][:, 0:w], ACT.Exp)
                nc.sync.dma_start(out[P * h : P * (h + 1), P * k0 : P * k0 + w], res[:, h, :])

        intensities("A", 0, 4, (2, 3))
        intensities("B", 4, 2, (4, 5))
        intensities("C", 6, 1, (6, 7))
        intensities("D", 7, 1, (0, 1))
